import numpy as np, ml_dtypes
CORES = [2,6,10,14,18,22,26,30]
N = 8
import mx_ref
BF = ml_dtypes.bfloat16
def gcols(t, e):
    v = np.concatenate([t.reshape(8, 16, -1, 4), np.zeros((8, 16, 1, 4), BF)], axis=2)
    return np.ascontiguousarray(np.stack([v[g][:, e[g]] for g in range(8)])).reshape(128, -1)
def tile(rs):
    return np.stack(rs, axis=2).reshape(128, -1).astype(BF)
def cut(t, i, w=512):
    return t[:, w * i:w * i + w]
def pick(q, e):
    c = np.concatenate([q[0].reshape(128, -1, 4), np.zeros((128, 1, 4), np.uint8)], axis=1); s = np.concatenate([q[1], np.ones((16, 1), np.uint8)], axis=1)
    return (np.ascontiguousarray(c[:, e].reshape(128, -1)), np.ascontiguousarray(s[:, e]))
def join(*qs):
    return (np.concatenate([q[0] for q in qs], axis=1), np.concatenate([q[1] for q in qs], axis=1))
def put(q, e, v):
    c, s = q[0].reshape(128, -1, 4).copy(), q[1].copy(); c[:, e] = v[0].reshape(128, -1, 4); s[:, e] = v[1]
    return (c.reshape(128, -1), s)
def pk(c, s):
    return (np.ascontiguousarray(c), mx_ref.live(s))
def emit(q):
    return q[0], q[1]
def packed(v, rng):
    q = [mx_ref.quantize(np.ascontiguousarray(v[r])) for r in range(N)]
    return np.stack([a for a, b in q]), np.stack([mx_ref.plane(b, rng) for a, b in q])
def f(rng, *shape):
    return mx_ref.flush((rng.standard_normal(shape, dtype=np.float32) * np.exp2(rng.integers(-2, 3, shape[:-1] + (1,)))).astype(BF))
def wide(rng, *shape, cols=0):
    v = rng.standard_normal(shape, dtype=np.float32) * np.exp2(rng.integers(-12, 13, shape)).astype(np.float32)
    if cols: v *= np.repeat(np.exp2(rng.integers(-cols, cols + 1, shape[:-2] + (1, shape[-1] // 4))) * (rng.random(shape[:-2] + (1, shape[-1] // 4)) > 0.0625), 4, axis=-1).astype(np.float32)
    return mx_ref.flush(v.astype(BF))
C, R = 256, 3
H = C // 2
STEP = [1, 2, 4]
def keep(t, gs):
    v = np.zeros((8, 16, t.shape[1]), BF)
    v[gs] = t.reshape(8, 16, -1)[gs]
    return v.reshape(128, -1)
def grams(a, b):
    n = a.shape[1] // 4
    qa = mx_ref.quantize(np.concatenate([keep(a, [m, m + 4]) for m in range(4)], axis=1))
    qb = mx_ref.quantize(np.concatenate([keep(b, [0, 1, 2, 3]), keep(b, [4, 5, 6, 7])], axis=1))
    z = np.zeros((8, n), np.float32)
    j = np.arange(32)
    for k in range(n // 32):
        e = 32 * k + j
        p = mx_ref.matmul(pick(qa, np.concatenate([e + n * m for m in range(4)])), pick(qb, np.concatenate([e, e + n])))
        for g in range(8): z[g, e] = p[32 * (g % 4) + j, 32 * (g // 4) + j]
    return z + np.float32(0.0)
def over(v):
    return np.repeat(np.repeat(v, 16, axis=0), 4, axis=1)
def big(v):
    v = v.astype(np.float32)
    v[np.abs(v) < np.float32(2.0 ** -16)] = 0
    return v.astype(BF)
def common(w, rng):
    c, p = packed(np.stack([w] * N), rng)
    return {"wc": c, "ws": p}
def weights(rng):
    return common(big(f(rng, 128, 2048)), rng)
def still(rng):
    w = np.zeros((128, 4, 128, 4), np.float32)
    i = np.arange(128)
    for b in range(4): w[i, b, i, b] = 32
    return common(w.reshape(128, 2048).astype(BF), rng)
def numbers_of(rng):
    return {"x": big(f(rng, N, 128, 4 * C)), "v": np.array(f(rng, N, 128, 512))}
def setup_inputs(rng):
    return {**numbers_of(rng), **weights(rng)}
def setup_inputs_ties(rng):
    d = numbers_of(rng)
    x = d["x"].reshape(N, 128, C, 4)
    o = rng.permutation(N)
    for r in range(N):
        k = np.zeros(C, int) if o[r] == 0 else rng.permutation(C) % 3
        a = x[r][:, :3].astype(np.float32)
        a[:, 2] = 0
        z = rng.choice([-1.0, 1.0], (128, 6, 4)).astype(np.float32)
        z[:, 5] = -z[:, 0]
        x[r] = (a[:, k] * z[:, rng.integers(0, 6, C)]).astype(BF)
        if o[r] == 1: x[r] = 0
    return {"x": x.reshape(N, 128, 4 * C), "v": d["v"], **weights(rng)}
def setup_inputs_near(rng):
    main = np.array([[0.75, 0.5, 0.25, 0.25, 0.25, 0, 0, 0], [0.25, 0.5, 0.5, 0.5, 0.25, 0.25, 0.25, 0], [0, 1, 0, 0, 0, 0, 0, 0]])
    size = np.where(rng.permutation(N) < N // 2, 2.0 ** -16, 1.0)
    x = np.zeros((N, 8, 16, C, 4))
    i = np.arange(H)
    s = 3 * i // 2
    tiny = 2.0 ** -11
    def fine(s):
        k = (s[:, None] >> np.array([0, 2, 4, 6])) & 3
        return (np.arange(4) < k[:, :, None]) * np.exp2(np.arange(4) - 11.0)[:, None]
    for r in range(N):
        for g in range(8):
            e = rng.permutation(C).reshape(H, 2)
            kind = np.where(i % 2 == 0, rng.integers(0, 2, H), rng.integers(0, 3, H))
            kind[:2] = (r + g) % 2, 2
            top, low = rng.choice([-1.0, 1.0], (2, H))
            z = np.zeros((C, 16, 4))
            z[e[:, 0], 0, 0] = 1
            z[e[:, 0], 8:12] = fine(s)
            z[e[:, 1], :8, 0] = top[:, None] * main[kind]
            z[e[:, 1], 8:12] = (top * low)[:, None, None] * fine(s + (kind == 2))
            for j in (H - 2, H - 1):
                z[e[j]] = 0
                z[e[j, 0], 0, 0] = 2
                z[e[j, 1], :8, 0] = 2 * main[0]
                z[e[j, 0], 8, :2] = tiny
                if j == H - 2:
                    z[e[j, 1], 8, 1:3] = tiny
                else:
                    z[e[j, 1], 8, 2:] = tiny
                    z[e[j], 9, 0] = 2 * tiny
                z[e[j, 1]] *= top[j]
            x[r, g] = z.transpose(1, 0, 2) * size[r]
    return {"x": x.astype(np.float32).reshape(N, 128, 4 * C).astype(BF), "v": np.array(f(rng, N, 128, 512)), **still(rng)}
def setup_inputs_huge(rng):
    o = rng.permutation(N)
    low = np.where(o == 0, 0.98, 0.8)[:, None, None, None, None]
    x = 2.0 ** 30 * (low + (1 - low) * rng.random((N, 8, 16, C, 4)))
    x[o == 0, :, ::8, :, 0] = 2.0 ** 30
    c = rng.choice([-1.0, 1.0], (N, 8, 1, C, 1))
    c[o % 2 == 1] = 1
    c[o % 2 == 0, :, :, ::3] = -1
    return {"x": (x * c).astype(np.float32).reshape(N, 128, 4 * C).astype(BF), "v": np.array(f(rng, N, 128, 512)), **still(rng)}
def setup_inputs_lean(rng):
    h = np.array([0.25, 0.5, 1.0, 2.0])[rng.integers(0, 4, (N, 1, C, 1))]
    o = rng.permutation(N)
    h[o == 0] = 0.125
    h[o == 1] = 4
    c = rng.choice([-1.0, 1.0], (N, 1, C, 1))
    a = rng.choice([-1.0, 1.0], (N, 128, 1, 4)) * (0.5 + rng.random((N, 128, 1, 4)))
    x = c * (a + h * rng.standard_normal((N, 128, C, 4)))
    return {"x": big(x.reshape(N, 128, 4 * C)), "v": np.array(f(rng, N, 128, 512)), **weights(rng)}
def setup_inputs_spread(rng):
    d = setup_inputs(rng)
    d["x"] = big(wide(rng, N, 128, 4 * C, cols=6))
    return d
def check_inputs(d):
    b = []
    for k in ("x", "v"):
        a = np.abs(d[k].astype(np.float32))
        if not (np.isfinite(a).all() and ((a == 0) | (a >= 2.0 ** -30) & (a <= 2.0 ** 30)).all()): b.append("a value of " + k)
    if ((d["wc"] & 127) == 127).any(): b.append("a code of wc")
    if (d["wc"] != d["wc"][:1]).any(): b.append("wc differs between ranks")
    s = [mx_ref.live(p) for p in d["ws"]]
    if any((p != s[0]).any() for p in s): b.append("ws differs between ranks")
    return b
def reference(x, v, wc, ws):
    w = pk(wc[0], ws[0])
    now = np.concatenate([x[r] for r in range(N)], axis=1)
    for t in range(R):
        d = grams(now, now)
        o = np.argsort(d.reshape(8, N, C), axis=2, kind="stable")
        at = o + C * np.arange(N)[:, None]
        even, odd = at[:, :, ::2].reshape(8, -1), at[:, :, 1::2].reshape(8, -1)
        a, b = gcols(now, even), gcols(now, odd)
        da = np.take_along_axis(d, even, axis=1)
        n = grams(a, b)
        c = np.where(np.abs(n) >= np.float32(0.75) * da, np.float32(1.0), np.where(np.abs(n) >= np.float32(0.25) * da, np.float32(0.5), np.float32(0.0))) * np.sign(n)
        left = (b.astype(np.float32) - over(c) * a.astype(np.float32)).astype(BF)
        swap = over(grams(left, left) < da)
        stay, go = np.where(swap, left, a), np.where(swap, a, left)
        q = mx_ref.quantize(np.ascontiguousarray(go))
        came = tile([mx_ref.matmul(pick(w, np.arange(128 * k, 128 * k + 128)), q) * np.float32(0.03125) for k in range(4)])
        now = np.concatenate([z for r in range(N) for z in (cut(stay, r, 4 * H), cut(came, (r - STEP[t]) % N, 4 * H))], axis=1)
    y, ol = np.zeros((N, 128, C), np.float32), np.zeros((N, 8, C), np.float32)
    oc, osc = np.zeros((N, 128, 4 * C), np.uint8), np.zeros((N, 16, C), np.uint8)
    for r in range(N):
        q = mx_ref.quantize(np.ascontiguousarray(cut(now, r, 4 * C)))
        y[r] = mx_ref.matmul(mx_ref.quantize(v[r]), q)
        ol[r] = o[:, r]
        oc[r], osc[r] = emit(q)
    return {"y": y, "ol": ol, "oc": oc, "osc": osc}

@@ -1,0 +1,616 @@
+import numpy as np
+from concourse.mybir import dt, AluOpType, ActivationFunctionType
+
+F32, BF, I32, U16, CD, U8 = "float32", "bfloat16", "int32", "uint16", "float8_e4m3fn_x4", "uint8"
+STEP = [1, 2, 4]
+STAGES = ["d0", "d0b", "n0", "e0", "d1", "n1", "e1", "d2", "n2", "e2"]
+TINY = 2.0 ** -100
+BELOW = 1.0 - 2.0 ** -24
+BIG = 65536.0
+SHARE = {"r0": 7, "r": 3, "d0a": 5, "d0b": 2, "d": 6, "e": 6, "cut": [0, 384, 512], "ss": 3}
+
+SCRATCH = {
+    "ps": ("psum", [128, 4096], F32),
+    "fa": ("sbuf", [128, 520], BF), "fb": ("sbuf", [128, 520], BF),
+    "mva": ("sbuf", [128, 1024], BF), "mvb": ("sbuf", [128, 1024], BF),
+    "xp": ("sbuf", [128, 1024], BF), "yp": ("sbuf", [128, 1024], BF), "ar": ("sbuf", [128, 1024], BF),
+    "fm": ("sbuf", [128, 512], BF), "xf": ("sbuf", [128, 1024], BF), "vt": ("sbuf", [128, 512], BF),
+    "wq": ("sbuf", [128, 512], CD), "wp": ("sbuf", [128, 512], U8),
+    "vq": ("sbuf", [128, 128], CD), "vp": ("sbuf", [128, 128], U8),
+    "xq": ("sbuf", [128, 256], CD), "xs": ("sbuf", [128, 256], U8),
+    "wa": ("sbuf", [128, 256], F32), "wb": ("sbuf", [128, 256], F32),
+    "va": ("sbuf", [128, 256], F32), "vb": ("sbuf", [128, 256], F32),
+    "ua": ("sbuf", [128, 256], F32), "dd": ("sbuf", [128, 512], F32), "ds": ("sbuf", [128, 256], F32),
+    "mk": ("sbuf", [128, 256], F32), "vd": ("sbuf", [128, 256], F32), "ee": ("sbuf", [128, 256], F32),
+    "dg": ("sbuf", [128, 256], BF), "pb": ("sbuf", [128, 256], BF), "dw": ("sbuf", [128, 256], F32),
+    "cm": ("sbuf", [128, 2400], BF), "cs": ("sbuf", [128, 3840], BF), "sg": ("sbuf", [128, 1920], BF),
+    "ra": ("sbuf", [128, 16], F32), "rku": ("sbuf", [128, 16], U16),
+    "oo": ("sbuf", [128, 256], BF), "ox": ("sbuf", [128, 256], F32), "oz": ("sbuf", [128, 256], F32),
+    "fr": ("sbuf", [128, 256], BF), "cu": ("sbuf", [128, 256], BF), "ofy": ("sbuf", [128, 16], U16),
+    "of": ("sbuf", [128, 256], F32), "ids": ("sbuf", [128, 256], BF), "so": ("sbuf", [128, 128], BF),
+    "sv": ("sbuf", [128, 128], BF),
+    "da": ("sbuf", [128, 128], F32), "dq": ("sbuf", [128, 128], F32),
+    "th": ("sbuf", [128, 96], F32),
+    "ub": ("sbuf", [128, 128], BF), "tb": ("sbuf", [128, 128], BF), "cc": ("sbuf", [128, 256], BF),
+    "bx": ("sbuf", [128, 128], F32), "jo": ("sbuf", [128, 32], F32),
+    "ofm": ("sbuf", [128, 16], U16), "yo": ("sbuf", [128, 256], F32),
+    "pi": ("sbuf", [128, 8], I32), "pf": ("sbuf", [128, 16], F32),
+    "ka": ("sbuf", [128, 128], F32), "pl": ("sbuf", [128, 32], U16), "im": ("sbuf", [128, 64], F32),
+    "rs32": ("sbuf", [128, 128], F32), "rsx": ("sbuf", [128, 128], F32),
+    "li": ("sbuf", [128, 32], I32), "lu": ("sbuf", [128, 32], U16),
+    "kc": ("sbuf", [128, 1024], BF), "ff": ("sbuf", [128, 128], F32),
+    "jb": ("sbuf", [128, 896], BF), "kb": ("sbuf", [128, 96], F32),
+}
+for _s in STAGES:
+    SCRATCH["q_" + _s] = ("sbuf", [128, 416], CD)
+    SCRATCH["s_" + _s] = ("sbuf", [128, 416], U8)
+    SCRATCH["tq_" + _s] = ("sbuf", [128, 512], CD)
+    SCRATCH["ts_" + _s] = ("sbuf", [128, 512], U8)
+for _t in range(3):
+    SCRATCH["mq%d" % _t] = ("sbuf", [128, 128], CD)
+    SCRATCH["ms%d" % _t] = ("sbuf", [128, 128], U8)
+    SCRATCH["lq%d" % _t] = ("sbuf", [128, 128], CD)
+    SCRATCH["ls%d" % _t] = ("sbuf", [128, 128], U8)
+
+POOL = {"v": 48, "a": 36, "t": 12, "g": 16}
+NDMA = 24
+SEMAPHORES = ([k + "%d" % i for k in POOL for i in range(POOL[k])] + ["dma%d" % i for i in range(NDMA)]
+              + ["arr0", "arr1", "arr2", "sent"])
+
+
+def V(name, a=None, b=None, s=None, p=None):
+    return (name, a, b, s, p, None)
+
+
+def IND(win, off):
+    return win[:5] + (off,)
+
+
+def lanes(T, topo, rank):
+    n = len(T.cores)
+    sets = [topo.engines(T.cores[rank], T.cores[(rank + s) % n]) for s in STEP]
+    return [k for k in sets[0] if all(k in z for z in sets)]
+
+
+def build(T, topo, core, rank):
+    ops = []
+    sent = [0]
+    A, AF = AluOpType, ActivationFunctionType
+
+    def ap(v, cast=None):
+        if not isinstance(v, tuple):
+            return v
+        name, a, b, s, p, off = v
+        x = T[name][slice(None) if p is None else slice(*p), slice(a, b, s)]
+        if cast is not None:
+            x = x.bitcast(cast)
+        if off is not None:
+            x = x.indirect(ap(off))
+        return x
+
+    def views(*xs):
+        r = []
+        for x in xs:
+            if isinstance(x, tuple):
+                r.append(x)
+                if x[5] is not None:
+                    r.append(x[5])
+        return r
+
+    def add(q, fn, rd, wr, kind="c", pre=None):
+        w = [x for x in wr if isinstance(x, tuple)]
+        ops.append((q, fn, views(*rd) + [x[5] for x in w if x[5] is not None], w, kind, pre))
+
+    def cp(o, i):
+        add("v", lambda e: e.tensor_copy(ap(o), ap(i)), [i], [o])
+
+    def tt(o, x, y, op):
+        add("v", lambda e: e.tensor_tensor(ap(o), ap(x), ap(y), op), [x, y], [o])
+
+    def ts(o, x, s1, op0, s2=None, op1=None):
+        if op1 is None:
+            add("v", lambda e: e.tensor_scalar(ap(o), ap(x), ap(s1), None, op0), [x, s1], [o])
+        else:
+            add("v", lambda e: e.tensor_scalar(ap(o), ap(x), ap(s1), ap(s2), op0, op1), [x, s1, s2], [o])
+
+    def scan(o, d0, d1, op0=A.mult, op1=A.add, first=0.0):
+        add("v", lambda e: e.tensor_tensor_scan(ap(o), ap(d0), ap(d1), ap(first), op0, op1), [d0, d1, first], [o])
+
+    def tr(o, i):
+        add("v", lambda e: e.transpose(ap(o), ap(i)), [i], [o])
+
+    def ms(o, c):
+        add("v", lambda e: e.memset(ap(o), c), [], [o])
+
+    def act(o, i, f=AF.Copy, bias=0.0, scale=1.0, acc=None):
+        if acc is not None:
+            add("a", lambda e: e.activation(ap(o), ap(i), f, bias=ap(bias), scale=ap(scale), accum_out=ap(acc)),
+                [i, bias, scale], [o, acc])
+        elif bias == 0.0 and scale == 1.0:
+            add("a", lambda e: e.activation(ap(o), ap(i), f), [i], [o])
+        else:
+            add("a", lambda e: e.activation(ap(o), ap(i), f, bias=ap(bias), scale=ap(scale)), [i, bias, scale], [o])
+
+    def mul(q, o, i, s):
+        if q == "v":
+            ts(o, i, s, A.mult)
+        else:
+            act(o, i, AF.Identity, scale=s)
+
+    def mov(q, o, i):
+        if q == "v":
+            cp(o, i)
+        elif q == "a":
+            act(o, i)
+        else:
+            add("g", lambda e: e.affine_select(ap(o), ap(i), [[0, 128]], A.is_ge, 0.0, 0, 0), [i], [o])
+
+    def quant(c, s, i):
+        add("v", lambda e: e.quantize_mx(ap(c), ap(s), ap(i)), [i], [c, s])
+
+    def mm(o, lq, ls, rq, rs, pre=None):
+        add("t", lambda e: e.matmul_mx(ap(o), ap(lq), ap(ls), ap(rq), ap(rs), True, True), [lq, ls, rq, rs], [o], "c", pre)
+
+    def iota(o, pat, base, fl=True):
+        if fl:
+            add("g", lambda e: e.iota(ap(o), pat, base, 0, allow_small_or_imprecise_dtypes=True), [], [o])
+        else:
+            add("g", lambda e: e.iota(ap(o), pat, base, 0), [], [o])
+
+    def dma(q, o, i, oc=None, ic=None, after=()):
+        add(q, lambda e: e.dma_start(ap(o, oc), ap(i, ic)), [i] + list(after), [o], "d")
+
+    def col(name, j):
+        return V(name, j, j + 1)
+
+    def bank(b, a=0, n=128):
+        return V("ps", 512 * b + a, 512 * b + a + n)
+
+    def plane(name, t, a=0, b=256, s=None):
+        return V(name, 256 * t + a, 256 * t + b, s)
+
+    QF, RF, CF, ODD, Q12, EVN, SC, JM, JS, Q1, Q2, Q8, LT = [col("pf", j) for j in range(13)]
+    PAR = [EVN, ODD]
+    EXL, CXL, DXL, N4L, THL = V("lu", 0, 8), V("lu", 8, 16), V("lu", 16, 24), V("lu", 24, 26), V("lu", 26, 28)
+    CO, RS4, JMT, JST = V("kb", 0, 32), V("kb", 32, 64), V("kb", 64, 72), V("kb", 72, 80)
+    C16, MK16, RS16, WX, WA, WB, WY = [V("kc", 128 * j, 128 * j + 128) for j in range(7)]
+    JALL, JK, JODD, JHALF, ONES = V("jb", 0, 256), V("jb", 128, 256), V("jb", 256, 384), V("jb", 384, 640), V("jb", 640, 896)
+    TH, GG, GS = V("th", 0, 32), V("th", 32, 64), V("th", 64, 96)
+    OFA, OFB, OFM, OFS = V("ofy", 0, 8), V("ofy", 8, 16), V("ofm", 0, 8), V("ofm", 8, 16)
+
+    dma("s", V("fa", 0, 512), T.x[:, 0:512])
+    dma("a", V("fb", 0, 512), T.x[:, 512:1024])
+    add("g", lambda e: e.iota(ap(col("pi", 0)), [[0, 1]], 0, 1), [], [col("pi", 0)])
+    iota(C16, [[0, 8], [1, 16]], 0)
+    iota(V("ka", 0, 32), [[32, 4], [0, 4], [16, 2]], -128)
+    iota(V("ka", 32, 64), [[0, 4], [1, 4], [0, 2]], 0)
+    iota(V("ka", 64, 128), [[1, 32], [0, 2]], 0)
+    iota(JMT, [[32, 8]], 0)
+    iota(V("li", 24, 26), [[128, 2]], 31, False)
+    iota(V("li", 26, 28), [[16, 2]], 0, False)
+    iota(V("li", 0, 8), [[32, 4], [128, 2]], 31, False)
+    iota(V("li", 8, 16), [[4, 4], [16, 2]], 3, False)
+    iota(V("li", 16, 24), [[16, 8]], 15, False)
+    iota(CO, [[0, 8], [-1, 2], [0, 2]], 0)
+    iota(RS4, [[0, 8], [1, 4]], 0)
+    dma("s", V("wq"), T.wc[:, :], dt.uint8, None, [col("fa", 0), col("fb", 0)])
+    dma("s", V("wp"), T.ws[:, :])
+    dma("s", V("vt"), T.v[:, :])
+    ms(V("fa", 512, 520), 0.0)
+    ms(V("fb", 512, 520), 0.0)
+    ms(V("rs32"), 1.0)
+    ts(col("pi", 1), col("pi", 0), 15, A.bitwise_and)
+    ts(col("pi", 2), col("pi", 0), 31, A.bitwise_and)
+    ts(col("pi", 3), col("pi", 0), 5, A.arith_shift_right)
+    ts(col("pi", 4), col("pi", 0), 4, A.arith_shift_right, 1, A.bitwise_and)
+    ts(col("pi", 5), col("pi", 0), 12, A.bitwise_and)
+    ms(V("rs32", 0, 128, 32), 0.0)
+    ms(V("rsx"), 1e29)
+    cp(V("pf", 0, 5), V("pi", 1, 6))
+    ms(V("cc", 0, 256, 2), 0.0)
+    act(EVN, ODD, AF.Identity, 1.0, -1.0)
+    act(Q1, QF, AF.Identity, 1.0)
+    act(Q2, QF, AF.Identity, 0.0, 2.0)
+    act(Q8, Q12, AF.Identity, 0.0, 8.0)
+    ts(LT, QF, 15.0, A.is_lt)
+    ts(MK16, C16, QF, A.is_equal)
+    ts(RS16, C16, 1.0, A.min)
+    ts(WY, C16, QF, A.is_lt)
+    ts(WA, C16, QF, A.not_equal)
+    ts(WB, C16, Q1, A.is_equal, BIG, A.mult)
+    act(SC, LT, AF.Identity, 1.0, 1.0 / BIG - 1.0)
+    act(JM, LT, AF.Identity, 1.0, BIG - 1.0)
+    act(JS, LT, AF.Identity, 1.0, BIG + 1023.0)
+    act(V("ff"), WY, AF.Identity, 1.0, BELOW - 1.0)
+    ts(V("ka", 0, 32), V("ka", 0, 32), QF, A.add)
+    ts(V("ka", 32, 64), V("ka", 32, 64), CF, A.is_equal)
+    tt(WX, WA, WB, A.max)
+    tt(V("ka", 0, 32), V("ka", 0, 32), V("ka", 32, 64), A.mult)
+    ts(V("im"), V("ka", 64, 128), RF, A.is_equal)
+    ts(V("pl"), V("ka", 0, 32), 128.0, A.add)
+    ts(JMT, JMT, Q2, A.add, JM, A.mult)
+    ms(ONES, 1.0)
+    ms(V("rsx", 0, 128, 32), TINY)
+    ts(JST, JMT, JS, A.add)
+    ts(V("li", 24, 28), V("li", 24, 28), Q8, A.add)
+
+    def late_constants():
+        cp(V("lu", 0, 28), V("li", 0, 28))
+        for t in range(4):
+            mov("g", plane("xp", t, 0, 128), V("fa", t, 512, 4))
+        for t in range(4):
+            mov("g", plane("xp", t, 128, 256), V("fb", t, 512, 4))
+        iota(JALL, [[1, 256]], 0)
+        iota(JODD, [[2, 128]], 1)
+        iota(JHALF, [[1, 128], [0, 2]], 0)
+        iota(V("ids", 128, 256), [[1, 128]], 128)
+
+    def q_full(st, f):
+        quant(V("q_" + st, 0, 130), V("s_" + st, 0, 130), V(f, 0, 520))
+
+    def q_twice(st, mv):
+        quant(V("q_" + st, 160, 416), V("s_" + st, 160, 416), V(mv))
+
+    def masked(e, mv, msrc, jobs):
+        for j in jobs:
+            t, w = j // 2, j % 2
+            mul(e, V(mv, 4 * w + t, 1024, 8), msrc(t), PAR[w])
+
+    def pick_q(st, a, b):
+        o, i = V("tq_" + st, a, b), IND(V("q_" + st, 0, 130), V("pl", a // 16, b // 16))
+        add("v", lambda e: e.tensor_copy(ap(o, dt.uint32), ap(i, dt.uint32)), [i], [o])
+
+    def pick_s(st, a, b):
+        act(V("ts_" + st, a, b), IND(V("s_" + st, 0, 130), V("pl", a // 16, b // 16)))
+
+    def products(st, b0, a, b):
+        for k in range(a // 128, b // 128):
+            m = 160 + min(64 * k, 128)
+            mm(bank(b0 + k), V("tq_" + st, 128 * k, 128 * k + 128), V("ts_" + st, 128 * k, 128 * k + 128),
+               V("q_" + st, m, m + 128), V("s_" + st, m, m + 128))
+
+    def picks(st, b0):
+        cut = SHARE["cut"]
+        for a, b in zip(cut, cut[1:]):
+            pick_q(st, a, b)
+            pick_s(st, a, b)
+            products(st, b0, a, b)
+
+    def gram_front(st, msrc, fill, nv):
+        fill("v", 0)
+        fill("a", 2)
+        fill("v", 1)
+        fill("a", 3)
+        masked("v", "mva", msrc, range(2))
+        q_full(st, "fa")
+        masked("a", "mva", msrc, range(nv, 8))
+        masked("v", "mva", msrc, range(2, nv))
+        q_twice(st, "mva")
+        picks(st, 0)
+
+    def diagonal(w, b0, k):
+        tt(V(w, 64 * k, 64 * k + 64), bank(b0 + k, 64 * (k // 3), 64), V("im"), A.mult)
+
+    def gram_back(w, v, b0):
+        for k in range(4):
+            diagonal(w, b0, k)
+        for h in range(2):
+            scan(V(v, 128 * h, 128 * h + 128), V("rsx"), V(w, h, 256, 2), A.min, A.max, TINY)
+
+    def spread(v, a, e="v"):
+        mov(e, V("ua", a, a + 128), IND(V(v), EXL))
+        tr(V("dd", a, a + 128), V("ua", a, a + 128))
+
+    def mask16(src, a):
+        tt(V("mk", a, a + 128), src, MK16, A.mult)
+
+    def wrap(a):
+        scan(V("vd", a, a + 128), RS16, V("mk", a, a + 128))
+
+    def near1(src, a):
+        tt(V("ee", a, a + 128), src, V("ff"), A.mult)
+
+    def near2(a):
+        tt(V("dg", a, a + 128), IND(V("vd", a, a + 128), DXL), V("ee", a, a + 128), A.is_gt)
+
+    def near3(a):
+        scan(V("pb", a, a + 128), RS16, V("dg", a, a + 128))
+
+    def count_v(slots, w, na, between=()):
+        between = list(between)
+        lag = 1 + (len(between) > 1)
+
+        def total(i):
+            z = V("cm", w * i, w * i + w)
+            scan(V("cs", w * (na + i), w * (na + i + 1)), z, z, A.add, A.max, col("pb", 16 * slots[i][0] + 15))
+        for i, (m, win) in enumerate(slots):
+            ts(V("cm", w * i, w * i + w), win, col("vd", 16 * m + 15), A.is_lt)
+            if between:
+                between.pop(0)()
+            if i >= lag:
+                total(i - lag)
+        for i in range(len(slots) - lag, len(slots)):
+            total(i)
+
+    def count_a(slots):
+        held = []
+        for i, (m, win) in enumerate(slots):
+            w = win[2] - win[1]
+            z = V("sg", w * i, w * i + w)
+            act(z, win, AF.Sign, col("vd", 16 * m + 15), -1.0)
+            if held:
+                y, n = held.pop()
+                act(y, y, AF.Relu, acc=col("ra", n))
+            held.append((z, m))
+        if held:
+            y, n = held.pop()
+            act(y, y, AF.Relu, acc=col("ra", n))
+
+    def ring(m):
+        return (m, V("dd", 16 * m + 16, 16 * m + 256))
+
+    def places(a, na, b, w):
+        if na:
+            tt(V("cs", w - 1, w * na, w), V("ra", a, a + na), V("pb", 16 * a + 15, 16 * (a + na), 16), A.add)
+        cp(V("rku", a, b), V("cs", w - 1, w * (b - a), w))
+
+    def pull(out, src):
+        scan(out, WX, src)
+
+    def below(a):
+        act(V("dd", 256 + a, 384 + a), V("dd", a, a + 128), AF.Identity, 0.0, BELOW)
+
+    eng = lanes(T, topo, rank)
+    mask = sum(1 << k for k in eng)
+
+    for t_ in range(3):
+        if t_ == 0:
+            fa, fb = (lambda t: V("fa", t, 512, 4)), (lambda t: V("fb", t, 512, 4))
+            na, nb = SHARE["d0a"], SHARE["d0b"]
+            q_full("d0", "fa")
+            masked("a", "mva", fa, range(na, 8))
+            masked("v", "mva", fa, range(na))
+            q_twice("d0", "mva")
+            q_full("d0b", "fb")
+            late_constants()
+            picks("d0", 0)
+            masked("a", "mvb", fb, range(nb, 8))
+            masked("v", "mvb", fb, range(nb))
+            gram_back("wa", "va", 0)
+            pick_q("d0b", 0, 256)
+            q_twice("d0b", "mvb")
+            pick_s("d0b", 0, 256)
+            products("d0b", 4, 0, 256)
+            pick_q("d0b", 256, 512)
+            pick_s("d0b", 256, 512)
+            products("d0b", 4, 256, 512)
+            spread("va", 0, "a")
+            gram_back("wb", "vb", 4)
+            below(0)
+            act(CO, CO, AF.Identity, 0.75, 0.5)
+            act(RS4, RS4, AF.Sign)
+            mask16(V("dd", 0, 128), 0)
+            spread("vb", 128, "a")
+            wrap(0)
+            below(128)
+            na = SHARE["r0"]
+            count_a([ring(m) for m in range(na)])
+            mask16(V("dd", 128, 256), 128)
+            near1(V("dd", 0, 128), 0)
+            wrap(128)
+            near2(0)
+            near1(V("dd", 128, 256), 128)
+            near3(0)
+            near2(128)
+            count_v([ring(m) for m in range(na, 16)], 240, na, [lambda: near3(128)])
+            places(0, na, 16, 240)
+            cp(IND(V("oo"), V("rku")), JALL)
+            pull(V("ox", 0, 128), V("oo", 0, 256, 2))
+            pull(V("ox", 128, 256), V("oo", 1, 256, 2))
+            ts(V("ofy"), V("ox", 15, 256, 16), SC, A.mult)
+        else:
+            gram_front("d%d" % t_, lambda t: V("fa", t, 512, 4),
+                       lambda e, t: mul(e, V("fa", t, 512, 4), bank(4 + t), 0.03125), SHARE["d"])
+            for t in range(4):
+                mov("g", plane("xp", t, 128, 256), V("fa", t, 512, 4))
+            for t in range(4):
+                act(plane("xp", t, 0, 128), IND(plane("ar", t), OFS))
+            gram_back("wa", "va", 0)
+            spread("va", 128)
+            below(128)
+            mask16(V("dd", 128, 256), 128)
+            wrap(128)
+            near1(V("dd", 128, 256), 128)
+            na = SHARE["r"]
+            count_a([ring(m) for m in range(8, 8 + na)])
+            count_v([ring(m) for m in range(8 + na, 16)], 240, na, [lambda: near2(128), lambda: near3(128)])
+            act(V("dd", 0, 128), IND(V("dw"), OFS))
+            if t_ == 2:
+                act(V("ids", 0, 128), IND(JHALF, OFS))
+            places(8, na, 16, 240)
+            cp(IND(V("oo"), V("rku", 8, 16)), JK)
+            ts(V("fr"), V("oo"), 0.0, A.is_equal)
+            pull(V("ox", 0, 128), V("oo", 0, 256, 2))
+            scan(V("cu"), ONES, V("fr"), first=-1.0)
+            pull(V("ox", 128, 256), V("oo", 1, 256, 2))
+            pull(V("oz", 0, 128), V("cu", 0, 256, 2))
+            pull(V("oz", 128, 256), V("cu", 1, 256, 2))
+            tt(V("jo", 16, 32), V("ox", 15, 256, 16), V("oz", 15, 256, 16), A.max)
+            ts(V("ofy"), V("jo", 16, 32), SC, A.mult)
+
+        st = "n%d" % t_
+        for t, e in ((0, "v"), (2, "a"), (1, "v"), (3, "a")):
+            mov(e, V("fa", t, 512, 4), IND(plane("xp", t), OFA))
+        q_full(st, "fa")
+        for t in range(4):
+            act(plane("yp", t, 1, 256, 2), IND(plane("xp", t), OFB))
+            mov("g", plane("yp", t, 0, 256, 2), V("fa", t, 512, 4))
+        pick_q(st, 0, 512)
+        pick_s(st, 0, 512)
+        masked("v", "mva", lambda t: plane("yp", t, 1, 256, 2), range(8))
+        q_twice(st, "mva")
+        products(st, 0, 0, 512)
+        cp(V("da"), IND(V("dd", 0, 256), OFA))
+        diagonal("wa", 0, 0)
+        tr(V("dq"), V("da"))
+        for k in range(1, 4):
+            diagonal("wa", 0, k)
+        tt(TH, IND(V("dq"), THL), CO, A.mult)
+        scan(V("va", 0, 128), V("rs32"), V("wa", 0, 256, 2))
+        ts(V("th", 1, 32, 2), V("th", 1, 32, 2), -BELOW, A.mult)
+        scan(V("va", 128, 256), V("rs32"), V("wa", 1, 256, 2))
+        tt(GG, IND(V("va"), N4L), TH, A.is_ge)
+        scan(GS, RS4, GG)
+        ts(V("ub"), IND(GS, CXL), -0.5, A.mult, 1.0, A.add)
+        tr(V("cc", 1, 256, 2), V("ub"))
+        for t in (2, 3, 0, 1):
+            scan(plane("ar", t), V("cc"), plane("yp", t))
+        gram_front("e%d" % t_, lambda t: plane("ar", t, 1, 256, 2),
+                   lambda e, t: mov(e, V("fa", t, 512, 4), plane("ar", t, 1, 256, 2)), SHARE["e"])
+        gram_back("wa", "va", 0)
+        tt(V("ub"), IND(V("va"), EXL), V("dq"), A.is_ge)
+        tr(V("tb"), V("ub"))
+        pull(V("bx"), V("tb"))
+        tt(V("jo", 0, 8), V("bx", 15, 128, 16), JMT, A.add)
+        ts(OFM, V("jo", 0, 8), SC, A.mult)
+        for t, e in ((0, "v"), (2, "a"), (1, "v"), (3, "a")):
+            mov(e, V("fm", t, 512, 4), IND(plane("ar", t), OFM))
+        mq, msn, lq, ls = V("mq%d" % t_), V("ms%d" % t_), V("lq%d" % t_), V("ls%d" % t_)
+        quant(mq, msn, V("fm"))
+        rid, pid, _e = topo.addr(T.cores[(rank + STEP[t_]) % len(T.cores)])
+        arr = T.sem["arr%d" % t_]
+        add("g", lambda e, mq=mq, lq=lq, arr=arr, rid=rid, pid=pid:
+            e.remote_dma(ap(lq, dt.uint8), ap(mq, dt.uint8), arr, T.sem.sent, pid, rid, mask), [mq], [], "r")
+        add("g", lambda e, msn=msn, ls=ls, arr=arr, rid=rid, pid=pid:
+            e.remote_dma(ap(ls), ap(msn), arr, T.sem.sent, pid, rid, mask), [msn], [], "r")
+        sent[0] += 2 * len(eng)
+
+        if t_ < 2:
+            tt(V("ua", 0, 128), IND(V("va"), EXL), V("dq"), A.min)
+            iota(V("oo"), [[0, 256]], 0)
+            tt(V("sv"), JODD, V("tb"), A.subtract)
+            tr(V("ds", 0, 128), V("ua", 0, 128))
+            act(V("ds", 128, 256), V("ds", 0, 128), AF.Identity, 0.0, BELOW)
+            mask16(V("ds", 0, 128), 0)
+            near1(V("ds", 0, 128), 0)
+            wrap(0)
+            na = SHARE["ss"]
+            win = [(m, V("ds", 16 * m + 16, 16 * m + 128)) for m in range(8)]
+            count_a(win[:na])
+            mov("g", V("dd", 256, 384), V("ds", 128, 256))
+            mov("g", V("dw", 0, 256, 2), V("ds", 0, 128))
+            mov("g", V("dw", 1, 256, 2), V("ds", 0, 128))
+            count_v(win[na:], 112, na, [lambda: near2(0), lambda: near3(0)])
+            places(0, na, 8, 112)
+            cp(IND(V("so"), V("rku", 0, 8)), V("sv"))
+            pull(V("bx"), V("so"))
+            ts(OFS, V("bx", 15, 128, 16), SC, A.mult)
+        else:
+            quant(V("vq"), V("vp"), V("vt"))
+            tt(V("jo", 8, 16), JST, V("bx", 15, 128, 16), A.subtract)
+            ts(OFS, V("jo", 8, 16), SC, A.mult)
+            for t, e in ((0, "v"), (2, "a"), (1, "v"), (3, "a")):
+                mov(e, V("xf", t, 512, 4), IND(plane("ar", t), OFS))
+            quant(V("xq", 0, 128), V("xs", 0, 128), V("xf", 0, 512))
+            mm(bank(0), V("vq"), V("vp"), V("xq", 0, 128), V("xs", 0, 128))
+            act(V("of", 0, 256, 2), IND(V("ids"), OFA))
+            act(V("of", 1, 256, 2), IND(V("ids"), OFB))
+            dma("s", T.oc[:, 0:512], V("xq", 0, 128), None, dt.uint8)
+            cp(V("yo", 0, 128), bank(0))
+            dma("s", T.ol[:, :], V("of", None, None, None, (0, 128, 16)))
+            dma("s", T.y[:, 0:128], V("yo", 0, 128))
+        come = 2 * len(lanes(T, topo, (rank - STEP[t_]) % len(T.cores)))
+        for b in (0, 2, 1, 3):
+            mm(bank(4 + b), V("wq", 128 * b, 128 * b + 128), V("wp", 128 * b, 128 * b + 128), lq, ls,
+               (arr, come) if b == 0 else None)
+
+    for t, e in ((0, "v"), (2, "a"), (1, "v"), (3, "v")):
+        mul(e, V("xf", 512 + t, 1024, 4), bank(4 + t), 0.03125)
+    quant(V("xq", 128, 256), V("xs", 128, 256), V("xf", 512, 1024))
+    mm(bank(1), V("vq"), V("vp"), V("xq", 128, 256), V("xs", 128, 256))
+    dma("a", T.oc[:, 512:1024], V("xq", 128, 256), None, dt.uint8)
+    for k, e in enumerate("saaa"):
+        dma(e, T.osc[4 * k:4 * k + 4, :], V("xs", None, None, None, (32 * k, 32 * k + 4)))
+    cp(V("yo", 128, 256), bank(1))
+    dma("s", T.y[:, 128:256], V("yo", 128, 256))
+    return ops, sent[0]
+
+
+def emit(g, T, ops, sent):
+    eng = {"v": g.vector, "a": g.scalar, "t": g.tensor, "g": g, "s": g.sync}
+
+    def cols(v):
+        n = SCRATCH[v[0]][1][1]
+        m = np.zeros(n, bool)
+        if v[0] == "ps":
+            m[v[1] // 512 * 512:v[1] // 512 * 512 + 512] = True
+        else:
+            m[slice(v[1], v[2], v[3])] = True
+        return m
+
+    seen = {}
+    known = {q: 0 for q in eng}
+    at_issue, waits, needed = [], [], set()
+    for i, (q, fn, rd, wr, kind, pre) in enumerate(ops):
+        deps = set()
+        acc = [(v[0], cols(v), False) for v in rd] + [(v[0], cols(v), True) for v in wr]
+        for name, m, w in acc:
+            for j, mj, wj in seen.get(name, []):
+                if (w or wj or (name == "ps" and ops[j][0] != q)) and not known[q] >> j & 1 and (m & mj).any():
+                    deps.add(j)
+        for name, m, w in acc:
+            seen.setdefault(name, []).append((i, m, w))
+        ws = []
+        for j in sorted(deps, reverse=True):
+            if not known[q] >> j & 1:
+                ws.append(j)
+                known[q] |= at_issue[j] | 1 << j
+        waits.append(ws)
+        needed.update(ws)
+        at_issue.append(known[q])
+
+    known = {q: 0 for q in eng}
+    at_issue, tag, last, turn, count = [], {}, {}, {q: 0 for q in eng}, {}
+    ndma = [0]
+    open_dma = []
+
+    def wait(q, j):
+        if not known[q] >> j & 1:
+            eng[q].wait_ge(T.sem[tag[j][0]], tag[j][1])
+            known[q] |= at_issue[j] | 1 << j
+
+    for i, (q, fn, rd, wr, kind, pre) in enumerate(ops):
+        if pre is not None:
+            eng[q].wait_ge(pre[0], pre[1])
+        for j in waits[i]:
+            wait(q, j)
+        name = None
+        if kind == "d":
+            name = "dma%d" % ndma[0]
+            ndma[0] += 1
+            tag[i] = (name, 16)
+            if i not in needed:
+                open_dma.append(i)
+        elif kind == "c" and i in needed:
+            name = q + "%d" % (turn[q] % POOL[q])
+            turn[q] += 1
+            if name in last:
+                wait(q, last[name])
+            last[name] = i
+            count[name] = count.get(name, 0) + 1
+            tag[i] = (name, count[name])
+        at_issue.append(known[q])
+        ins = fn(eng[q])
+        if name is not None:
+            ins.then_inc(T.sem[name], 16 if kind == "d" else 1)
+    for j in open_dma:
+        wait(ops[j][0], j)
+    g.wait_ge(T.sem.sent, sent)
+
+
+def rank_program(g, core, T, topo):
+    rank = T.rank_of(core)
+    if rank is None:
+        return
+    ops, sent = build(T, topo, core, rank)
+    emit(g, T, ops, sent)

@@ -7,40 +7,18 @@ STAGES = ["d0", "d0b", "n0", "e0", "d1", "n1", "e1", "d2", "n2", "e2"]
 TINY = 2.0 ** -100
 BELOW = 1.0 - 2.0 ** -24
 BIG = 65536.0
-SHARE = {"r0": 7, "r": 3, "d0a": 5, "d0b": 2, "d": 6, "e": 6, "cut": [0, 384, 512], "ss": 3}
+SHARE = {"r0": 7, "r": 3, "d0a": 5, "d0b": 2, "d": 6, "e": 6, "cut": 384, "ss": 3}
 
-SCRATCH = {
-    "ps": ("psum", [128, 4096], F32),
-    "fa": ("sbuf", [128, 520], BF), "fb": ("sbuf", [128, 520], BF),
-    "mva": ("sbuf", [128, 1024], BF), "mvb": ("sbuf", [128, 1024], BF),
-    "xp": ("sbuf", [128, 1024], BF), "yp": ("sbuf", [128, 1024], BF), "ar": ("sbuf", [128, 1024], BF),
-    "fm": ("sbuf", [128, 512], BF), "xf": ("sbuf", [128, 1024], BF), "vt": ("sbuf", [128, 512], BF),
-    "wq": ("sbuf", [128, 512], CD), "wp": ("sbuf", [128, 512], U8),
-    "vq": ("sbuf", [128, 128], CD), "vp": ("sbuf", [128, 128], U8),
-    "xq": ("sbuf", [128, 256], CD), "xs": ("sbuf", [128, 256], U8),
-    "wa": ("sbuf", [128, 256], F32), "wb": ("sbuf", [128, 256], F32),
-    "va": ("sbuf", [128, 256], F32), "vb": ("sbuf", [128, 256], F32),
-    "ua": ("sbuf", [128, 256], F32), "dd": ("sbuf", [128, 512], F32), "ds": ("sbuf", [128, 256], F32),
-    "mk": ("sbuf", [128, 256], F32), "vd": ("sbuf", [128, 256], F32), "ee": ("sbuf", [128, 256], F32),
-    "dg": ("sbuf", [128, 256], BF), "pb": ("sbuf", [128, 256], BF), "dw": ("sbuf", [128, 256], F32),
-    "cm": ("sbuf", [128, 2400], BF), "cs": ("sbuf", [128, 3840], BF), "sg": ("sbuf", [128, 1920], BF),
-    "ra": ("sbuf", [128, 16], F32), "rku": ("sbuf", [128, 16], U16),
-    "oo": ("sbuf", [128, 256], BF), "ox": ("sbuf", [128, 256], F32), "oz": ("sbuf", [128, 256], F32),
-    "fr": ("sbuf", [128, 256], BF), "cu": ("sbuf", [128, 256], BF), "ofy": ("sbuf", [128, 16], U16),
-    "of": ("sbuf", [128, 256], F32), "ids": ("sbuf", [128, 256], BF), "so": ("sbuf", [128, 128], BF),
-    "sv": ("sbuf", [128, 128], BF),
-    "da": ("sbuf", [128, 128], F32), "dq": ("sbuf", [128, 128], F32),
-    "th": ("sbuf", [128, 96], F32),
-    "ub": ("sbuf", [128, 128], BF), "tb": ("sbuf", [128, 128], BF), "cc": ("sbuf", [128, 256], BF),
-    "bx": ("sbuf", [128, 128], F32), "jo": ("sbuf", [128, 32], F32),
-    "ofm": ("sbuf", [128, 16], U16), "yo": ("sbuf", [128, 256], F32),
-    "pi": ("sbuf", [128, 8], I32), "pf": ("sbuf", [128, 16], F32),
-    "ka": ("sbuf", [128, 128], F32), "pl": ("sbuf", [128, 32], U16), "im": ("sbuf", [128, 64], F32),
-    "rs32": ("sbuf", [128, 128], F32), "rsx": ("sbuf", [128, 128], F32),
-    "li": ("sbuf", [128, 32], I32), "lu": ("sbuf", [128, 32], U16),
-    "kc": ("sbuf", [128, 1024], BF), "ff": ("sbuf", [128, 128], F32),
-    "jb": ("sbuf", [128, 896], BF), "kb": ("sbuf", [128, 96], F32),
-}
+SCRATCH = {"ps": ("psum", [128, 4096], F32)}
+for _d, _l in ((BF, "fa520 fb520 mva1024 mvb1024 xp1024 yp1024 ar1024 fm512 xf1024 vt512 dg256 pb256 cm2400 cs3840 "
+                    "sg1920 oo256 fr256 cu256 ids256 so128 sv128 ub128 tb128 cc256 kc1024 jb896"),
+               (F32, "wa256 wb256 va256 vb256 ua256 dd512 ds256 mk256 vd256 ee256 dw256 ra16 ox256 oz256 of256 da128 "
+                     "dq128 th96 bx128 jo32 yo256 pf20 ka128 im64 rsa128 rsx128 ff128 kb96"),
+               (U16, "rku16 ofy16 ofm16 pl32 lu32"), (I32, "pi8 li32"),
+               (CD, "wq512 vq128 xq256"), (U8, "wp512 vp128 xs256")):
+    for _w in _l.split():
+        _n = _w.rstrip("0123456789")
+        SCRATCH[_n] = ("sbuf", [128, int(_w[len(_n):])], _d)
 for _s in STAGES:
     SCRATCH["q_" + _s] = ("sbuf", [128, 416], CD)
     SCRATCH["s_" + _s] = ("sbuf", [128, 416], U8)
@@ -169,13 +147,22 @@ def build(T, topo, core, rank):
     def plane(name, t, a=0, b=256, s=None):
         return V(name, 256 * t + a, 256 * t + b, s)
 
-    QF, RF, CF, ODD, Q12, EVN, SC, JM, JS, Q1, Q2, Q8, LT = [col("pf", j) for j in range(13)]
+    def half(name, h, a=0, n=64):
+        return V(name, a + n * h, a + n * h + n)
+
+    def turns(*steps):
+        for f in steps:
+            f(0)
+            f(1)
+
+    QF, RF, CF, ODD, Q12, P8, P4, EVN, SC, JM, JS, Q1, Q2, Q8, LT, QT = [col("pf", j) for j in range(16)]
     PAR = [EVN, ODD]
-    EXL, CXL, DXL, N4L, THL = V("lu", 0, 8), V("lu", 8, 16), V("lu", 16, 24), V("lu", 24, 26), V("lu", 26, 28)
-    CO, RS4, JMT, JST = V("kb", 0, 32), V("kb", 32, 64), V("kb", 64, 72), V("kb", 72, 80)
+    EXL, CXL, DXL, N4L, THL = V("lu", 0, 4), V("lu", 4, 8), V("lu", 8, 16), V("lu", 16, 17), V("lu", 18, 20)
+    CO, RS4, JMT, JST = V("kb", 0, 32), V("kb", 32, 48), V("kb", 64, 72), V("kb", 72, 80)
     C16, MK16, RS16, WX, WA, WB, WY = [V("kc", 128 * j, 128 * j + 128) for j in range(7)]
+    MK16H, RS16H, WXH = V("kc", 128, 192), V("kc", 256, 320), V("kc", 384, 448)
     JALL, JK, JODD, JHALF, ONES = V("jb", 0, 256), V("jb", 128, 256), V("jb", 256, 384), V("jb", 384, 640), V("jb", 640, 896)
-    TH, GG, GS = V("th", 0, 32), V("th", 32, 64), V("th", 64, 96)
+    TH = V("th", 0, 32)
     OFA, OFB, OFM, OFS = V("ofy", 0, 8), V("ofy", 8, 16), V("ofm", 0, 8), V("ofm", 8, 16)
 
     dma("s", V("fa", 0, 512), T.x[:, 0:512])
@@ -185,33 +172,37 @@ def build(T, topo, core, rank):
     iota(V("ka", 0, 32), [[32, 4], [0, 4], [16, 2]], -128)
     iota(V("ka", 32, 64), [[0, 4], [1, 4], [0, 2]], 0)
     iota(V("ka", 64, 128), [[1, 32], [0, 2]], 0)
+    iota(V("li", 16, 18), [[0, 2]], 31, False)
+    iota(V("li", 18, 20), [[64, 2]], 0, False)
     iota(JMT, [[32, 8]], 0)
-    iota(V("li", 24, 26), [[128, 2]], 31, False)
-    iota(V("li", 26, 28), [[16, 2]], 0, False)
-    iota(V("li", 0, 8), [[32, 4], [128, 2]], 31, False)
-    iota(V("li", 8, 16), [[4, 4], [16, 2]], 3, False)
-    iota(V("li", 16, 24), [[16, 8]], 15, False)
+    iota(V("li", 0, 4), [[32, 2], [64, 2]], 31, False)
+    iota(V("li", 4, 8), [[4, 2], [8, 2]], 3, False)
+    iota(V("li", 8, 16), [[16, 8]], 15, False)
     iota(CO, [[0, 8], [-1, 2], [0, 2]], 0)
-    iota(RS4, [[0, 8], [1, 4]], 0)
+    iota(RS4, [[0, 4], [1, 4]], 0)
     dma("s", V("wq"), T.wc[:, :], dt.uint8, None, [col("fa", 0), col("fb", 0)])
     dma("s", V("wp"), T.ws[:, :])
     dma("s", V("vt"), T.v[:, :])
     ms(V("fa", 512, 520), 0.0)
     ms(V("fb", 512, 520), 0.0)
-    ms(V("rs32"), 1.0)
+    ms(V("rsa", 0, 64), 1.0)
+    ms(V("rsx", 0, 64), 1e29)
     ts(col("pi", 1), col("pi", 0), 15, A.bitwise_and)
     ts(col("pi", 2), col("pi", 0), 31, A.bitwise_and)
     ts(col("pi", 3), col("pi", 0), 5, A.arith_shift_right)
     ts(col("pi", 4), col("pi", 0), 4, A.arith_shift_right, 1, A.bitwise_and)
     ts(col("pi", 5), col("pi", 0), 12, A.bitwise_and)
-    ms(V("rs32", 0, 128, 32), 0.0)
-    ms(V("rsx"), 1e29)
-    cp(V("pf", 0, 5), V("pi", 1, 6))
+    ts(col("pi", 6), col("pi", 0), 8, A.bitwise_and)
+    ts(col("pi", 7), col("pi", 0), 4, A.bitwise_and)
     ms(V("cc", 0, 256, 2), 0.0)
+    cp(V("pf", 0, 7), V("pi", 1, 8))
+    ms(V("rsa", 0, 64, 32), 0.0)
+    ms(V("rsx", 0, 64, 32), TINY)
     act(EVN, ODD, AF.Identity, 1.0, -1.0)
     act(Q1, QF, AF.Identity, 1.0)
     act(Q2, QF, AF.Identity, 0.0, 2.0)
     act(Q8, Q12, AF.Identity, 0.0, 8.0)
+    act(P8, P8, AF.Identity, 0.0, 2.0)
     ts(LT, QF, 15.0, A.is_lt)
     ts(MK16, C16, QF, A.is_equal)
     ts(RS16, C16, 1.0, A.min)
@@ -221,21 +212,20 @@ def build(T, topo, core, rank):
     act(SC, LT, AF.Identity, 1.0, 1.0 / BIG - 1.0)
     act(JM, LT, AF.Identity, 1.0, BIG - 1.0)
     act(JS, LT, AF.Identity, 1.0, BIG + 1023.0)
+    act(QT, P4, AF.Identity, P8, 8.0)
     act(V("ff"), WY, AF.Identity, 1.0, BELOW - 1.0)
+    act(Q2, Q2, AF.Identity, 0.0, JM)
     ts(V("ka", 0, 32), V("ka", 0, 32), QF, A.add)
     ts(V("ka", 32, 64), V("ka", 32, 64), CF, A.is_equal)
     tt(WX, WA, WB, A.max)
     tt(V("ka", 0, 32), V("ka", 0, 32), V("ka", 32, 64), A.mult)
     ts(V("im"), V("ka", 64, 128), RF, A.is_equal)
     ts(V("pl"), V("ka", 0, 32), 128.0, A.add)
-    ts(JMT, JMT, Q2, A.add, JM, A.mult)
-    ms(ONES, 1.0)
-    ms(V("rsx", 0, 128, 32), TINY)
-    ts(JST, JMT, JS, A.add)
-    ts(V("li", 24, 28), V("li", 24, 28), Q8, A.add)
+    ts(V("li", 16, 18), V("li", 16, 18), Q8, A.add)
+    ts(V("li", 18, 20), V("li", 18, 20), QT, A.add)
 
     def late_constants():
-        cp(V("lu", 0, 28), V("li", 0, 28))
+        cp(V("lu", 0, 20), V("li", 0, 20))
         for t in range(4):
             mov("g", plane("xp", t, 0, 128), V("fa", t, 512, 4))
         for t in range(4):
@@ -244,23 +234,19 @@ def build(T, topo, core, rank):
         iota(JODD, [[2, 128]], 1)
         iota(JHALF, [[1, 128], [0, 2]], 0)
         iota(V("ids", 128, 256), [[1, 128]], 128)
+        iota(ONES, [[0, 256]], 1)
 
     def q_full(st, f):
         quant(V("q_" + st, 0, 130), V("s_" + st, 0, 130), V(f, 0, 520))
-
-    def q_twice(st, mv):
-        quant(V("q_" + st, 160, 416), V("s_" + st, 160, 416), V(mv))
 
     def masked(e, mv, msrc, jobs):
         for j in jobs:
             t, w = j // 2, j % 2
             mul(e, V(mv, 4 * w + t, 1024, 8), msrc(t), PAR[w])
 
-    def pick_q(st, a, b):
+    def pick(st, a, b):
         o, i = V("tq_" + st, a, b), IND(V("q_" + st, 0, 130), V("pl", a // 16, b // 16))
         add("v", lambda e: e.tensor_copy(ap(o, dt.uint32), ap(i, dt.uint32)), [i], [o])
-
-    def pick_s(st, a, b):
         act(V("ts_" + st, a, b), IND(V("s_" + st, 0, 130), V("pl", a // 16, b // 16)))
 
     def products(st, b0, a, b):
@@ -269,37 +255,50 @@ def build(T, topo, core, rank):
             mm(bank(b0 + k), V("tq_" + st, 128 * k, 128 * k + 128), V("ts_" + st, 128 * k, 128 * k + 128),
                V("q_" + st, m, m + 128), V("s_" + st, m, m + 128))
 
-    def picks(st, b0):
+    def finish(st, mv, b0):
         cut = SHARE["cut"]
-        for a, b in zip(cut, cut[1:]):
-            pick_q(st, a, b)
-            pick_s(st, a, b)
-            products(st, b0, a, b)
+        quant(V("q_" + st, 160, 416), V("s_" + st, 160, 416), V(mv))
+        products(st, b0, 0, cut)
+        pick(st, cut, 512)
+        products(st, b0, cut, 512)
 
     def gram_front(st, msrc, fill, nv):
         fill("v", 0)
         fill("a", 2)
-        fill("v", 1)
         fill("a", 3)
-        masked("v", "mva", msrc, range(2))
+        if st[0] == "e":
+            masked("v", "mva", msrc, range(2))
+            fill("v", 1)
+            masked("v", "mva", msrc, [2])
+        else:
+            fill("v", 1)
+            masked("v", "mva", msrc, range(3))
         q_full(st, "fa")
         masked("a", "mva", msrc, range(nv, 8))
-        masked("v", "mva", msrc, range(2, nv))
-        q_twice(st, "mva")
-        picks(st, 0)
+        masked("v", "mva", msrc, range(3, nv))
+        pick(st, 0, SHARE["cut"])
+        finish(st, "mva", 0)
 
-    def diagonal(w, b0, k):
-        tt(V(w, 64 * k, 64 * k + 64), bank(b0 + k, 64 * (k // 3), 64), V("im"), A.mult)
+    def gram_back(w, v, b0, sizes=True):
+        def diagonal(k):
+            tt(V(w, 64 * k, 64 * k + 64), bank(b0 + k, 64 * (k // 3), 64), V("im"), A.mult)
 
-    def gram_back(w, v, b0):
-        for k in range(4):
-            diagonal(w, b0, k)
-        for h in range(2):
-            scan(V(v, 128 * h, 128 * h + 128), V("rsx"), V(w, h, 256, 2), A.min, A.max, TINY)
+        def gather(h, pi):
+            o, i = V(v, 128 * h + 64 * pi, 128 * h + 64 * pi + 64), V(w, 128 * h + pi, 128 * h + 128, 2)
+            if sizes:
+                scan(o, V("rsx", 0, 64), i, A.min, A.max, TINY)
+            else:
+                scan(o, V("rsa", 0, 64), i)
+        diagonal(0)
+        diagonal(1)
+        diagonal(2)
+        gather(0, 0)
+        gather(0, 1)
+        diagonal(3)
+        return lambda: (gather(1, 0), gather(1, 1))
 
-    def spread(v, a, e="v"):
-        mov(e, V("ua", a, a + 128), IND(V(v), EXL))
-        tr(V("dd", a, a + 128), V("ua", a, a + 128))
+    def wide(v, h):
+        return IND(half(v, h, 0, 128), EXL)
 
     def mask16(src, a):
         tt(V("mk", a, a + 128), src, MK16, A.mult)
@@ -316,7 +315,7 @@ def build(T, topo, core, rank):
     def near3(a):
         scan(V("pb", a, a + 128), RS16, V("dg", a, a + 128))
 
-    def count_v(slots, w, na, between=()):
+    def count_v(slots, w, a, na, between=()):
         between = list(between)
         lag = 1 + (len(between) > 1)
 
@@ -329,8 +328,12 @@ def build(T, topo, core, rank):
                 between.pop(0)()
             if i >= lag:
                 total(i - lag)
-        for i in range(len(slots) - lag, len(slots)):
+        for i in range(len(slots) - lag, len(slots) - 1):
             total(i)
+        tt(V("cs", w - 1, w * na, w), V("ra", a, a + na), V("pb", 16 * a + 15, 16 * (a + na), 16), A.add)
+        total(len(slots) - 1)
+        b = a + na + len(slots)
+        cp(V("rku", a, b), V("cs", w - 1, w * (b - a), w))
 
     def count_a(slots):
         held = []
@@ -342,17 +345,11 @@ def build(T, topo, core, rank):
                 y, n = held.pop()
                 act(y, y, AF.Relu, acc=col("ra", n))
             held.append((z, m))
-        if held:
-            y, n = held.pop()
-            act(y, y, AF.Relu, acc=col("ra", n))
+        y, n = held.pop()
+        act(y, y, AF.Relu, acc=col("ra", n))
 
     def ring(m):
         return (m, V("dd", 16 * m + 16, 16 * m + 256))
-
-    def places(a, na, b, w):
-        if na:
-            tt(V("cs", w - 1, w * na, w), V("ra", a, a + na), V("pb", 16 * a + 15, 16 * (a + na), 16), A.add)
-        cp(V("rku", a, b), V("cs", w - 1, w * (b - a), w))
 
     def pull(out, src):
         scan(out, WX, src)
@@ -370,27 +367,28 @@ def build(T, topo, core, rank):
             q_full("d0", "fa")
             masked("a", "mva", fa, range(na, 8))
             masked("v", "mva", fa, range(na))
-            q_twice("d0", "mva")
             q_full("d0b", "fb")
             late_constants()
-            picks("d0", 0)
+            pick("d0", 0, SHARE["cut"])
+            finish("d0", "mva", 0)
             masked("a", "mvb", fb, range(nb, 8))
             masked("v", "mvb", fb, range(nb))
-            gram_back("wa", "va", 0)
-            pick_q("d0b", 0, 256)
-            q_twice("d0b", "mvb")
-            pick_s("d0b", 0, 256)
-            products("d0b", 4, 0, 256)
-            pick_q("d0b", 256, 512)
-            pick_s("d0b", 256, 512)
-            products("d0b", 4, 256, 512)
-            spread("va", 0, "a")
-            gram_back("wb", "vb", 4)
-            below(0)
+            gram_back("wa", "va", 0)()
+            pick("d0b", 0, SHARE["cut"])
+            finish("d0b", "mvb", 4)
+            turns(lambda h: act(half("ua", h), wide("va", h)))
+            act(JMT, JMT, AF.Identity, Q2, JM)
             act(CO, CO, AF.Identity, 0.75, 0.5)
             act(RS4, RS4, AF.Sign)
+            act(JST, JMT, AF.Identity, JS)
+            tr(V("dd", 0, 128), V("ua", 0, 128))
+            rest = gram_back("wb", "vb", 4)
+            below(0)
+            act(half("ua", 0, 128), wide("vb", 0))
+            rest()
+            act(half("ua", 1, 128), wide("vb", 1))
             mask16(V("dd", 0, 128), 0)
-            spread("vb", 128, "a")
+            tr(V("dd", 128, 256), V("ua", 128, 256))
             wrap(0)
             below(128)
             na = SHARE["r0"]
@@ -402,12 +400,11 @@ def build(T, topo, core, rank):
             near1(V("dd", 128, 256), 128)
             near3(0)
             near2(128)
-            count_v([ring(m) for m in range(na, 16)], 240, na, [lambda: near3(128)])
-            places(0, na, 16, 240)
+            count_v([ring(m) for m in range(na, 16)], 240, 0, na, [lambda: near3(128)])
             cp(IND(V("oo"), V("rku")), JALL)
             pull(V("ox", 0, 128), V("oo", 0, 256, 2))
             pull(V("ox", 128, 256), V("oo", 1, 256, 2))
-            ts(V("ofy"), V("ox", 15, 256, 16), SC, A.mult)
+            turns(lambda h: ts(half("ofy", h, 0, 8), V("ox", 128 * h + 15, 128 * h + 128, 16), SC, A.mult))
         else:
             gram_front("d%d" % t_, lambda t: V("fa", t, 512, 4),
                        lambda e, t: mul(e, V("fa", t, 512, 4), bank(4 + t), 0.03125), SHARE["d"])
@@ -415,66 +412,88 @@ def build(T, topo, core, rank):
                 mov("g", plane("xp", t, 128, 256), V("fa", t, 512, 4))
             for t in range(4):
                 act(plane("xp", t, 0, 128), IND(plane("ar", t), OFS))
-            gram_back("wa", "va", 0)
-            spread("va", 128)
+            rest = gram_back("wa", "va", 0)
+            cp(half("ua", 0, 128), wide("va", 0))
+            rest()
+            tr(half("dd", 0, 128), half("ua", 0, 128))
+            cp(half("ua", 1, 128), wide("va", 1))
+            tt(half("mk", 0, 128), half("dd", 0, 128), MK16H, A.mult)
+            tr(half("dd", 1, 128), half("ua", 1, 128))
             below(128)
-            mask16(V("dd", 128, 256), 128)
-            wrap(128)
-            near1(V("dd", 128, 256), 128)
+            scan(half("vd", 0, 128), RS16H, half("mk", 0, 128))
             na = SHARE["r"]
             count_a([ring(m) for m in range(8, 8 + na)])
-            count_v([ring(m) for m in range(8 + na, 16)], 240, na, [lambda: near2(128), lambda: near3(128)])
+            tt(half("mk", 1, 128), half("dd", 1, 128), MK16H, A.mult)
+            near1(V("dd", 128, 256), 128)
+            scan(half("vd", 1, 128), RS16H, half("mk", 1, 128))
+            count_v([ring(m) for m in range(8 + na, 16)], 240, 8, na, [lambda: near2(128), lambda: near3(128)])
             act(V("dd", 0, 128), IND(V("dw"), OFS))
             if t_ == 2:
                 act(V("ids", 0, 128), IND(JHALF, OFS))
-            places(8, na, 16, 240)
             cp(IND(V("oo"), V("rku", 8, 16)), JK)
             ts(V("fr"), V("oo"), 0.0, A.is_equal)
             pull(V("ox", 0, 128), V("oo", 0, 256, 2))
             scan(V("cu"), ONES, V("fr"), first=-1.0)
             pull(V("ox", 128, 256), V("oo", 1, 256, 2))
-            pull(V("oz", 0, 128), V("cu", 0, 256, 2))
-            pull(V("oz", 128, 256), V("cu", 1, 256, 2))
-            tt(V("jo", 16, 32), V("ox", 15, 256, 16), V("oz", 15, 256, 16), A.max)
-            ts(V("ofy"), V("jo", 16, 32), SC, A.mult)
+            turns(lambda h: pull(half("oz", h, 0, 128), V("cu", h, 256, 2)),
+                  lambda h: tt(half("jo", h, 16, 8), V("ox", 128 * h + 15, 128 * h + 128, 16),
+                               V("oz", 128 * h + 15, 128 * h + 128, 16), A.max),
+                  lambda h: ts(half("ofy", h, 0, 8), half("jo", h, 16, 8), SC, A.mult))
 
         st = "n%d" % t_
         for t, e in ((0, "v"), (2, "a"), (1, "v"), (3, "a")):
             mov(e, V("fa", t, 512, 4), IND(plane("xp", t), OFA))
-        q_full(st, "fa")
         for t in range(4):
             act(plane("yp", t, 1, 256, 2), IND(plane("xp", t), OFB))
             mov("g", plane("yp", t, 0, 256, 2), V("fa", t, 512, 4))
-        pick_q(st, 0, 512)
-        pick_s(st, 0, 512)
-        masked("v", "mva", lambda t: plane("yp", t, 1, 256, 2), range(8))
-        q_twice(st, "mva")
-        products(st, 0, 0, 512)
         cp(V("da"), IND(V("dd", 0, 256), OFA))
-        diagonal("wa", 0, 0)
+        q_full(st, "fa")
         tr(V("dq"), V("da"))
-        for k in range(1, 4):
-            diagonal("wa", 0, k)
+        pick(st, 0, SHARE["cut"])
         tt(TH, IND(V("dq"), THL), CO, A.mult)
-        scan(V("va", 0, 128), V("rs32"), V("wa", 0, 256, 2))
+        masked("v", "mva", lambda t: plane("yp", t, 1, 256, 2), range(8))
         ts(V("th", 1, 32, 2), V("th", 1, 32, 2), -BELOW, A.mult)
-        scan(V("va", 128, 256), V("rs32"), V("wa", 1, 256, 2))
-        tt(GG, IND(V("va"), N4L), TH, A.is_ge)
-        scan(GS, RS4, GG)
-        ts(V("ub"), IND(GS, CXL), -0.5, A.mult, 1.0, A.add)
-        tr(V("cc", 1, 256, 2), V("ub"))
-        for t in (2, 3, 0, 1):
-            scan(plane("ar", t), V("cc"), plane("yp", t))
+        finish(st, "mva", 0)
+        rest = gram_back("wa", "va", 0, False)
+        chain = [lambda h: tt(half("th", h, 32, 16), IND(half("va", h, 0, 128), N4L), half("th", h, 0, 16), A.is_ge),
+                 lambda h: scan(half("th", h, 64, 16), RS4, half("th", h, 32, 16)),
+                 lambda h: ts(half("ub", h), IND(half("th", h, 64, 16), CXL), -0.5, A.mult, 1.0, A.add),
+                 lambda h: tr(V("cc", 128 * h + 1, 128 * h + 128, 2), half("ub", h))]
+        chain[0](0)
+        rest()
+        for i in range(3):
+            chain[i + 1](0)
+            chain[i](1)
+
+        def reduce(t, h):
+            scan(plane("ar", t, 128 * h, 128 * h + 128), half("cc", h, 0, 128), plane("yp", t, 128 * h, 128 * h + 128))
+        reduce(2, 0)
+        chain[3](1)
+        for t, h in ((0, 0), (3, 0), (2, 1), (0, 1), (3, 1), (1, 0), (1, 1)):
+            reduce(t, h)
         gram_front("e%d" % t_, lambda t: plane("ar", t, 1, 256, 2),
                    lambda e, t: mov(e, V("fa", t, 512, 4), plane("ar", t, 1, 256, 2)), SHARE["e"])
-        gram_back("wa", "va", 0)
-        tt(V("ub"), IND(V("va"), EXL), V("dq"), A.is_ge)
-        tr(V("tb"), V("ub"))
-        pull(V("bx"), V("tb"))
-        tt(V("jo", 0, 8), V("bx", 15, 128, 16), JMT, A.add)
-        ts(OFM, V("jo", 0, 8), SC, A.mult)
+        rest = gram_back("wa", "va", 0)
+        chain = [lambda h: tt(half("ub", h), wide("va", h), half("dq", h), A.is_ge),
+                 lambda h: tr(half("tb", h), half("ub", h)),
+                 lambda h: scan(half("bx", h), WXH, half("tb", h)),
+                 lambda h: tt(half("jo", h, 0, 4), V("bx", 64 * h + 15, 64 * h + 64, 16), half("kb", h, 64, 4), A.add),
+                 lambda h: ts(half("ofm", h, 0, 4), half("jo", h, 0, 4), SC, A.mult)]
+        chain[0](0)
+        rest()
+        for i in range(4):
+            chain[i + 1](0)
+            chain[i](1)
+
+        def leave(e, t, h):
+            mov(e, V("fm", 256 * h + t, 256 * h + 256, 4), IND(plane("ar", t), half("ofm", h, 0, 4)))
+        leave("a", 2, 0)
+        leave("v", 0, 0)
+        chain[4](1)
+        leave("a", 3, 0)
+        leave("v", 1, 0)
         for t, e in ((0, "v"), (2, "a"), (1, "v"), (3, "a")):
-            mov(e, V("fm", t, 512, 4), IND(plane("ar", t), OFM))
+            leave(e, t, 1)
         mq, msn, lq, ls = V("mq%d" % t_), V("ms%d" % t_), V("lq%d" % t_), V("ls%d" % t_)
         quant(mq, msn, V("fm"))
         rid, pid, _e = topo.addr(T.cores[(rank + STEP[t_]) % len(T.cores)])
@@ -486,28 +505,27 @@ def build(T, topo, core, rank):
         sent[0] += 2 * len(eng)
 
         if t_ < 2:
-            tt(V("ua", 0, 128), IND(V("va"), EXL), V("dq"), A.min)
+            turns(lambda h: tt(half("ua", h), wide("va", h), half("dq", h), A.min))
             iota(V("oo"), [[0, 256]], 0)
-            tt(V("sv"), JODD, V("tb"), A.subtract)
-            tr(V("ds", 0, 128), V("ua", 0, 128))
+            turns(lambda h: tr(half("ds", h), half("ua", h)))
             act(V("ds", 128, 256), V("ds", 0, 128), AF.Identity, 0.0, BELOW)
-            mask16(V("ds", 0, 128), 0)
+            turns(lambda h: tt(half("mk", h), half("ds", h), MK16H, A.mult))
             near1(V("ds", 0, 128), 0)
             wrap(0)
+            tt(V("sv"), JODD, V("tb"), A.subtract)
             na = SHARE["ss"]
             win = [(m, V("ds", 16 * m + 16, 16 * m + 128)) for m in range(8)]
             count_a(win[:na])
             mov("g", V("dd", 256, 384), V("ds", 128, 256))
             mov("g", V("dw", 0, 256, 2), V("ds", 0, 128))
             mov("g", V("dw", 1, 256, 2), V("ds", 0, 128))
-            count_v(win[na:], 112, na, [lambda: near2(0), lambda: near3(0)])
-            places(0, na, 8, 112)
+            count_v(win[na:], 112, 0, na, [lambda: near2(0), lambda: near3(0)])
             cp(IND(V("so"), V("rku", 0, 8)), V("sv"))
-            pull(V("bx"), V("so"))
+            turns(lambda h: scan(half("bx", h), WXH, half("so", h)))
             ts(OFS, V("bx", 15, 128, 16), SC, A.mult)
         else:
-            quant(V("vq"), V("vp"), V("vt"))
             tt(V("jo", 8, 16), JST, V("bx", 15, 128, 16), A.subtract)
+            quant(V("vq"), V("vp"), V("vt"))
             ts(OFS, V("jo", 8, 16), SC, A.mult)
             for t, e in ((0, "v"), (2, "a"), (1, "v"), (3, "a")):
                 mov(e, V("xf", t, 512, 4), IND(plane("ar", t), OFS))

@@ -7,21 +7,25 @@ STAGES = ["d0", "d0b", "n0", "e0", "d1", "n1", "e1", "d2", "n2", "e2"]
 TINY = 2.0 ** -100
 BELOW = 1.0 - 2.0 ** -24
 BIG = 65536.0
-SHARE = {"r0": 7, "r": 3, "d0a": 5, "d0b": 2, "d": 6, "e": 6, "cut": 384, "ss": 3}
+SMALL = 2.0 ** -26
+PAD = 16
+TUNE = {"r0": 3, "r0b": 4, "r": 4, "ss": 3, "wake": 200, "dma": 2200, "far": 3000, "send": 350, "least": 64, "extra": 0,
+        "gather": 1.56, "scatter": 3.8, "abh": 2, "mh": 1, "spare": 60, "turns": 6}
 
 SCRATCH = {"ps": ("psum", [128, 4096], F32)}
-for _d, _l in ((BF, "fa520 fb520 mva1024 mvb1024 xp1024 yp1024 ar1024 fm512 xf1024 vt512 dg256 pb256 cm2400 cs3840 "
-                    "sg1920 oo256 fr256 cu256 ids256 so128 sv128 ub128 tb128 cc256 kc1024 jb896"),
-               (F32, "wa256 wb256 va256 vb256 ua256 dd512 ds256 mk256 vd256 ee256 dw256 ra16 ox256 oz256 of256 da128 "
-                     "dq128 th96 bx128 jo32 yo256 pf20 ka128 im64 rsa128 rsx128 ff128 kb96"),
-               (U16, "rku16 ofy16 ofm16 pl32 lu32"), (I32, "pi8 li32"),
+for _d, _l in ((BF, "fa528 fb528 fk528 ab1040 ar1040 mvd1024 mvb1024 mvn1024 mve1024 xp1024 ap1024 fm512 xf1024 vt512 "
+                    "cma2048 cmb2048 csa1024 csb1024 oo512 on256 ox512 ids256 so128 fi256 fs256 ub128 uc128 cc256 bx256 "
+                    "by256 bz128 kc1792 jb1024"),
+               (F32, "wd256 wb256 wn256 we256 vd256 vb256 vn256 ve256 ua256 us128 dd512 mk256 wr256 ee256 dw256 ra16 "
+                     "of256 da256 dq128 th96 yo256 pf24 ka160 im64 rs128 ff128 kb32"),
+               (U16, "rku16 rks8 ofy16 ofm32 ofz32 ofs8 pl96 lu40"), (I32, "pi12"),
                (CD, "wq512 vq128 xq256"), (U8, "wp512 vp128 xs256")):
     for _w in _l.split():
         _n = _w.rstrip("0123456789")
         SCRATCH[_n] = ("sbuf", [128, int(_w[len(_n):])], _d)
 for _s in STAGES:
-    SCRATCH["q_" + _s] = ("sbuf", [128, 416], CD)
-    SCRATCH["s_" + _s] = ("sbuf", [128, 416], U8)
+    SCRATCH["q_" + _s] = ("sbuf", [128, 544], CD)
+    SCRATCH["s_" + _s] = ("sbuf", [128, 544], U8)
     SCRATCH["tq_" + _s] = ("sbuf", [128, 512], CD)
     SCRATCH["ts_" + _s] = ("sbuf", [128, 512], U8)
 for _t in range(3):
@@ -34,6 +38,7 @@ POOL = {"v": 48, "a": 36, "t": 12, "g": 16}
 NDMA = 24
 SEMAPHORES = ([k + "%d" % i for k in POOL for i in range(POOL[k])] + ["dma%d" % i for i in range(NDMA)]
               + ["arr0", "arr1", "arr2", "sent"])
+PLAN = {}
 
 
 def V(name, a=None, b=None, s=None, p=None):
@@ -44,13 +49,19 @@ def IND(win, off):
     return win[:5] + (off,)
 
 
+def size(v):
+    if v[5] is not None:
+        return 16 * size(v[5])
+    return len(range(*slice(v[1], v[2], v[3]).indices(SCRATCH[v[0]][1][1])))
+
+
 def lanes(T, topo, rank):
     n = len(T.cores)
     sets = [topo.engines(T.cores[rank], T.cores[(rank + s) % n]) for s in STEP]
     return [k for k in sets[0] if all(k in z for z in sets)]
 
 
-def build(T, topo, core, rank):
+def build(T, topo, rank):
     ops = []
     sent = [0]
     A, AF = AluOpType, ActivationFunctionType
@@ -66,77 +77,86 @@ def build(T, topo, core, rank):
             x = x.indirect(ap(off))
         return x
 
-    def views(*xs):
-        r = []
-        for x in xs:
-            if isinstance(x, tuple):
-                r.append(x)
-                if x[5] is not None:
-                    r.append(x[5])
-        return r
+    def add(alt, rd, wr, kind="c", pre=None):
+        rd = [x for x in rd if isinstance(x, tuple)]
+        wr = [x for x in wr if isinstance(x, tuple)]
+        ops.append((alt, rd + [x[5] for x in rd + wr if x[5] is not None], wr, kind, pre))
 
-    def add(q, fn, rd, wr, kind="c", pre=None):
-        w = [x for x in wr if isinstance(x, tuple)]
-        ops.append((q, fn, views(*rd) + [x[5] for x in w if x[5] is not None], w, kind, pre))
-
-    def cp(o, i):
-        add("v", lambda e: e.tensor_copy(ap(o), ap(i)), [i], [o])
+    def time(q, o, ins, rate=1.0):
+        if o[5] is not None:
+            return 60 + TUNE["scatter"] * size(o)
+        if ins and ins[0][5] is not None:
+            return (60 if q == "v" else 78) + TUNE["gather"] * size(o)
+        if q == "v" and rate == 1.0 and all(SCRATCH[x[0]][2] in (BF, U16) for x in [o] + ins):
+            rate = 0.5
+        return max(TUNE["least"], rate * size(o)) + TUNE["extra"]
 
     def tt(o, x, y, op):
-        add("v", lambda e: e.tensor_tensor(ap(o), ap(x), ap(y), op), [x, y], [o])
+        add({"v": (lambda e: e.tensor_tensor(ap(o), ap(x), ap(y), op), time("v", o, [x, y], 1.01 if x[0] == "ps" else 2.0))},
+            [x, y], [o])
 
     def ts(o, x, s1, op0, s2=None, op1=None):
         if op1 is None:
-            add("v", lambda e: e.tensor_scalar(ap(o), ap(x), ap(s1), None, op0), [x, s1], [o])
+            f = lambda e: e.tensor_scalar(ap(o), ap(x), ap(s1), None, op0)
         else:
-            add("v", lambda e: e.tensor_scalar(ap(o), ap(x), ap(s1), ap(s2), op0, op1), [x, s1, s2], [o])
+            f = lambda e: e.tensor_scalar(ap(o), ap(x), ap(s1), ap(s2), op0, op1)
+        add({"v": (f, time("v", o, [x]))}, [x, s1, s2], [o])
 
     def scan(o, d0, d1, op0=A.mult, op1=A.add, first=0.0):
-        add("v", lambda e: e.tensor_tensor_scan(ap(o), ap(d0), ap(d1), ap(first), op0, op1), [d0, d1, first], [o])
+        add({"v": (lambda e: e.tensor_tensor_scan(ap(o), ap(d0), ap(d1), first, op0, op1), time("v", o, [d0, d1]))},
+            [d0, d1], [o])
 
     def tr(o, i):
-        add("v", lambda e: e.transpose(ap(o), ap(i)), [i], [o])
+        add({"v": (lambda e: e.transpose(ap(o), ap(i)), time("v", o, [i]))}, [i], [o])
 
     def ms(o, c):
-        add("v", lambda e: e.memset(ap(o), c), [], [o])
+        add({"v": (lambda e: e.memset(ap(o), c), time("v", o, []))}, [], [o])
 
-    def act(o, i, f=AF.Copy, bias=0.0, scale=1.0, acc=None):
+    def act(o, i, f, bias=0.0, scale=1.0, acc=None):
         if acc is not None:
-            add("a", lambda e: e.activation(ap(o), ap(i), f, bias=ap(bias), scale=ap(scale), accum_out=ap(acc)),
-                [i, bias, scale], [o, acc])
-        elif bias == 0.0 and scale == 1.0:
-            add("a", lambda e: e.activation(ap(o), ap(i), f), [i], [o])
+            g = lambda e: e.activation(ap(o), ap(i), f, bias=ap(bias), scale=ap(scale), accum_out=ap(acc))
         else:
-            add("a", lambda e: e.activation(ap(o), ap(i), f, bias=ap(bias), scale=ap(scale)), [i, bias, scale], [o])
+            g = lambda e: e.activation(ap(o), ap(i), f, bias=ap(bias), scale=ap(scale))
+        add({"a": (g, time("a", o, [i]) + (24 if acc else 0))}, [i, bias, scale], [o, acc])
 
-    def mul(q, o, i, s):
-        if q == "v":
-            ts(o, i, s, A.mult)
-        else:
-            act(o, i, AF.Identity, scale=s)
+    def lin(o, i, scale, bias=None, on="va"):
+        alt = {}
+        if "v" in on:
+            if bias is None:
+                alt["v"] = (lambda e: e.tensor_scalar(ap(o), ap(i), ap(scale), None, A.mult), time("v", o, [i]))
+            else:
+                alt["v"] = (lambda e: e.tensor_scalar(ap(o), ap(i), ap(scale), ap(bias), A.mult, A.add), time("v", o, [i]))
+        if "a" in on:
+            alt["a"] = (lambda e: e.activation(ap(o), ap(i), AF.Identity, bias=ap(0.0 if bias is None else bias),
+                                               scale=ap(scale)), time("a", o, [i]))
+        add(alt, [i, scale, bias], [o])
 
-    def mov(q, o, i):
-        if q == "v":
-            cp(o, i)
-        elif q == "a":
-            act(o, i)
-        else:
-            add("g", lambda e: e.affine_select(ap(o), ap(i), [[0, 128]], A.is_ge, 0.0, 0, 0), [i], [o])
+    def mov(o, i, on="va"):
+        alt = {}
+        if "v" in on:
+            alt["v"] = (lambda e: e.tensor_copy(ap(o), ap(i)), time("v", o, [i]))
+        if "a" in on:
+            alt["a"] = (lambda e: e.activation(ap(o), ap(i), AF.Copy), time("a", o, [i]))
+        if "g" in on:
+            alt["g"] = (lambda e: e.affine_select(ap(o), ap(i), [[0, size(o)]], A.is_ge, 0.0, 0, 0), 205 + 2 * size(o))
+        add(alt, [i], [o])
 
     def quant(c, s, i):
-        add("v", lambda e: e.quantize_mx(ap(c), ap(s), ap(i)), [i], [c, s])
+        add({"v": (lambda e: e.quantize_mx(ap(c), ap(s), ap(i)), 15 + 0.265 * size(i))}, [i], [c, s])
 
     def mm(o, lq, ls, rq, rs, pre=None):
-        add("t", lambda e: e.matmul_mx(ap(o), ap(lq), ap(ls), ap(rq), ap(rs), True, True), [lq, ls, rq, rs], [o], "c", pre)
+        add({"t": (lambda e: e.matmul_mx(ap(o), ap(lq), ap(ls), ap(rq), ap(rs), True, True), 16 + size(o))},
+            [lq, ls, rq, rs], [o], "c", pre)
 
-    def iota(o, pat, base, fl=True):
-        if fl:
-            add("g", lambda e: e.iota(ap(o), pat, base, 0, allow_small_or_imprecise_dtypes=True), [], [o])
+    def iota(o, pat, base, cm=0):
+        if SCRATCH[o[0]][2] == I32:
+            f = lambda e: e.iota(ap(o), pat, base, cm)
         else:
-            add("g", lambda e: e.iota(ap(o), pat, base, 0), [], [o])
+            f = lambda e: e.iota(ap(o), pat, base, cm, allow_small_or_imprecise_dtypes=True)
+        add({"g": (f, 156 + 2 * size(o))}, [], [o])
 
     def dma(q, o, i, oc=None, ic=None, after=()):
-        add(q, lambda e: e.dma_start(ap(o, oc), ap(i, ic)), [i] + list(after), [o], "d")
+        add({q: (lambda e: e.dma_start(ap(o, oc), ap(i, ic)), 100)}, [i] + list(after), [o], "d")
 
     def col(name, j):
         return V(name, j, j + 1)
@@ -144,461 +164,378 @@ def build(T, topo, core, rank):
     def bank(b, a=0, n=128):
         return V("ps", 512 * b + a, 512 * b + a + n)
 
-    def plane(name, t, a=0, b=256, s=None):
-        return V(name, 256 * t + a, 256 * t + b, s)
+    def plane(name, t, a=0, b=256):
+        return V(name, 256 * t + a, 256 * t + b)
 
     def half(name, h, a=0, n=64):
         return V(name, a + n * h, a + n * h + n)
 
-    def turns(*steps):
-        for f in steps:
-            f(0)
-            f(1)
-
-    QF, RF, CF, ODD, Q12, P8, P4, EVN, SC, JM, JS, Q1, Q2, Q8, LT, QT = [col("pf", j) for j in range(16)]
+    QF, RF, CF, ODD, PL, T4, Q7, Q8, B2, EVN, SC, SC4, T44, Q1, Q2, Q21, Q22, P2, P21, P22, X1, X2 = [
+        col("pf", j) for j in range(22)]
     PAR = [EVN, ODD]
-    EXL, CXL, DXL, N4L, THL = V("lu", 0, 4), V("lu", 4, 8), V("lu", 8, 16), V("lu", 16, 17), V("lu", 18, 20)
-    CO, RS4, JMT, JST = V("kb", 0, 32), V("kb", 32, 48), V("kb", 64, 72), V("kb", 72, 80)
-    C16, MK16, RS16, WX, WA, WB, WY = [V("kc", 128 * j, 128 * j + 128) for j in range(7)]
-    MK16H, RS16H, WXH = V("kc", 128, 192), V("kc", 256, 320), V("kc", 384, 448)
-    JALL, JK, JODD, JHALF, ONES = V("jb", 0, 256), V("jb", 128, 256), V("jb", 256, 384), V("jb", 384, 640), V("jb", 640, 896)
-    TH = V("th", 0, 32)
-    OFA, OFB, OFM, OFS = V("ofy", 0, 8), V("ofy", 8, 16), V("ofm", 0, 8), V("ofm", 8, 16)
+    EXL, CXL, N4L, NL, DXL = V("lu", 0, 4), V("lu", 4, 8), V("lu", 8, 9), V("lu", 10, 18), V("lu", 18, 26)
+    RS4 = V("kb", 0, 16)
+    C16, MK16, RS16, WX, C8, WM, WN = [V("kc", 128 * j, 128 * j + 128) for j in range(7)]
+    C32, WP, TMP = V("kc", 896, 1152), V("kc", 1152, 1408), V("kc", 1408, 1664)
+    MK16H, RS16H = V("kc", 128, 192), V("kc", 256, 320)
+    JALL, JKS, JHALF, ONES, MS = V("jb", 0, 256), V("jb", 896, 1024), V("jb", 256, 512), V("jb", 512, 768), V("fs")
 
-    dma("s", V("fa", 0, 512), T.x[:, 0:512])
-    dma("a", V("fb", 0, 512), T.x[:, 512:1024])
-    add("g", lambda e: e.iota(ap(col("pi", 0)), [[0, 1]], 0, 1), [], [col("pi", 0)])
-    iota(C16, [[0, 8], [1, 16]], 0)
-    iota(V("ka", 0, 32), [[32, 4], [0, 4], [16, 2]], -128)
+    def mark(o, c, spots):
+        tmp = V(TMP[0], TMP[1], TMP[1] + size(o))
+        for i, (s, v) in enumerate(spots):
+            ts(tmp if i else o, c, s, A.is_equal, v - 1.0, A.mult)
+            if i:
+                tt(o, o, tmp, A.add)
+        ts(o, o, 1.0, A.add)
+
+    dma("s", V("fa", PAD), T.x[:, 0:512])
+    dma("a", V("fb", PAD), T.x[:, 512:1024])
+    dma("s", V("wq"), T.wc[:, :], dt.uint8, None, [col("fa", PAD), col("fb", PAD)])
+    dma("s", V("wp"), T.ws[:, :], None, None, [col("fa", PAD), col("fb", PAD)])
+    dma("s", V("vt"), T.v[:, :], None, None, [col("fa", PAD), col("fb", PAD)])
+    iota(col("pi", 0), [[0, 1]], 0, 1)
+    for f in ("fa", "fb", "fk", "ab", "ar"):
+        ms(V(f, 0, PAD), 0.0)
+    p = col("pi", 0)
+    ts(col("pi", 1), p, 15, A.bitwise_and)
+    ts(col("pi", 2), p, 31, A.bitwise_and)
+    ts(col("pi", 3), p, 5, A.arith_shift_right)
+    ts(col("pi", 4), p, 4, A.arith_shift_right, 1, A.bitwise_and)
+    ts(col("pi", 5), p, 2, A.arith_shift_right, 3, A.bitwise_and)
+    ts(col("pi", 6), p, 3, A.bitwise_and)
+    ts(col("pi", 7), p, 7, A.bitwise_and)
+    ts(col("pi", 8), p, 3, A.arith_shift_right, 1, A.bitwise_and)
+    ts(col("pi", 9), p, 2, A.arith_shift_right, 1, A.bitwise_and)
+    mov(V("pf", 0, 9), V("pi", 1, 10), "v")
+    lin(EVN, ODD, -1.0, 1.0)
+    iota(V("ka", 0, 32), [[32, 4], [0, 4], [16, 2]], 0)
     iota(V("ka", 32, 64), [[0, 4], [1, 4], [0, 2]], 0)
-    iota(V("ka", 64, 128), [[1, 32], [0, 2]], 0)
-    iota(V("li", 16, 18), [[0, 2]], 31, False)
-    iota(V("li", 18, 20), [[64, 2]], 0, False)
-    iota(JMT, [[32, 8]], 0)
-    iota(V("li", 0, 4), [[32, 2], [64, 2]], 31, False)
-    iota(V("li", 4, 8), [[4, 2], [8, 2]], 3, False)
-    iota(V("li", 8, 16), [[16, 8]], 15, False)
-    iota(CO, [[0, 8], [-1, 2], [0, 2]], 0)
-    iota(RS4, [[0, 4], [1, 4]], 0)
-    dma("s", V("wq"), T.wc[:, :], dt.uint8, None, [col("fa", 0), col("fb", 0)])
-    dma("s", V("wp"), T.ws[:, :])
-    dma("s", V("vt"), T.v[:, :])
-    ms(V("fa", 512, 520), 0.0)
-    ms(V("fb", 512, 520), 0.0)
-    ms(V("rsa", 0, 64), 1.0)
-    ms(V("rsx", 0, 64), 1e29)
-    ts(col("pi", 1), col("pi", 0), 15, A.bitwise_and)
-    ts(col("pi", 2), col("pi", 0), 31, A.bitwise_and)
-    ts(col("pi", 3), col("pi", 0), 5, A.arith_shift_right)
-    ts(col("pi", 4), col("pi", 0), 4, A.arith_shift_right, 1, A.bitwise_and)
-    ts(col("pi", 5), col("pi", 0), 12, A.bitwise_and)
-    ts(col("pi", 6), col("pi", 0), 8, A.bitwise_and)
-    ts(col("pi", 7), col("pi", 0), 4, A.bitwise_and)
-    ms(V("cc", 0, 256, 2), 0.0)
-    cp(V("pf", 0, 7), V("pi", 1, 8))
-    ms(V("rsa", 0, 64, 32), 0.0)
-    ms(V("rsx", 0, 64, 32), TINY)
-    act(EVN, ODD, AF.Identity, 1.0, -1.0)
-    act(Q1, QF, AF.Identity, 1.0)
-    act(Q2, QF, AF.Identity, 0.0, 2.0)
-    act(Q8, Q12, AF.Identity, 0.0, 8.0)
-    act(P8, P8, AF.Identity, 0.0, 2.0)
-    ts(LT, QF, 15.0, A.is_lt)
-    ts(MK16, C16, QF, A.is_equal)
-    ts(RS16, C16, 1.0, A.min)
-    ts(WY, C16, QF, A.is_lt)
-    ts(WA, C16, QF, A.not_equal)
-    ts(WB, C16, Q1, A.is_equal, BIG, A.mult)
-    act(SC, LT, AF.Identity, 1.0, 1.0 / BIG - 1.0)
-    act(JM, LT, AF.Identity, 1.0, BIG - 1.0)
-    act(JS, LT, AF.Identity, 1.0, BIG + 1023.0)
-    act(QT, P4, AF.Identity, P8, 8.0)
-    act(V("ff"), WY, AF.Identity, 1.0, BELOW - 1.0)
-    act(Q2, Q2, AF.Identity, 0.0, JM)
     ts(V("ka", 0, 32), V("ka", 0, 32), QF, A.add)
     ts(V("ka", 32, 64), V("ka", 32, 64), CF, A.is_equal)
-    tt(WX, WA, WB, A.max)
-    tt(V("ka", 0, 32), V("ka", 0, 32), V("ka", 32, 64), A.mult)
-    ts(V("im"), V("ka", 64, 128), RF, A.is_equal)
-    ts(V("pl"), V("ka", 0, 32), 128.0, A.add)
-    ts(V("li", 16, 18), V("li", 16, 18), Q8, A.add)
-    ts(V("li", 18, 20), V("li", 18, 20), QT, A.add)
+    for i, (s, b) in enumerate(((1.0, 2.0), (2.0, 2.0), (2.0, 3.0))):
+        z = V("ka", 64 + 32 * i, 96 + 32 * i)
+        lin(z, V("ka", 0, 32), s, b, "v")
+        tt(z, z, V("ka", 32, 64), A.mult)
+        mov(V("pl", 32 * i, 32 * i + 32), z, "v")
+    iota(V("im"), [[1, 32], [0, 2]], 0)
+    ts(V("im"), V("im"), RF, A.is_equal)
+    ms(V("rs", 0, 64), 1.0)
+    ms(V("rs", 64, 128), 1e29)
+    ms(V("rs", 0, 64, 32), 0.0)
+    ms(V("rs", 64, 128, 32), TINY)
+    iota(V("th", 0, 4), [[32, 2], [64, 2]], 31)
+    iota(V("th", 4, 8), [[4, 4]], 3)
+    iota(V("th", 8, 10), [[0, 2]], 31)
+    iota(V("th", 10, 18), [[2, 8]], 0)
+    iota(V("th", 18, 26), [[0, 8]], 15)
+    lin(X1, B2, 64.0, None, "v")
+    lin(X2, Q8, 32.0, X1, "v")
+    ts(V("th", 8, 10), V("th", 8, 10), X2, A.add)
+    lin(X1, Q7, 16.0, None, "v")
+    ts(V("th", 10, 18), V("th", 10, 18), X1, A.add, Q8, A.add)
+    ts(V("th", 18, 26), V("th", 18, 26), X1, A.add)
+    mov(V("lu", 0, 26), V("th", 0, 26), "v")
+    iota(C16, [[0, 8], [1, 16]], 0)
+    iota(C8, [[0, 16], [1, 8]], 0)
+    iota(C32, [[0, 8], [1, 32]], 0)
+    iota(V("ff"), [[1, 16], [0, 8]], 0)
+    iota(RS4, [[0, 4], [1, 4]], 0)
+    iota(JALL, [[1, 256]], 0)
+    iota(JHALF, [[1, 128], [0, 2]], 0)
+    iota(V("ids", 128, 256), [[1, 128]], 128)
+    iota(ONES, [[0, 256]], 1)
+    iota(V("cc", 0, 256, 2), [[0, 128]], 0)
+    iota(V("fi", 1, 256, 2), [[2, 128]], 0)
+    iota(V("jb", 768, 896), [[0, 64], [-1, 2]], 0)
+    MS = V("jb", 768, 896)
+    lin(JKS, V("jb", 128, 256), SMALL)
+    ts(MK16, C16, QF, A.is_equal)
+    ts(RS16, C16, 1.0, A.min)
+    ts(RS4, RS4, 1.0, A.min)
+    ts(V("ff"), V("ff"), QF, A.is_lt)
+    lin(V("ff"), V("ff"), BELOW - 1.0, 1.0, "v")
+    ts(SC, QF, 15.0, A.is_lt, 1.0 / BIG - 1.0, A.mult)
+    ts(SC, SC, 1.0, A.add)
+    ts(SC4, PL, 3.0, A.is_lt, 4.0 / BIG - 4.0, A.mult)
+    ts(SC4, SC4, 4.0, A.add)
+    for o, i, s, b in ((T44, T4, 1.0, 4.0), (Q1, QF, 1.0, 1.0), (Q2, QF, 2.0, 0.0), (Q21, QF, 2.0, 1.0), (Q22, QF, 2.0, 2.0),
+                       (P2, PL, 2.0, 0.0), (P21, PL, 2.0, 1.0), (P22, PL, 2.0, 2.0)):
+        lin(o, i, s, b, "v")
+    mark(WX, C16, [(QF, 0.0), (Q1, BIG + 1.0)])
+    mark(WP, C32, [(Q2, 0.0), (Q21, 1.0 / SMALL + 1.0), (Q22, BIG + 1.0)])
+    mark(WM, C8, [(P2, 0.0), (P22, BIG + 1.0)])
+    mark(WN, C8, [(P2, 0.0), (P21, -1.0), (P22, BIG + 1.0)])
+    for t in range(4):
+        mov(plane("xp", t, 0, 128), V("fa", PAD + t, None, 4), "g")
+        mov(plane("xp", t, 128, 256), V("fb", PAD + t, None, 4), "g")
 
-    def late_constants():
-        cp(V("lu", 0, 20), V("li", 0, 20))
-        for t in range(4):
-            mov("g", plane("xp", t, 0, 128), V("fa", t, 512, 4))
-        for t in range(4):
-            mov("g", plane("xp", t, 128, 256), V("fb", t, 512, 4))
-        iota(JALL, [[1, 256]], 0)
-        iota(JODD, [[2, 128]], 1)
-        iota(JHALF, [[1, 128], [0, 2]], 0)
-        iota(V("ids", 128, 256), [[1, 128]], 128)
-        iota(ONES, [[0, 256]], 1)
-
-    def q_full(st, f):
-        quant(V("q_" + st, 0, 130), V("s_" + st, 0, 130), V(f, 0, 520))
-
-    def masked(e, mv, msrc, jobs):
-        for j in jobs:
-            t, w = j // 2, j % 2
-            mul(e, V(mv, 4 * w + t, 1024, 8), msrc(t), PAR[w])
-
-    def pick(st, a, b):
-        o, i = V("tq_" + st, a, b), IND(V("q_" + st, 0, 130), V("pl", a // 16, b // 16))
-        add("v", lambda e: e.tensor_copy(ap(o, dt.uint32), ap(i, dt.uint32)), [i], [o])
-        act(V("ts_" + st, a, b), IND(V("s_" + st, 0, 130), V("pl", a // 16, b // 16)))
-
-    def products(st, b0, a, b):
-        for k in range(a // 128, b // 128):
-            m = 160 + min(64 * k, 128)
-            mm(bank(b0 + k), V("tq_" + st, 128 * k, 128 * k + 128), V("ts_" + st, 128 * k, 128 * k + 128),
-               V("q_" + st, m, m + 128), V("s_" + st, m, m + 128))
-
-    def finish(st, mv, b0):
-        cut = SHARE["cut"]
-        quant(V("q_" + st, 160, 416), V("s_" + st, 160, 416), V(mv))
-        products(st, b0, 0, cut)
-        pick(st, cut, 512)
-        products(st, b0, cut, 512)
-
-    def gram_front(st, msrc, fill, nv):
-        fill("v", 0)
-        fill("a", 2)
-        fill("a", 3)
-        if st[0] == "e":
-            masked("v", "mva", msrc, range(2))
-            fill("v", 1)
-            masked("v", "mva", msrc, [2])
-        else:
-            fill("v", 1)
-            masked("v", "mva", msrc, range(3))
-        q_full(st, "fa")
-        masked("a", "mva", msrc, range(nv, 8))
-        masked("v", "mva", msrc, range(3, nv))
-        pick(st, 0, SHARE["cut"])
-        finish(st, "mva", 0)
-
-    def gram_back(w, v, b0, sizes=True):
-        def diagonal(k):
-            tt(V(w, 64 * k, 64 * k + 64), bank(b0 + k, 64 * (k // 3), 64), V("im"), A.mult)
-
-        def gather(h, pi):
-            o, i = V(v, 128 * h + 64 * pi, 128 * h + 64 * pi + 64), V(w, 128 * h + pi, 128 * h + 128, 2)
-            if sizes:
-                scan(o, V("rsx", 0, 64), i, A.min, A.max, TINY)
-            else:
-                scan(o, V("rsa", 0, 64), i)
-        diagonal(0)
-        diagonal(1)
-        diagonal(2)
-        gather(0, 0)
-        gather(0, 1)
-        diagonal(3)
-        return lambda: (gather(1, 0), gather(1, 1))
+    def gram(st, f, wide, mv, w, v, b0, lst):
+        q, s = "q_" + st, "s_" + st
+        quant(V(q, 0, 130), V(s, 0, 130), V(f, 8, 528))
+        if wide:
+            quant(V(q, 130, 258), V(s, 130, 258), V(f, 528, 1040))
+        n = TUNE["mh"]
+        for h in range(n):
+            for t in range(4):
+                for par in range(2):
+                    z = 1024 // n
+                    src = (V(f, PAD + z * h + 4 + t, PAD + z * h + z, 8) if wide
+                           else V(f, PAD + z // 2 * h + t, PAD + z // 2 * (h + 1), 4))
+                    lin(V(mv, z * h + 4 * par + t, z * h + z, 8), src, PAR[par])
+        for h in range(2):
+            m = 288 + 128 * h
+            quant(V(q, m, m + 128), V(s, m, m + 128), half(mv, h, 0, 512))
+            top = 258 if wide and h else 130
+            off = V("pl", 32 * lst + 16 * h, 32 * lst + 16 * h + 16)
+            o, i = half("tq_" + st, h, 0, 256), IND(V(q, 0, top), off)
+            add({"v": (lambda e, o=o, i=i: e.tensor_copy(ap(o, dt.uint32), ap(i, dt.uint32)), time("v", o, [i]))}, [i], [o])
+            mov(half("ts_" + st, h, 0, 256), IND(V(s, 0, top), off), "a")
+            for k in (2 * h, 2 * h + 1):
+                mm(bank(b0 + k), half("tq_" + st, k, 0, 128), half("ts_" + st, k, 0, 128), V(q, m, m + 128), V(s, m, m + 128))
+                tt(half(w, k), bank(b0 + k, 64 * (k % 2), 64), V("im"), A.mult)
+            for pi in range(2):
+                o, i = V(v, 128 * h + 64 * pi, 128 * h + 64 * pi + 64), V(w, 128 * h + pi, 128 * h + 128, 2)
+                if st[0] == "n":
+                    scan(o, V("rs", 0, 64), i)
+                else:
+                    scan(o, V("rs", 64, 128), i, A.min, A.max, TINY)
 
     def wide(v, h):
         return IND(half(v, h, 0, 128), EXL)
 
-    def mask16(src, a):
-        tt(V("mk", a, a + 128), src, MK16, A.mult)
-
-    def wrap(a):
-        scan(V("vd", a, a + 128), RS16, V("mk", a, a + 128))
-
-    def near1(src, a):
-        tt(V("ee", a, a + 128), src, V("ff"), A.mult)
-
-    def near2(a):
-        tt(V("dg", a, a + 128), IND(V("vd", a, a + 128), DXL), V("ee", a, a + 128), A.is_gt)
-
-    def near3(a):
-        scan(V("pb", a, a + 128), RS16, V("dg", a, a + 128))
-
-    def count_v(slots, w, a, na, between=()):
-        between = list(between)
-        lag = 1 + (len(between) > 1)
-
-        def total(i):
-            z = V("cm", w * i, w * i + w)
-            scan(V("cs", w * (na + i), w * (na + i + 1)), z, z, A.add, A.max, col("pb", 16 * slots[i][0] + 15))
-        for i, (m, win) in enumerate(slots):
-            ts(V("cm", w * i, w * i + w), win, col("vd", 16 * m + 15), A.is_lt)
-            if between:
-                between.pop(0)()
-            if i >= lag:
-                total(i - lag)
-        for i in range(len(slots) - lag, len(slots) - 1):
-            total(i)
-        tt(V("cs", w - 1, w * na, w), V("ra", a, a + na), V("pb", 16 * a + 15, 16 * (a + na), 16), A.add)
-        total(len(slots) - 1)
-        b = a + na + len(slots)
-        cp(V("rku", a, b), V("cs", w - 1, w * (b - a), w))
-
-    def count_a(slots):
-        held = []
-        for i, (m, win) in enumerate(slots):
-            w = win[2] - win[1]
-            z = V("sg", w * i, w * i + w)
-            act(z, win, AF.Sign, col("vd", 16 * m + 15), -1.0)
-            if held:
-                y, n = held.pop()
-                act(y, y, AF.Relu, acc=col("ra", n))
-            held.append((z, m))
-        y, n = held.pop()
-        act(y, y, AF.Relu, acc=col("ra", n))
-
-    def ring(m):
-        return (m, V("dd", 16 * m + 16, 16 * m + 256))
-
-    def pull(out, src):
-        scan(out, WX, src)
-
-    def below(a):
-        act(V("dd", 256 + a, 384 + a), V("dd", a, a + 128), AF.Identity, 0.0, BELOW)
+    def places(a, low, slot, w, na, cm, cs, out, times):
+        lin(V("dd", low, low + 128), V("dd", a, a + 128), BELOW)
+        for h in range(2):
+            tt(half("mk", h, slot), half("dd", h, a), MK16H, A.mult)
+            scan(half("wr", h, slot), RS16H, half("mk", h, slot))
+        tt(V("ee", slot, slot + 128), IND(V("dd", a, a + 128), NL), V("ff"), A.mult)
+        tt(V(cm, 8 * w, 8 * w + 128), IND(V("wr", slot, slot + 128), DXL), V("ee", slot, slot + 128), A.is_gt)
+        n = (w + 16) // 2
+        for m in range(8):
+            win, me = V("dd", a + 16 * m + 16, a + 16 * m + 16 + w), col("wr", slot + 16 * m + 15)
+            if m < na:
+                act(V(cm, m, 8 * w, 8), win, AF.Sign, me, -1.0)
+                z = V(cm, m, 16 * n, 8)
+                act(z, z, AF.Relu, acc=col("ra", slot // 16 + m))
+            else:
+                ts(V(cm, m, 8 * w, 8), win, me, A.is_lt)
+                scan(V(cs, n * m, n * m + n), V(cm, m, 8 * n, 8), V(cm, 8 * n + m, 16 * n, 8), A.add, A.add)
+        b = out[1]
+        if na:
+            ts(V(out[0], b, b + na), V("ra", slot // 16, slot // 16 + na), times, A.mult)
+        ts(V(out[0], b + na, b + 8), V(cs, n * na + n - 1, 8 * n, n), times, A.mult)
 
     eng = lanes(T, topo, rank)
     mask = sum(1 << k for k in eng)
 
     for t_ in range(3):
         if t_ == 0:
-            fa, fb = (lambda t: V("fa", t, 512, 4)), (lambda t: V("fb", t, 512, 4))
-            na, nb = SHARE["d0a"], SHARE["d0b"]
-            q_full("d0", "fa")
-            masked("a", "mva", fa, range(na, 8))
-            masked("v", "mva", fa, range(na))
-            q_full("d0b", "fb")
-            late_constants()
-            pick("d0", 0, SHARE["cut"])
-            finish("d0", "mva", 0)
-            masked("a", "mvb", fb, range(nb, 8))
-            masked("v", "mvb", fb, range(nb))
-            gram_back("wa", "va", 0)()
-            pick("d0b", 0, SHARE["cut"])
-            finish("d0b", "mvb", 4)
-            turns(lambda h: act(half("ua", h), wide("va", h)))
-            act(JMT, JMT, AF.Identity, Q2, JM)
-            act(CO, CO, AF.Identity, 0.75, 0.5)
-            act(RS4, RS4, AF.Sign)
-            act(JST, JMT, AF.Identity, JS)
-            tr(V("dd", 0, 128), V("ua", 0, 128))
-            rest = gram_back("wb", "vb", 4)
-            below(0)
-            act(half("ua", 0, 128), wide("vb", 0))
-            rest()
-            act(half("ua", 1, 128), wide("vb", 1))
-            mask16(V("dd", 0, 128), 0)
-            tr(V("dd", 128, 256), V("ua", 128, 256))
-            wrap(0)
-            below(128)
-            na = SHARE["r0"]
-            count_a([ring(m) for m in range(na)])
-            mask16(V("dd", 128, 256), 128)
-            near1(V("dd", 0, 128), 0)
-            wrap(128)
-            near2(0)
-            near1(V("dd", 128, 256), 128)
-            near3(0)
-            near2(128)
-            count_v([ring(m) for m in range(na, 16)], 240, 0, na, [lambda: near3(128)])
-            cp(IND(V("oo"), V("rku")), JALL)
-            pull(V("ox", 0, 128), V("oo", 0, 256, 2))
-            pull(V("ox", 128, 256), V("oo", 1, 256, 2))
-            turns(lambda h: ts(half("ofy", h, 0, 8), V("ox", 128 * h + 15, 128 * h + 128, 16), SC, A.mult))
+            gram("d0", "fa", False, "mvd", "wd", "vd", 0, 0)
+            gram("d0b", "fb", False, "mvb", "wb", "vb", 4, 0)
+            for h in range(2):
+                for a, v in ((0, "vd"), (128, "vb")):
+                    mov(half("ua", h, a), wide(v, h))
+                    tr(half("dd", h, a), half("ua", h, a))
+            places(0, 256, 0, 240, TUNE["r0"], "cma", "csa", V("rku", 0, 8), 1.0)
+            places(128, 384, 128, 240, TUNE["r0b"], "cmb", "csb", V("rku", 8, 16), 1.0)
+            mov(IND(V("on"), V("rku")), JALL, "v")
+            for h in range(2):
+                scan(half("ox", h, 0, 128), WX, half("on", h, 0, 128), A.mult, A.max)
+                ts(half("ofy", h, 0, 8), V("ox", 128 * h + 15, 128 * h + 128, 16), SC, A.mult)
         else:
-            gram_front("d%d" % t_, lambda t: V("fa", t, 512, 4),
-                       lambda e, t: mul(e, V("fa", t, 512, 4), bank(4 + t), 0.03125), SHARE["d"])
             for t in range(4):
-                mov("g", plane("xp", t, 128, 256), V("fa", t, 512, 4))
+                lin(V("fk", PAD + t, None, 4), bank(4 + t), 0.03125)
+                mov(plane("xp", t, 128, 256), V("fk", PAD + t, None, 4), "g")
+            gram("d%d" % t_, "fk", False, "mvd", "wd", "vd", 0, 0)
+            for h in range(2):
+                mov(half("ua", h), wide("vd", h))
+                tr(half("dd", h, 128), half("ua", h))
+            places(128, 384, 128, 240, TUNE["r"], "cmb", "csb", V("rku", 8, 16), 2.0)
+            mov(IND(V("oo"), V("rku", 8, 16)), JKS, "v")
+            scan(V("oo", 1, 512, 2), ONES, V("oo", 0, 512, 2), A.mult, A.subtract, -1.0)
+            for h in range(2):
+                scan(half("ox", h, 0, 256), WP, half("oo", h, 0, 256), A.mult, A.max)
+                ts(half("ofy", h, 0, 8), V("ox", 256 * h + 31, 256 * h + 256, 32), SC, A.mult)
+
+        n = TUNE["abh"]
+        for h in range(n):
             for t in range(4):
-                act(plane("xp", t, 0, 128), IND(plane("ar", t), OFS))
-            rest = gram_back("wa", "va", 0)
-            cp(half("ua", 0, 128), wide("va", 0))
-            rest()
-            tr(half("dd", 0, 128), half("ua", 0, 128))
-            cp(half("ua", 1, 128), wide("va", 1))
-            tt(half("mk", 0, 128), half("dd", 0, 128), MK16H, A.mult)
-            tr(half("dd", 1, 128), half("ua", 1, 128))
-            below(128)
-            scan(half("vd", 0, 128), RS16H, half("mk", 0, 128))
-            na = SHARE["r"]
-            count_a([ring(m) for m in range(8, 8 + na)])
-            tt(half("mk", 1, 128), half("dd", 1, 128), MK16H, A.mult)
-            near1(V("dd", 128, 256), 128)
-            scan(half("vd", 1, 128), RS16H, half("mk", 1, 128))
-            count_v([ring(m) for m in range(8 + na, 16)], 240, 8, na, [lambda: near2(128), lambda: near3(128)])
-            act(V("dd", 0, 128), IND(V("dw"), OFS))
-            if t_ == 2:
-                act(V("ids", 0, 128), IND(JHALF, OFS))
-            cp(IND(V("oo"), V("rku", 8, 16)), JK)
-            ts(V("fr"), V("oo"), 0.0, A.is_equal)
-            pull(V("ox", 0, 128), V("oo", 0, 256, 2))
-            scan(V("cu"), ONES, V("fr"), first=-1.0)
-            pull(V("ox", 128, 256), V("oo", 1, 256, 2))
-            turns(lambda h: pull(half("oz", h, 0, 128), V("cu", h, 256, 2)),
-                  lambda h: tt(half("jo", h, 16, 8), V("ox", 128 * h + 15, 128 * h + 128, 16),
-                               V("oz", 128 * h + 15, 128 * h + 128, 16), A.max),
-                  lambda h: ts(half("ofy", h, 0, 8), half("jo", h, 16, 8), SC, A.mult))
-
-        st = "n%d" % t_
-        for t, e in ((0, "v"), (2, "a"), (1, "v"), (3, "a")):
-            mov(e, V("fa", t, 512, 4), IND(plane("xp", t), OFA))
-        for t in range(4):
-            act(plane("yp", t, 1, 256, 2), IND(plane("xp", t), OFB))
-            mov("g", plane("yp", t, 0, 256, 2), V("fa", t, 512, 4))
-        cp(V("da"), IND(V("dd", 0, 256), OFA))
-        q_full(st, "fa")
-        tr(V("dq"), V("da"))
-        pick(st, 0, SHARE["cut"])
-        tt(TH, IND(V("dq"), THL), CO, A.mult)
-        masked("v", "mva", lambda t: plane("yp", t, 1, 256, 2), range(8))
-        ts(V("th", 1, 32, 2), V("th", 1, 32, 2), -BELOW, A.mult)
-        finish(st, "mva", 0)
-        rest = gram_back("wa", "va", 0, False)
-        chain = [lambda h: tt(half("th", h, 32, 16), IND(half("va", h, 0, 128), N4L), half("th", h, 0, 16), A.is_ge),
-                 lambda h: scan(half("th", h, 64, 16), RS4, half("th", h, 32, 16)),
-                 lambda h: ts(half("ub", h), IND(half("th", h, 64, 16), CXL), -0.5, A.mult, 1.0, A.add),
-                 lambda h: tr(V("cc", 128 * h + 1, 128 * h + 128, 2), half("ub", h))]
-        chain[0](0)
-        rest()
-        for i in range(3):
-            chain[i + 1](0)
-            chain[i](1)
-
-        def reduce(t, h):
-            scan(plane("ar", t, 128 * h, 128 * h + 128), half("cc", h, 0, 128), plane("yp", t, 128 * h, 128 * h + 128))
-        reduce(2, 0)
-        chain[3](1)
-        for t, h in ((0, 0), (3, 0), (2, 1), (0, 1), (3, 1), (1, 0), (1, 1)):
-            reduce(t, h)
-        gram_front("e%d" % t_, lambda t: plane("ar", t, 1, 256, 2),
-                   lambda e, t: mov(e, V("fa", t, 512, 4), plane("ar", t, 1, 256, 2)), SHARE["e"])
-        rest = gram_back("wa", "va", 0)
-        chain = [lambda h: tt(half("ub", h), wide("va", h), half("dq", h), A.is_ge),
-                 lambda h: tr(half("tb", h), half("ub", h)),
-                 lambda h: scan(half("bx", h), WXH, half("tb", h)),
-                 lambda h: tt(half("jo", h, 0, 4), V("bx", 64 * h + 15, 64 * h + 64, 16), half("kb", h, 64, 4), A.add),
-                 lambda h: ts(half("ofm", h, 0, 4), half("jo", h, 0, 4), SC, A.mult)]
-        chain[0](0)
-        rest()
-        for i in range(4):
-            chain[i + 1](0)
-            chain[i](1)
-
-        def leave(e, t, h):
-            mov(e, V("fm", 256 * h + t, 256 * h + 256, 4), IND(plane("ar", t), half("ofm", h, 0, 4)))
-        leave("a", 2, 0)
-        leave("v", 0, 0)
-        chain[4](1)
-        leave("a", 3, 0)
-        leave("v", 1, 0)
-        for t, e in ((0, "v"), (2, "a"), (1, "v"), (3, "a")):
-            leave(e, t, 1)
+                z = 1024 // n
+                mov(V("ab", PAD + z * h + t, PAD + z * h + z, 4), IND(plane("xp", t), half("ofy", h, 0, 16 // n)))
+        for h in range(2):
+            mov(half("da", h, 0, 128), IND(V("dd", 0, 256), half("ofy", h, 0, 8)))
+            tr(half("dq", h), V("da", 128 * h, 128 * h + 128, 2))
+        if t_ == 2:
+            mov(V("of"), IND(V("ids"), V("ofy")))
+            dma("s", T.ol[:, :], V("of", None, None, None, (0, 128, 16)))
+        for i, c in ((0, 0.75), (2, 0.25)):
+            lin(V("th", i, 32, 4), V("dq", 0, 128, 16), c)
+            lin(V("th", i + 1, 32, 4), V("th", i, 32, 4), -BELOW)
+        gram("n%d" % t_, "ab", True, "mvn", "wn", "vn", 0, 1)
+        for h in range(2):
+            tt(half("th", h, 32, 16), IND(half("vn", h, 0, 128), N4L), half("th", h, 0, 16), A.is_ge)
+            scan(half("th", h, 64, 16), RS4, half("th", h, 32, 16))
+            lin(half("uc", h), IND(half("th", h, 64, 16), CXL), -0.5, 1.0)
+            tr(V("cc", 128 * h + 1, 128 * h + 128, 2), half("uc", h))
+            for t in range(4):
+                a = PAD + 512 * h + t
+                scan(V("ar", a, PAD + 512 * h + 512, 4), half("cc", h, 0, 128), V("ab", a, PAD + 512 * h + 512, 4))
+        gram("e%d" % t_, "ar", True, "mve", "we", "ve", 0, 2)
+        for h in range(2):
+            tt(half("ub", h), wide("ve", h), half("dq", h), A.is_ge)
+            tr(V("fi", 128 * h, 128 * h + 128, 2), half("ub", h))
+            scan(half("bx", h, 0, 128), WM, half("fi", h, 0, 128))
+            ts(half("ofm", h, 0, 16), V("bx", 128 * h + 7, 128 * h + 128, 8), SC4, A.mult, T4, A.add)
+            for z in (2 * h, 2 * h + 1):
+                mov(half("fm", z, 0, 128), IND(V("ar", PAD), half("ofm", z, 0, 8)))
         mq, msn, lq, ls = V("mq%d" % t_), V("ms%d" % t_), V("lq%d" % t_), V("ls%d" % t_)
         quant(mq, msn, V("fm"))
         rid, pid, _e = topo.addr(T.cores[(rank + STEP[t_]) % len(T.cores)])
         arr = T.sem["arr%d" % t_]
-        add("g", lambda e, mq=mq, lq=lq, arr=arr, rid=rid, pid=pid:
-            e.remote_dma(ap(lq, dt.uint8), ap(mq, dt.uint8), arr, T.sem.sent, pid, rid, mask), [mq], [], "r")
-        add("g", lambda e, msn=msn, ls=ls, arr=arr, rid=rid, pid=pid:
-            e.remote_dma(ap(ls), ap(msn), arr, T.sem.sent, pid, rid, mask), [msn], [], "r")
+        add({"g": (lambda e, mq=mq, lq=lq, arr=arr, rid=rid, pid=pid:
+                   e.remote_dma(ap(lq, dt.uint8), ap(mq, dt.uint8), arr, T.sem.sent, pid, rid, mask), TUNE["send"])},
+            [mq], [lq], "r")
+        add({"g": (lambda e, msn=msn, ls=ls, arr=arr, rid=rid, pid=pid:
+                   e.remote_dma(ap(ls), ap(msn), arr, T.sem.sent, pid, rid, mask), TUNE["send"])}, [msn], [ls], "r")
         sent[0] += 2 * len(eng)
 
         if t_ < 2:
-            turns(lambda h: tt(half("ua", h), wide("va", h), half("dq", h), A.min))
-            iota(V("oo"), [[0, 256]], 0)
-            turns(lambda h: tr(half("ds", h), half("ua", h)))
-            act(V("ds", 128, 256), V("ds", 0, 128), AF.Identity, 0.0, BELOW)
-            turns(lambda h: tt(half("mk", h), half("ds", h), MK16H, A.mult))
-            near1(V("ds", 0, 128), 0)
-            wrap(0)
-            tt(V("sv"), JODD, V("tb"), A.subtract)
-            na = SHARE["ss"]
-            win = [(m, V("ds", 16 * m + 16, 16 * m + 128)) for m in range(8)]
-            count_a(win[:na])
-            mov("g", V("dd", 256, 384), V("ds", 128, 256))
-            mov("g", V("dw", 0, 256, 2), V("ds", 0, 128))
-            mov("g", V("dw", 1, 256, 2), V("ds", 0, 128))
-            count_v(win[na:], 112, 0, na, [lambda: near2(0), lambda: near3(0)])
-            cp(IND(V("so"), V("rku", 0, 8)), V("sv"))
-            turns(lambda h: scan(half("bx", h), WXH, half("so", h)))
-            ts(OFS, V("bx", 15, 128, 16), SC, A.mult)
+            iota(V("oo", 0, 512, 2), [[0, 256]], -1)
+            for h in range(2):
+                tt(half("us", h), wide("ve", h), half("dq", h), A.min)
+                tr(half("dd", h, 128), half("us", h))
+                scan(half("fs", h, 0, 128), MS, half("fi", h, 0, 128))
+            places(128, 256, 0, 112, TUNE["ss"], "cma", "csa", V("rks", 0, 8), 1.0)
+            mov(V("dw", 0, 256, 2), V("dd", 128, 256), "g")
+            mov(V("dw", 1, 256, 2), V("dd", 128, 256), "g")
+            for t in range(4):
+                mov(plane("ap", t), V("ar", PAD + t, None, 4), "g")
+            mov(IND(V("so"), V("rks")), V("fs", 1, 256, 2), "v")
+            scan(V("bz"), WX, V("so"))
+            ts(V("ofs"), V("bz", 15, 128, 16), SC, A.mult, 1.0, A.add)
+            for t in range(4):
+                mov(plane("xp", t, 0, 128), IND(plane("ap", t), V("ofs")))
+            mov(V("dd", 0, 128), IND(V("dw"), V("ofs")))
+            if t_ == 1:
+                mov(V("ids", 0, 128), IND(JHALF, V("ofs")))
         else:
-            tt(V("jo", 8, 16), JST, V("bx", 15, 128, 16), A.subtract)
+            for h in range(2):
+                scan(half("by", h, 0, 128), WN, half("fi", h, 0, 128))
+                ts(half("ofz", h, 0, 16), V("by", 128 * h + 7, 128 * h + 128, 8), SC4, A.mult, T44, A.add)
+                mov(half("xf", h, 0, 256), IND(V("ar", PAD), half("ofz", h, 0, 16)))
             quant(V("vq"), V("vp"), V("vt"))
-            ts(OFS, V("jo", 8, 16), SC, A.mult)
-            for t, e in ((0, "v"), (2, "a"), (1, "v"), (3, "a")):
-                mov(e, V("xf", t, 512, 4), IND(plane("ar", t), OFS))
             quant(V("xq", 0, 128), V("xs", 0, 128), V("xf", 0, 512))
             mm(bank(0), V("vq"), V("vp"), V("xq", 0, 128), V("xs", 0, 128))
-            act(V("of", 0, 256, 2), IND(V("ids"), OFA))
-            act(V("of", 1, 256, 2), IND(V("ids"), OFB))
             dma("s", T.oc[:, 0:512], V("xq", 0, 128), None, dt.uint8)
-            cp(V("yo", 0, 128), bank(0))
-            dma("s", T.ol[:, :], V("of", None, None, None, (0, 128, 16)))
+            mov(V("yo", 0, 128), bank(0))
             dma("s", T.y[:, 0:128], V("yo", 0, 128))
         come = 2 * len(lanes(T, topo, (rank - STEP[t_]) % len(T.cores)))
-        for b in (0, 2, 1, 3):
-            mm(bank(4 + b), V("wq", 128 * b, 128 * b + 128), V("wp", 128 * b, 128 * b + 128), lq, ls,
-               (arr, come) if b == 0 else None)
+        for b in range(4):
+            mm(bank(4 + b), half("wq", b, 0, 128), half("wp", b, 0, 128), lq, ls, (arr, come))
 
-    for t, e in ((0, "v"), (2, "a"), (1, "v"), (3, "v")):
-        mul(e, V("xf", 512 + t, 1024, 4), bank(4 + t), 0.03125)
+    for t in range(4):
+        lin(V("xf", 512 + t, 1024, 4), bank(4 + t), 0.03125)
     quant(V("xq", 128, 256), V("xs", 128, 256), V("xf", 512, 1024))
     mm(bank(1), V("vq"), V("vp"), V("xq", 128, 256), V("xs", 128, 256))
     dma("a", T.oc[:, 512:1024], V("xq", 128, 256), None, dt.uint8)
     for k, e in enumerate("saaa"):
         dma(e, T.osc[4 * k:4 * k + 4, :], V("xs", None, None, None, (32 * k, 32 * k + 4)))
-    cp(V("yo", 128, 256), bank(1))
+    mov(V("yo", 128, 256), bank(1))
     dma("s", T.y[:, 128:256], V("yo", 128, 256))
     return ops, sent[0]
 
 
-def emit(g, T, ops, sent):
-    eng = {"v": g.vector, "a": g.scalar, "t": g.tensor, "g": g, "s": g.sync}
-
+def order(ops):
     def cols(v):
-        n = SCRATCH[v[0]][1][1]
-        m = np.zeros(n, bool)
+        m = np.zeros(SCRATCH[v[0]][1][1], bool)
         if v[0] == "ps":
             m[v[1] // 512 * 512:v[1] // 512 * 512 + 512] = True
         else:
             m[slice(v[1], v[2], v[3])] = True
-        return m
+        return int.from_bytes(np.packbits(m).tobytes(), "big")
 
-    seen = {}
-    known = {q: 0 for q in eng}
-    at_issue, waits, needed = [], [], set()
-    for i, (q, fn, rd, wr, kind, pre) in enumerate(ops):
-        deps = set()
-        acc = [(v[0], cols(v), False) for v in rd] + [(v[0], cols(v), True) for v in wr]
-        for name, m, w in acc:
-            for j, mj, wj in seen.get(name, []):
-                if (w or wj or (name == "ps" and ops[j][0] != q)) and not known[q] >> j & 1 and (m & mj).any():
-                    deps.add(j)
+    seen, deps = {}, []
+    for i, (alt, rd, wr, kind, pre) in enumerate(ops):
+        acc = [(v[0], cols(v), v[0] == "ps") for v in rd] + [(v[0], cols(v), True) for v in wr]
+        deps.append({j for name, m, w in acc for j, mj, wj in seen.get(name, []) if (w or wj) and m & mj})
         for name, m, w in acc:
             seen.setdefault(name, []).append((i, m, w))
-        ws = []
-        for j in sorted(deps, reverse=True):
-            if not known[q] >> j & 1:
-                ws.append(j)
-                known[q] |= at_issue[j] | 1 << j
-        waits.append(ws)
-        needed.update(ws)
-        at_issue.append(known[q])
+    late = {"c": TUNE["wake"], "d": TUNE["dma"], "r": TUNE["far"]}
+    n = len(ops)
+    togo = [0.0] * n
+    for i in range(n - 1, -1, -1):
+        togo[i] += min(c for f, c in ops[i][0].values()) + late[ops[i][3]]
+        for j in deps[i]:
+            togo[j] = max(togo[j], togo[i])
+    users = [set() for i in range(n)]
+    for i in range(n):
+        for j in deps[i]:
+            users[j].add(i)
+
+    def place(seq, back):
+        busy, start, end, queue = {q: [] for q in "vatgs"}, {}, {}, {}
+        for i in seq:
+            if back:
+                ready = max([end[j] for j in users[i]], default=0.0) + late[ops[i][3]]
+            else:
+                ready = max([end[j] + late[ops[j][3]] for j in deps[i]], default=0.0)
+            best = None
+            for q, (f, c) in ops[i][0].items():
+                t, k, row = ready, 0, busy[q]
+                while k < len(row) and t + c > row[k][0]:
+                    t = max(t, row[k][1])
+                    k += 1
+                mark = t + c + (TUNE["spare"] if q == "v" else 0)
+                if best is None or mark < best[0]:
+                    best = (mark, t, q, k, t + c)
+            busy[best[2]].insert(best[3], (best[1], best[4]))
+            start[i], end[i], queue[i] = best[1], best[4], best[2]
+        return max(end[i] + (0 if back else late[ops[i][3]]) for i in seq), start, end, queue
+
+    seq, best = sorted(range(n), key=lambda i: (-togo[i], i)), None
+    for turn in range(TUNE["turns"]):
+        now = place(seq, False)
+        if best is None or now[0] < best[0]:
+            best = now
+        back = place(sorted(range(n), key=lambda i: (-now[2][i], -i)), True)
+        seq = sorted(range(n), key=lambda i: (-back[2][i], i))
+    PLAN["time"] = best[0]
+    return deps, best[3], sorted(range(n), key=lambda i: (best[1][i], i))
+
+
+def emit(g, T, ops, sent):
+    eng = {"v": g.vector, "a": g.scalar, "t": g.tensor, "g": g, "s": g.sync}
+    if "order" not in PLAN:
+        PLAN["order"] = order(ops)
+    deps, queue, seq = PLAN["order"]
+    at = {i: k for k, i in enumerate(seq)}
 
     known = {q: 0 for q in eng}
-    at_issue, tag, last, turn, count = [], {}, {}, {q: 0 for q in eng}, {}
-    ndma = [0]
-    open_dma = []
+    at_issue, waits, needed = {}, {}, set()
+    for i in seq:
+        q, ws = queue[i], []
+        for j in sorted(deps[i], key=lambda j: -at[j]):
+            if ops[j][3] != "r" and not known[q] >> j & 1:
+                ws.append(j)
+                known[q] |= at_issue[j] | 1 << j
+        waits[i] = ws
+        needed.update(ws)
+        at_issue[i] = known[q]
+
+    known = {q: 0 for q in eng}
+    at_issue, tag, last, turn, count = {}, {}, {}, {q: 0 for q in eng}, {}
+    ndma, open_dma, come = [0], [], []
 
     def wait(q, j):
         if not known[q] >> j & 1:
             eng[q].wait_ge(T.sem[tag[j][0]], tag[j][1])
             known[q] |= at_issue[j] | 1 << j
 
-    for i, (q, fn, rd, wr, kind, pre) in enumerate(ops):
-        if pre is not None:
+    for i in seq:
+        alt, rd, wr, kind, pre = ops[i]
+        q = queue[i]
+        if pre is not None and rd[2] not in come:
+            come.append(rd[2])
             eng[q].wait_ge(pre[0], pre[1])
         for j in waits[i]:
             wait(q, j)
@@ -617,12 +554,12 @@ def emit(g, T, ops, sent):
             last[name] = i
             count[name] = count.get(name, 0) + 1
             tag[i] = (name, count[name])
-        at_issue.append(known[q])
-        ins = fn(eng[q])
+        at_issue[i] = known[q]
+        ins = alt[q][0](eng[q])
         if name is not None:
             ins.then_inc(T.sem[name], 16 if kind == "d" else 1)
     for j in open_dma:
-        wait(ops[j][0], j)
+        wait(queue[j], j)
     g.wait_ge(T.sem.sent, sent)
 
 
@@ -630,5 +567,5 @@ def rank_program(g, core, T, topo):
     rank = T.rank_of(core)
     if rank is None:
         return
-    ops, sent = build(T, topo, core, rank)
+    ops, sent = build(T, topo, rank)
     emit(g, T, ops, sent)

@@ -9,35 +9,36 @@ BELOW = 1.0 - 2.0 ** -24
 BIG = 65536.0
 SMALL = 2.0 ** -26
 PAD = 16
-TUNE = {"r0": 3, "r0b": 4, "r": 4, "ss": 3, "wake": 200, "dma": 2200, "far": 3000, "send": 350, "least": 64, "extra": 0,
-        "gather": 1.56, "scatter": 3.8, "abh": 2, "mh": 1, "spare": 60, "turns": 6}
+TUNE = {"r0": "AAAVVVVV", "r0b": "AAAAVVVV", "r": ("Aaav", "AVVV"), "ss": "AAAAVVVV", "kq": "avav",
+        "wake": 250, "dma": 2200, "far": 3600, "send": 350, "least": 64, "gather": 1.56, "scatter": 3.8,
+        "mh": 2, "mh0": 2, "pk": (1, 1), "spare": 60, "lead": 900, "mlead": 200, "turns": 12, "shake": 100, "seed": 0}
 
 SCRATCH = {"ps": ("psum", [128, 4096], F32)}
-for _d, _l in ((BF, "fa528 fb528 fk528 ab1040 ar1040 mvd1024 mvb1024 mvn1024 mve1024 xp1024 ap1024 fm512 xf1024 vt512 "
+for _d, _l in ((BF, "fa528 fb528 fk528 ab1040 ar1040 mvd1024 mvn1024 mve1024 xp1024 ap1024 fm1024 xf1024 vt512 "
                     "cma2048 cmb2048 csa1024 csb1024 oo512 on256 ox512 ids256 so128 fi256 fs256 ub128 uc128 cc256 bx256 "
-                    "by256 bz128 kc1792 jb1024"),
-               (F32, "wd256 wb256 wn256 we256 vd256 vb256 vn256 ve256 ua256 us128 dd512 mk256 wr256 ee256 dw256 ra16 "
-                     "of256 da256 dq128 th96 yo256 pf24 ka160 im64 rs128 ff128 kb32"),
-               (U16, "rku16 rks8 ofy16 ofm32 ofz32 ofs8 pl96 lu40"), (I32, "pi12"),
+                    "bz256 kc1280 jb1024"),
+               (F32, "wd256 wn256 we256 vd256 vb256 vn256 ve256 ua256 us128 de256 um256 dd512 mk256 wr256 ee256 dw256 ra16 "
+                     "of256 da256 dq128 th96 yo256 pf24 ka160 im64 rs128 ff192 kb16"),
+               (U16, "rku16 rks8 ofy16 ofm32 ofz32 ofs8 pl96 lu48"), (I32, "pi12"),
                (CD, "wq512 vq128 xq256"), (U8, "wp512 vp128 xs256")):
     for _w in _l.split():
         _n = _w.rstrip("0123456789")
         SCRATCH[_n] = ("sbuf", [128, int(_w[len(_n):])], _d)
 for _s in STAGES:
-    SCRATCH["q_" + _s] = ("sbuf", [128, 544], CD)
-    SCRATCH["s_" + _s] = ("sbuf", [128, 544], U8)
+    SCRATCH["q_" + _s] = ("sbuf", [128, 576], CD)
+    SCRATCH["s_" + _s] = ("sbuf", [128, 576], U8)
     SCRATCH["tq_" + _s] = ("sbuf", [128, 512], CD)
     SCRATCH["ts_" + _s] = ("sbuf", [128, 512], U8)
 for _t in range(3):
-    SCRATCH["mq%d" % _t] = ("sbuf", [128, 128], CD)
-    SCRATCH["ms%d" % _t] = ("sbuf", [128, 128], U8)
-    SCRATCH["lq%d" % _t] = ("sbuf", [128, 128], CD)
-    SCRATCH["ls%d" % _t] = ("sbuf", [128, 128], U8)
+    SCRATCH["mq%d" % _t] = ("sbuf", [128, 256], CD)
+    SCRATCH["ms%d" % _t] = ("sbuf", [128, 256], U8)
+    SCRATCH["lq%d" % _t] = ("sbuf", [128, 256], CD)
+    SCRATCH["ls%d" % _t] = ("sbuf", [128, 256], U8)
 
 POOL = {"v": 48, "a": 36, "t": 12, "g": 16}
 NDMA = 24
 SEMAPHORES = ([k + "%d" % i for k in POOL for i in range(POOL[k])] + ["dma%d" % i for i in range(NDMA)]
-              + ["arr0", "arr1", "arr2", "sent"])
+              + ["arr%d" % i for i in range(6)] + ["sent"])
 PLAN = {}
 
 
@@ -63,7 +64,7 @@ def lanes(T, topo, rank):
 
 def build(T, topo, rank):
     ops = []
-    sent = [0]
+    sent, lead, room = [0], [0], [0]
     A, AF = AluOpType, ActivationFunctionType
 
     def ap(v, cast=None):
@@ -80,7 +81,12 @@ def build(T, topo, rank):
     def add(alt, rd, wr, kind="c", pre=None):
         rd = [x for x in rd if isinstance(x, tuple)]
         wr = [x for x in wr if isinstance(x, tuple)]
-        ops.append((alt, rd + [x[5] for x in rd + wr if x[5] is not None], wr, kind, pre))
+        ops.append((alt, rd + [x[5] for x in rd + wr if x[5] is not None], wr, kind, pre, lead[0]))
+
+    def halves():
+        for h in range(2):
+            lead[0] = TUNE["lead"] * (1 - h)
+            yield h
 
     def time(q, o, ins, rate=1.0):
         if o[5] is not None:
@@ -89,7 +95,7 @@ def build(T, topo, rank):
             return (60 if q == "v" else 78) + TUNE["gather"] * size(o)
         if q == "v" and rate == 1.0 and all(SCRATCH[x[0]][2] in (BF, U16) for x in [o] + ins):
             rate = 0.5
-        return max(TUNE["least"], rate * size(o)) + TUNE["extra"]
+        return max(TUNE["least"], rate * size(o))
 
     def tt(o, x, y, op):
         add({"v": (lambda e: e.tensor_tensor(ap(o), ap(x), ap(y), op), time("v", o, [x, y], 1.01 if x[0] == "ps" else 2.0))},
@@ -103,8 +109,8 @@ def build(T, topo, rank):
         add({"v": (f, time("v", o, [x]))}, [x, s1, s2], [o])
 
     def scan(o, d0, d1, op0=A.mult, op1=A.add, first=0.0):
-        add({"v": (lambda e: e.tensor_tensor_scan(ap(o), ap(d0), ap(d1), first, op0, op1), time("v", o, [d0, d1]))},
-            [d0, d1], [o])
+        add({"v": (lambda e: e.tensor_tensor_scan(ap(o), ap(d0), ap(d1), ap(first), op0, op1), time("v", o, [d0, d1]))},
+            [d0, d1, first], [o])
 
     def tr(o, i):
         add({"v": (lambda e: e.transpose(ap(o), ap(i)), time("v", o, [i]))}, [i], [o])
@@ -172,21 +178,27 @@ def build(T, topo, rank):
 
     QF, RF, CF, ODD, PL, T4, Q7, Q8, B2, EVN, SC, SC4, T44, Q1, Q2, Q21, Q22, P2, P21, P22, X1, X2 = [
         col("pf", j) for j in range(22)]
-    PAR = [EVN, ODD]
-    EXL, CXL, N4L, NL, DXL = V("lu", 0, 4), V("lu", 4, 8), V("lu", 8, 9), V("lu", 10, 18), V("lu", 18, 26)
-    RS4 = V("kb", 0, 16)
-    C16, MK16, RS16, WX, C8, WM, WN = [V("kc", 128 * j, 128 * j + 128) for j in range(7)]
-    C32, WP, TMP = V("kc", 896, 1152), V("kc", 1152, 1408), V("kc", 1408, 1664)
+    PAR, PARS = [EVN, ODD], [col("pf", 22), col("pf", 23)]
+    EXL, CXL, N4L = V("lu", 0, 4), V("lu", 4, 8), V("lu", 8, 9)
+    NEAR = {8: (V("lu", 10, 18), V("lu", 18, 26), V("ff", 0, 128)), 4: (V("lu", 26, 30), V("lu", 30, 34), V("ff", 128, 192))}
+    RS4 = V("kb")
+    C16, MK16, RS16, WX, WM, WN = [V("kc", 128 * j, 128 * j + 128) for j in range(6)]
+    WP, TMP = V("kc", 768, 1024), 1024
     MK16H, RS16H = V("kc", 128, 192), V("kc", 256, 320)
-    JALL, JKS, JHALF, ONES, MS = V("jb", 0, 256), V("jb", 896, 1024), V("jb", 256, 512), V("jb", 512, 768), V("fs")
+    JALL, JHALF, ONES, MS, JKS = V("jb", 0, 256), V("jb", 256, 512), V("jb", 512, 768), V("jb", 768, 896), V("jb", 896, 1024)
 
-    def mark(o, c, spots):
-        tmp = V(TMP[0], TMP[1], TMP[1] + size(o))
+    def mark(o, spots, n):
+        head = V(o[0], o[1], o[1] + n)
         for i, (s, v) in enumerate(spots):
-            ts(tmp if i else o, c, s, A.is_equal, v - 1.0, A.mult)
+            tmp = V("kc", TMP + 32 * room[0], TMP + 32 * room[0] + n)
+            room[0] += 1 if i else 0
+            ts(tmp if i else head, V("jb", 0, n), s, A.is_equal, v - 1.0, A.mult)
             if i:
-                tt(o, o, tmp, A.add)
-        ts(o, o, 1.0, A.add)
+                tt(head, head, tmp, A.add)
+        lin(head, head, 1.0, 1.0)
+        while n < size(o):
+            mov(V(o[0], o[1] + n, o[1] + 2 * n), V(o[0], o[1], o[1] + n), "a")
+            n *= 2
 
     dma("s", V("fa", PAD), T.x[:, 0:512])
     dma("a", V("fb", PAD), T.x[:, 512:1024])
@@ -196,6 +208,10 @@ def build(T, topo, rank):
     iota(col("pi", 0), [[0, 1]], 0, 1)
     for f in ("fa", "fb", "fk", "ab", "ar"):
         ms(V(f, 0, PAD), 0.0)
+    ms(V("fm", 0, 512), 0.0)
+    mov(V("fk", PAD), V("fm", 0, 512), "a")
+    for t in range(3):
+        quant(V("lq%d" % t, 0, 128), V("ls%d" % t, 0, 128), V("fm", 0, 512))
     p = col("pi", 0)
     ts(col("pi", 1), p, 15, A.bitwise_and)
     ts(col("pi", 2), p, 31, A.bitwise_and)
@@ -208,13 +224,15 @@ def build(T, topo, rank):
     ts(col("pi", 9), p, 2, A.arith_shift_right, 1, A.bitwise_and)
     mov(V("pf", 0, 9), V("pi", 1, 10), "v")
     lin(EVN, ODD, -1.0, 1.0)
+    lin(PARS[0], EVN, 0.03125)
+    lin(PARS[1], ODD, 0.03125)
     iota(V("ka", 0, 32), [[32, 4], [0, 4], [16, 2]], 0)
     iota(V("ka", 32, 64), [[0, 4], [1, 4], [0, 2]], 0)
     ts(V("ka", 0, 32), V("ka", 0, 32), QF, A.add)
     ts(V("ka", 32, 64), V("ka", 32, 64), CF, A.is_equal)
     for i, (s, b) in enumerate(((1.0, 2.0), (2.0, 2.0), (2.0, 3.0))):
         z = V("ka", 64 + 32 * i, 96 + 32 * i)
-        lin(z, V("ka", 0, 32), s, b, "v")
+        lin(z, V("ka", 0, 32), s, b)
         tt(z, z, V("ka", 32, 64), A.mult)
         mov(V("pl", 32 * i, 32 * i + 32), z, "v")
     iota(V("im"), [[1, 32], [0, 2]], 0)
@@ -228,17 +246,21 @@ def build(T, topo, rank):
     iota(V("th", 8, 10), [[0, 2]], 31)
     iota(V("th", 10, 18), [[2, 8]], 0)
     iota(V("th", 18, 26), [[0, 8]], 15)
-    lin(X1, B2, 64.0, None, "v")
-    lin(X2, Q8, 32.0, X1, "v")
+    iota(V("th", 26, 30), [[4, 4]], 0)
+    iota(V("th", 30, 34), [[0, 4]], 15)
+    lin(X1, B2, 64.0)
+    lin(X2, Q8, 32.0, X1)
     ts(V("th", 8, 10), V("th", 8, 10), X2, A.add)
-    lin(X1, Q7, 16.0, None, "v")
+    lin(X1, Q7, 16.0)
     ts(V("th", 10, 18), V("th", 10, 18), X1, A.add, Q8, A.add)
     ts(V("th", 18, 26), V("th", 18, 26), X1, A.add)
-    mov(V("lu", 0, 26), V("th", 0, 26), "v")
+    lin(X2, T4, 16.0)
+    ts(V("th", 26, 30), V("th", 26, 30), X2, A.add, PL, A.add)
+    ts(V("th", 30, 34), V("th", 30, 34), X2, A.add)
+    mov(V("lu", 0, 34), V("th", 0, 34), "v")
     iota(C16, [[0, 8], [1, 16]], 0)
-    iota(C8, [[0, 16], [1, 8]], 0)
-    iota(C32, [[0, 8], [1, 32]], 0)
-    iota(V("ff"), [[1, 16], [0, 8]], 0)
+    iota(V("ff", 0, 128), [[1, 16], [0, 8]], 0)
+    iota(V("ff", 128, 192), [[1, 16], [0, 4]], 0)
     iota(RS4, [[0, 4], [1, 4]], 0)
     iota(JALL, [[1, 256]], 0)
     iota(JHALF, [[1, 128], [0, 2]], 0)
@@ -246,50 +268,61 @@ def build(T, topo, rank):
     iota(ONES, [[0, 256]], 1)
     iota(V("cc", 0, 256, 2), [[0, 128]], 0)
     iota(V("fi", 1, 256, 2), [[2, 128]], 0)
-    iota(V("jb", 768, 896), [[0, 64], [-1, 2]], 0)
-    MS = V("jb", 768, 896)
+    iota(MS, [[0, 64], [-1, 2]], 0)
     lin(JKS, V("jb", 128, 256), SMALL)
     ts(MK16, C16, QF, A.is_equal)
     ts(RS16, C16, 1.0, A.min)
     ts(RS4, RS4, 1.0, A.min)
     ts(V("ff"), V("ff"), QF, A.is_lt)
-    lin(V("ff"), V("ff"), BELOW - 1.0, 1.0, "v")
+    lin(V("ff"), V("ff"), BELOW - 1.0, 1.0)
     ts(SC, QF, 15.0, A.is_lt, 1.0 / BIG - 1.0, A.mult)
-    ts(SC, SC, 1.0, A.add)
+    lin(SC, SC, 1.0, 1.0)
     ts(SC4, PL, 3.0, A.is_lt, 4.0 / BIG - 4.0, A.mult)
-    ts(SC4, SC4, 4.0, A.add)
+    lin(SC4, SC4, 1.0, 4.0)
     for o, i, s, b in ((T44, T4, 1.0, 4.0), (Q1, QF, 1.0, 1.0), (Q2, QF, 2.0, 0.0), (Q21, QF, 2.0, 1.0), (Q22, QF, 2.0, 2.0),
                        (P2, PL, 2.0, 0.0), (P21, PL, 2.0, 1.0), (P22, PL, 2.0, 2.0)):
-        lin(o, i, s, b, "v")
-    mark(WX, C16, [(QF, 0.0), (Q1, BIG + 1.0)])
-    mark(WP, C32, [(Q2, 0.0), (Q21, 1.0 / SMALL + 1.0), (Q22, BIG + 1.0)])
-    mark(WM, C8, [(P2, 0.0), (P22, BIG + 1.0)])
-    mark(WN, C8, [(P2, 0.0), (P21, -1.0), (P22, BIG + 1.0)])
+        lin(o, i, s, b)
+    mark(WX, [(QF, 0.0), (Q1, BIG + 1.0)], 16)
+    mark(WP, [(Q2, 0.0), (Q21, 1.0 / SMALL + 1.0), (Q22, BIG + 1.0)], 32)
+    mark(WM, [(P2, 0.0), (P22, BIG + 1.0)], 8)
+    mark(WN, [(P2, 0.0), (P21, -1.0), (P22, BIG + 1.0)], 8)
     for t in range(4):
         mov(plane("xp", t, 0, 128), V("fa", PAD + t, None, 4), "g")
         mov(plane("xp", t, 128, 256), V("fb", PAD + t, None, 4), "g")
 
-    def gram(st, f, wide, mv, w, v, b0, lst):
+    def gram(st, f, kind, mv, w, v, b0, lst, only=(0, 1)):
         q, s = "q_" + st, "s_" + st
-        quant(V(q, 0, 130), V(s, 0, 130), V(f, 8, 528))
-        if wide:
-            quant(V(q, 130, 258), V(s, 130, 258), V(f, 528, 1040))
-        n = TUNE["mh"]
-        for h in range(n):
-            for t in range(4):
-                for par in range(2):
-                    z = 1024 // n
-                    src = (V(f, PAD + z * h + 4 + t, PAD + z * h + z, 8) if wide
-                           else V(f, PAD + z // 2 * h + t, PAD + z // 2 * (h + 1), 4))
-                    lin(V(mv, z * h + 4 * par + t, z * h + z, 8), src, PAR[par])
-        for h in range(2):
-            m = 288 + 128 * h
+        wide = kind == "wide"
+        n = TUNE["mh"] if wide else TUNE["mh0"]
+        for h in halves():
+            if h not in only:
+                continue
+            base, top = 0, 130
+            if wide and h:
+                quant(V(q, 130, 258), V(s, 130, 258), V(f, 528, 1040))
+                top = 258
+            elif kind == "late" and h:
+                base, top = 160, 290
+                quant(V(q, base, top), V(s, base, top), V(f, 8, 528))
+            elif h == 0:
+                quant(V(q, 0, 130), V(s, 0, 130), V(f, 8, 528))
+            if h < n and kind != "late":
+                lead[0] += TUNE["mlead"]
+                for t in range(4):
+                    for par in range(2):
+                        z = 1024 // n
+                        src = (V(f, PAD + z * h + 4 + t, PAD + z * h + z, 8) if wide
+                               else V(f, PAD + z // 2 * h + t, PAD + z // 2 * (h + 1), 4))
+                        lin(V(mv, z * h + 4 * par + t, z * h + z, 8), src, PAR[par])
+                lead[0] -= TUNE["mlead"]
+            m = 320 + 128 * h
             quant(V(q, m, m + 128), V(s, m, m + 128), half(mv, h, 0, 512))
-            top = 258 if wide and h else 130
-            off = V("pl", 32 * lst + 16 * h, 32 * lst + 16 * h + 16)
-            o, i = half("tq_" + st, h, 0, 256), IND(V(q, 0, top), off)
-            add({"v": (lambda e, o=o, i=i: e.tensor_copy(ap(o, dt.uint32), ap(i, dt.uint32)), time("v", o, [i]))}, [i], [o])
-            mov(half("ts_" + st, h, 0, 256), IND(V(s, 0, top), off), "a")
+            for z in range(TUNE["pk"][h]):
+                cw = 16 // TUNE["pk"][h]
+                off = half("pl", z, 32 * lst + 16 * h, cw)
+                o, i = half("tq_" + st, z, 256 * h, 16 * cw), IND(V(q, base, top), off)
+                add({"v": (lambda e, o=o, i=i: e.tensor_copy(ap(o, dt.uint32), ap(i, dt.uint32)), time("v", o, [i]))}, [i], [o])
+                mov(half("ts_" + st, z, 256 * h, 16 * cw), IND(V(s, base, top), off), "a")
             for k in (2 * h, 2 * h + 1):
                 mm(bank(b0 + k), half("tq_" + st, k, 0, 128), half("ts_" + st, k, 0, 128), V(q, m, m + 128), V(s, m, m + 128))
                 tt(half(w, k), bank(b0 + k, 64 * (k % 2), 64), V("im"), A.mult)
@@ -303,66 +336,111 @@ def build(T, topo, rank):
     def wide(v, h):
         return IND(half(v, h, 0, 128), EXL)
 
-    def places(a, low, slot, w, na, cm, cs, out, times):
-        lin(V("dd", low, low + 128), V("dd", a, a + 128), BELOW)
-        for h in range(2):
-            tt(half("mk", h, slot), half("dd", h, a), MK16H, A.mult)
-            scan(half("wr", h, slot), RS16H, half("mk", h, slot))
-        tt(V("ee", slot, slot + 128), IND(V("dd", a, a + 128), NL), V("ff"), A.mult)
-        tt(V(cm, 8 * w, 8 * w + 128), IND(V("wr", slot, slot + 128), DXL), V("ee", slot, slot + 128), A.is_gt)
-        n = (w + 16) // 2
-        for m in range(8):
-            win, me = V("dd", a + 16 * m + 16, a + 16 * m + 16 + w), col("wr", slot + 16 * m + 15)
-            if m < na:
-                act(V(cm, m, 8 * w, 8), win, AF.Sign, me, -1.0)
-                z = V(cm, m, 16 * n, 8)
-                act(z, z, AF.Relu, acc=col("ra", slot // 16 + m))
-            else:
-                ts(V(cm, m, 8 * w, 8), win, me, A.is_lt)
-                scan(V(cs, n * m, n * m + n), V(cm, m, 8 * n, 8), V(cm, 8 * n + m, 16 * n, 8), A.add, A.add)
+    def sizes(v, h, a, low, fast, also=None):
+        mov(half("ua", h, a), wide(v, h))
+        tr(half("dd", h, a), half("ua", h, a))
+        lin(half("dd", h, low), half("dd", h, a), BELOW)
+        if also:
+            tr(half("de", h, also[0]), half("ua", h, a))
+            lin(half("de", h, also[1]), half("de", h, also[0]), BELOW)
+        if fast:
+            tt(half("um", h, a), wide(v, h), MK16H, A.mult)
+            tr(half("mk", h, a), half("um", h, a))
+        else:
+            tt(half("mk", h, a), half("dd", h, a), MK16H, A.mult)
+        scan(half("wr", h, a), RS16H, half("mk", h, a))
+
+    def places(a, slot, who, cm, cs, wins, out, times):
+        n, na = len(who), who.count("A")
+        nl, dx, ff = NEAR[n]
+        (cm, c0), (cs, s0) = cm, cs
+        w = [size(z) for z in wins(0)] + [0]
+        tt(V("ee", slot, slot + 16 * n), IND(V("dd", a, a + 16 * n), nl), ff, A.mult)
+        tt(V(cm, c0 + n * w[0], c0 + n * w[0] + 16 * n), IND(V("wr", slot, slot + 16 * n), dx), V("ee", slot, slot + 16 * n),
+           A.is_gt)
+
+        def part(m, x, y):
+            return V(cm, c0 + n * x + m, c0 + n * y, n)
+
+        def total(m, x, y, end, first=0.0):
+            u = (y - x) // 2
+            scan(V(cs, end - u, end), part(m, x, x + u), part(m, x + u, y), A.add, A.add, first)
+        for m, e in enumerate(who):
+            me, acc, mid = col("wr", slot + 16 * m + 15), col("ra", slot // 16 + m), w[0] + 16
+            for i, win in enumerate(wins(m)):
+                o = part(m, mid * i, mid * i + w[i])
+                if e == "A" or e == "a" and not i:
+                    act(o, win, AF.Sign, me, -1.0)
+                else:
+                    ts(o, win, me, A.is_lt)
+            end = s0 + 128 * m + 128
+            if e in "Aa":
+                z = part(m, 0, mid + w[1] * (e == "A"))
+                act(z, z, AF.Relu, acc=acc)
+            if e == "v":
+                total(m, 0, mid, end - w[1] // 2)
+                acc = col(cs, end - w[1] // 2 - 1)
+            if e == "V":
+                total(m, 0, mid + w[1], end)
+            if e in "av":
+                total(m, mid, mid + w[1], end, acc)
         b = out[1]
         if na:
             ts(V(out[0], b, b + na), V("ra", slot // 16, slot // 16 + na), times, A.mult)
-        ts(V(out[0], b + na, b + 8), V(cs, n * na + n - 1, 8 * n, n), times, A.mult)
+        if na < n:
+            ts(V(out[0], b + na, b + n), V(cs, s0 + 128 * na + 127, s0 + 128 * n, 128), times, A.mult)
+
+    def ring(name, a, w):
+        return lambda m: [V(name, a + 16 * m + 16, a + 16 * m + 16 + w)]
 
     eng = lanes(T, topo, rank)
     mask = sum(1 << k for k in eng)
 
+    def layer(t_, h, f, a):
+        come = 2 * len(lanes(T, topo, (rank - STEP[t_]) % len(T.cores)))
+        lq, ls = V("lq%d" % t_, 64 + 64 * h, 192 + 64 * h), V("ls%d" % t_, 64 + 64 * h, 192 + 64 * h)
+        lead[0] = TUNE["lead"] * (1 - h)
+        for b in range(4):
+            mm(bank(4 + b), half("wq", b, 0, 128), half("wp", b, 0, 128), lq, ls, (T.sem["arr%d" % (2 * t_ + h)], come))
+            lin(V(f, a + 256 * h + b, a + 256 * h + 256, 4), bank(4 + b, 64, 64), 0.03125, None, TUNE["kq"][b])
+            for par in range(2 if t_ < 2 else 0):
+                lin(V("mvd", 512 * h + 4 * par + b, 512 * h + 512, 8), bank(4 + b, 64, 64), PARS[par], None, TUNE["kq"][b])
+
     for t_ in range(3):
         if t_ == 0:
-            gram("d0", "fa", False, "mvd", "wd", "vd", 0, 0)
-            gram("d0b", "fb", False, "mvb", "wb", "vb", 4, 0)
-            for h in range(2):
-                for a, v in ((0, "vd"), (128, "vb")):
-                    mov(half("ua", h, a), wide(v, h))
-                    tr(half("dd", h, a), half("ua", h, a))
-            places(0, 256, 0, 240, TUNE["r0"], "cma", "csa", V("rku", 0, 8), 1.0)
-            places(128, 384, 128, 240, TUNE["r0b"], "cmb", "csb", V("rku", 8, 16), 1.0)
+            gram("d0", "fa", "", "mvd", "wd", "vd", 0, 0)
+            gram("d0b", "fb", "", "mvn", "wn", "vb", 4, 0)
+            for h in halves():
+                sizes("vd", h, 0, 256, False, (0, 128))
+            for h in halves():
+                sizes("vb", h, 128, 384, True)
+            places(0, 0, TUNE["r0"], ("cma", 0), ("csa", 0), lambda m: ring("de", 0, 112)(m) + [V("dd", 128, 256)],
+                   V("rku", 0, 8), 1.0)
+            places(128, 128, TUNE["r0b"], ("cmb", 0), ("csb", 0), ring("dd", 128, 240), V("rku", 8, 16), 1.0)
             mov(IND(V("on"), V("rku")), JALL, "v")
-            for h in range(2):
+            for h in halves():
                 scan(half("ox", h, 0, 128), WX, half("on", h, 0, 128), A.mult, A.max)
                 ts(half("ofy", h, 0, 8), V("ox", 128 * h + 15, 128 * h + 128, 16), SC, A.mult)
         else:
-            for t in range(4):
-                lin(V("fk", PAD + t, None, 4), bank(4 + t), 0.03125)
-                mov(plane("xp", t, 128, 256), V("fk", PAD + t, None, 4), "g")
-            gram("d%d" % t_, "fk", False, "mvd", "wd", "vd", 0, 0)
             for h in range(2):
-                mov(half("ua", h), wide("vd", h))
-                tr(half("dd", h, 128), half("ua", h))
-            places(128, 384, 128, 240, TUNE["r"], "cmb", "csb", V("rku", 8, 16), 2.0)
+                layer(t_ - 1, h, "fk", PAD)
+                for t in range(4 * h):
+                    mov(plane("xp", t, 128, 256), V("fk", PAD + t, None, 4), "g")
+                gram("d%d" % t_, "fk", "late", "mvd", "wd", "vd", 0, 0, (h,))
+                lead[0] = TUNE["lead"] * (1 - h)
+                sizes("vd", h, 128, 384, h, None if h else (0, 192))
+            places(128, 128, TUNE["r"][0], ("cmb", 0), ("csb", 0), lambda m: ring("de", 0, 176)(m) + [V("dd", 192, 256)],
+                   V("rku", 8, 12), 2.0)
+            places(192, 192, TUNE["r"][1], ("cmb", 1024), ("csb", 512), ring("dd", 192, 240), V("rku", 12, 16), 2.0)
             mov(IND(V("oo"), V("rku", 8, 16)), JKS, "v")
             scan(V("oo", 1, 512, 2), ONES, V("oo", 0, 512, 2), A.mult, A.subtract, -1.0)
-            for h in range(2):
+            for h in halves():
                 scan(half("ox", h, 0, 256), WP, half("oo", h, 0, 256), A.mult, A.max)
                 ts(half("ofy", h, 0, 8), V("ox", 256 * h + 31, 256 * h + 256, 32), SC, A.mult)
 
-        n = TUNE["abh"]
-        for h in range(n):
+        for h in halves():
             for t in range(4):
-                z = 1024 // n
-                mov(V("ab", PAD + z * h + t, PAD + z * h + z, 4), IND(plane("xp", t), half("ofy", h, 0, 16 // n)))
-        for h in range(2):
+                mov(V("ab", PAD + 512 * h + t, PAD + 512 * h + 512, 4), IND(plane("xp", t), half("ofy", h, 0, 8)))
             mov(half("da", h, 0, 128), IND(V("dd", 0, 256), half("ofy", h, 0, 8)))
             tr(half("dq", h), V("da", 128 * h, 128 * h + 128, 2))
         if t_ == 2:
@@ -371,8 +449,8 @@ def build(T, topo, rank):
         for i, c in ((0, 0.75), (2, 0.25)):
             lin(V("th", i, 32, 4), V("dq", 0, 128, 16), c)
             lin(V("th", i + 1, 32, 4), V("th", i, 32, 4), -BELOW)
-        gram("n%d" % t_, "ab", True, "mvn", "wn", "vn", 0, 1)
-        for h in range(2):
+        gram("n%d" % t_, "ab", "wide", "mvn", "wn", "vn", 0, 1)
+        for h in halves():
             tt(half("th", h, 32, 16), IND(half("vn", h, 0, 128), N4L), half("th", h, 0, 16), A.is_ge)
             scan(half("th", h, 64, 16), RS4, half("th", h, 32, 16))
             lin(half("uc", h), IND(half("th", h, 64, 16), CXL), -0.5, 1.0)
@@ -380,38 +458,41 @@ def build(T, topo, rank):
             for t in range(4):
                 a = PAD + 512 * h + t
                 scan(V("ar", a, PAD + 512 * h + 512, 4), half("cc", h, 0, 128), V("ab", a, PAD + 512 * h + 512, 4))
-        gram("e%d" % t_, "ar", True, "mve", "we", "ve", 0, 2)
-        for h in range(2):
+        to = topo.addr(T.cores[(rank + STEP[t_]) % len(T.cores)])
+        gram("e%d" % t_, "ar", "wide", "mve", "we", "ve", 0, 2)
+        for h in halves():
             tt(half("ub", h), wide("ve", h), half("dq", h), A.is_ge)
             tr(V("fi", 128 * h, 128 * h + 128, 2), half("ub", h))
             scan(half("bx", h, 0, 128), WM, half("fi", h, 0, 128))
             ts(half("ofm", h, 0, 16), V("bx", 128 * h + 7, 128 * h + 128, 8), SC4, A.mult, T4, A.add)
             for z in (2 * h, 2 * h + 1):
-                mov(half("fm", z, 0, 128), IND(V("ar", PAD), half("ofm", z, 0, 8)))
-        mq, msn, lq, ls = V("mq%d" % t_), V("ms%d" % t_), V("lq%d" % t_), V("ls%d" % t_)
-        quant(mq, msn, V("fm"))
-        rid, pid, _e = topo.addr(T.cores[(rank + STEP[t_]) % len(T.cores)])
-        arr = T.sem["arr%d" % t_]
-        add({"g": (lambda e, mq=mq, lq=lq, arr=arr, rid=rid, pid=pid:
-                   e.remote_dma(ap(lq, dt.uint8), ap(mq, dt.uint8), arr, T.sem.sent, pid, rid, mask), TUNE["send"])},
-            [mq], [lq], "r")
-        add({"g": (lambda e, msn=msn, ls=ls, arr=arr, rid=rid, pid=pid:
-                   e.remote_dma(ap(ls), ap(msn), arr, T.sem.sent, pid, rid, mask), TUNE["send"])}, [msn], [ls], "r")
-        sent[0] += 2 * len(eng)
+                mov(half("fm", z, 512, 128), IND(V("ar", PAD), half("ofm", z, 0, 8)))
+            m = 128 * h
+            quant(V("mq%d" % t_, m, m + 128), V("ms%d" % t_, m, m + 128), V("fm", 256 + 2 * m, 768 + 2 * m))
+            for src, dst, cast in (("mq", "lq", dt.uint8), ("ms", "ls", None)):
+                o, i = V(dst + "%d" % t_, 128 + 64 * h, 192 + 64 * h), V(src + "%d" % t_, m + 64, m + 128)
+                add({"g": (lambda e, o=o, i=i, cast=cast, arr=T.sem["arr%d" % (2 * t_ + h)], to=to:
+                           e.remote_dma(ap(o, cast), ap(i, cast), arr, T.sem.sent, to[1], to[0], mask), TUNE["send"])},
+                    [i], [o], "r")
+                sent[0] += len(eng)
 
         if t_ < 2:
             iota(V("oo", 0, 512, 2), [[0, 256]], -1)
-            for h in range(2):
+            for h in halves():
                 tt(half("us", h), wide("ve", h), half("dq", h), A.min)
                 tr(half("dd", h, 128), half("us", h))
                 scan(half("fs", h, 0, 128), MS, half("fi", h, 0, 128))
-            places(128, 256, 0, 112, TUNE["ss"], "cma", "csa", V("rks", 0, 8), 1.0)
-            mov(V("dw", 0, 256, 2), V("dd", 128, 256), "g")
-            mov(V("dw", 1, 256, 2), V("dd", 128, 256), "g")
+                lin(half("dd", h, 256), half("dd", h, 128), BELOW)
+                tt(half("mk", h), half("dd", h, 128), MK16H, A.mult)
+                scan(half("wr", h), RS16H, half("mk", h))
+            lin(V("de", 64, 192), V("dd", 128, 256), BELOW)
+            places(128, 0, TUNE["ss"], ("cma", 0), ("csa", 0), ring("dd", 128, 112), V("rks", 0, 8), 1.0)
+            mov(V("dw", 0, 256, 2), V("dd", 128, 256), "ga")
+            mov(V("dw", 1, 256, 2), V("dd", 128, 256), "ga")
             for t in range(4):
-                mov(plane("ap", t), V("ar", PAD + t, None, 4), "g")
+                mov(plane("ap", t), V("ar", PAD + t, None, 4), "ga")
             mov(IND(V("so"), V("rks")), V("fs", 1, 256, 2), "v")
-            scan(V("bz"), WX, V("so"))
+            scan(V("bz", 0, 128), WX, V("so"))
             ts(V("ofs"), V("bz", 15, 128, 16), SC, A.mult, 1.0, A.add)
             for t in range(4):
                 mov(plane("xp", t, 0, 128), IND(plane("ap", t), V("ofs")))
@@ -419,9 +500,9 @@ def build(T, topo, rank):
             if t_ == 1:
                 mov(V("ids", 0, 128), IND(JHALF, V("ofs")))
         else:
-            for h in range(2):
-                scan(half("by", h, 0, 128), WN, half("fi", h, 0, 128))
-                ts(half("ofz", h, 0, 16), V("by", 128 * h + 7, 128 * h + 128, 8), SC4, A.mult, T44, A.add)
+            for h in halves():
+                scan(half("bz", h, 0, 128), WN, half("fi", h, 0, 128))
+                ts(half("ofz", h, 0, 16), V("bz", 128 * h + 7, 128 * h + 128, 8), SC4, A.mult, T44, A.add)
                 mov(half("xf", h, 0, 256), IND(V("ar", PAD), half("ofz", h, 0, 16)))
             quant(V("vq"), V("vp"), V("vt"))
             quant(V("xq", 0, 128), V("xs", 0, 128), V("xf", 0, 512))
@@ -429,12 +510,9 @@ def build(T, topo, rank):
             dma("s", T.oc[:, 0:512], V("xq", 0, 128), None, dt.uint8)
             mov(V("yo", 0, 128), bank(0))
             dma("s", T.y[:, 0:128], V("yo", 0, 128))
-        come = 2 * len(lanes(T, topo, (rank - STEP[t_]) % len(T.cores)))
-        for b in range(4):
-            mm(bank(4 + b), half("wq", b, 0, 128), half("wp", b, 0, 128), lq, ls, (arr, come))
 
-    for t in range(4):
-        lin(V("xf", 512 + t, 1024, 4), bank(4 + t), 0.03125)
+    for h in range(2):
+        layer(2, h, "xf", 512)
     quant(V("xq", 128, 256), V("xs", 128, 256), V("xf", 512, 1024))
     mm(bank(1), V("vq"), V("vp"), V("xq", 128, 256), V("xs", 128, 256))
     dma("a", T.oc[:, 512:1024], V("xq", 128, 256), None, dt.uint8)
@@ -455,21 +533,19 @@ def order(ops):
         return int.from_bytes(np.packbits(m).tobytes(), "big")
 
     seen, deps = {}, []
-    for i, (alt, rd, wr, kind, pre) in enumerate(ops):
-        acc = [(v[0], cols(v), v[0] == "ps") for v in rd] + [(v[0], cols(v), True) for v in wr]
-        deps.append({j for name, m, w in acc for j, mj, wj in seen.get(name, []) if (w or wj) and m & mj})
+    for i, (alt, rd, wr, kind, pre, lead) in enumerate(ops):
+        acc = [(v[0], cols(v), False) for v in rd] + [(v[0], cols(v), True) for v in wr]
+        deps.append({j for name, m, w in acc for j, mj, wj in seen.get(name, []) if m & mj and (
+            w or wj or name == "ps" and len(set(alt) | set(ops[j][0])) > 1)})
         for name, m, w in acc:
             seen.setdefault(name, []).append((i, m, w))
     late = {"c": TUNE["wake"], "d": TUNE["dma"], "r": TUNE["far"]}
     n = len(ops)
-    togo = [0.0] * n
+    togo, users = [0.0] * n, [set() for i in range(n)]
     for i in range(n - 1, -1, -1):
         togo[i] += min(c for f, c in ops[i][0].values()) + late[ops[i][3]]
         for j in deps[i]:
-            togo[j] = max(togo[j], togo[i])
-    users = [set() for i in range(n)]
-    for i in range(n):
-        for j in deps[i]:
+            togo[j] = max(togo[j], togo[i] + max(0, ops[j][5] - ops[i][5]))
             users[j].add(i)
 
     def place(seq, back):
@@ -492,13 +568,29 @@ def order(ops):
             start[i], end[i], queue[i] = best[1], best[4], best[2]
         return max(end[i] + (0 if back else late[ops[i][3]]) for i in seq), start, end, queue
 
-    seq, best = sorted(range(n), key=lambda i: (-togo[i], i)), None
+    def sort(key, first, then):
+        left = [len(z) for z in first]
+        ready, seq = sorted((key[i], i) for i in range(n) if not left[i]), []
+        while ready:
+            i = ready.pop(0)[1]
+            seq.append(i)
+            new = []
+            for j in then[i]:
+                left[j] -= 1
+                if not left[j]:
+                    new.append((key[j], j))
+            if new:
+                ready = sorted(ready + new)
+        return seq
+
+    rng = np.random.default_rng(TUNE["seed"])
+    best = place(sorted(range(n), key=lambda i: (-togo[i], i)), False)
     for turn in range(TUNE["turns"]):
-        now = place(seq, False)
-        if best is None or now[0] < best[0]:
+        shake = rng.random(n) * TUNE["shake"] * (turn > 0)
+        back = place(sort([-best[2][i] + shake[i] for i in range(n)], users, deps), True)
+        now = place(sorted(range(n), key=lambda i: (-back[2][i], i)), False)
+        if now[0] <= best[0]:
             best = now
-        back = place(sorted(range(n), key=lambda i: (-now[2][i], -i)), True)
-        seq = sorted(range(n), key=lambda i: (-back[2][i], i))
     PLAN["time"] = best[0]
     return deps, best[3], sorted(range(n), key=lambda i: (best[1][i], i))
 
@@ -532,7 +624,7 @@ def emit(g, T, ops, sent):
             known[q] |= at_issue[j] | 1 << j
 
     for i in seq:
-        alt, rd, wr, kind, pre = ops[i]
+        alt, rd, wr, kind, pre, lead = ops[i]
         q = queue[i]
         if pre is not None and rd[2] not in come:
             come.append(rd[2])

@@ -1,3 +1,4 @@
+import math
 import numpy as np
 from concourse.mybir import dt, AluOpType, ActivationFunctionType
 
@@ -7,20 +8,23 @@ STAGES = ["d0", "d0b", "n0", "e0", "d1", "n1", "e1", "d2", "n2", "e2"]
 TINY = 2.0 ** -100
 BELOW = 1.0 - 2.0 ** -24
 BIG = 65536.0
-SMALL = 2.0 ** -26
+SMALL = 2.0 ** -23
 PAD = 16
-TUNE = {"r0": "AAAVVVVV", "r0b": "AAAAVVVV", "r": ("Aaav", "AVVV"), "ss": "AAAAVVVV", "kq": "avav",
-        "wake": 250, "dma": 2200, "far": 3600, "send": 350, "least": 64, "gather": 1.56, "scatter": 3.8,
-        "mh": 2, "mh0": 2, "pk": (1, 1), "spare": 60, "lead": 900, "mlead": 200, "turns": 12, "shake": 100, "seed": 0}
+TUNE = {"r0": (3, 4), "r": (2, 2), "ss": 4, "kq": "avav",
+        "wake": 268, "dma": 3100, "far": 2400, "send": 360, "first": 120, "least": 64, "gather": 1.56, "scatter": 3.8,
+        "amin": 64, "afix": 0, "spare": 80, "leads": (360, 700, 700, 400), "lead": 900, "mlead": -150, "ahead": 500,
+        "early": 20000, "gx": 1.4, "turns": 2, "shake": 100, "seed": 3, "weights": (0.6, 1.3),
+        "passes": (0, 45, 20), "step": 90, "span": 140, "moves": 9000, "reach": 30, "heat": 8,
+        "cases": ((1.0, 2400), (1.25, 3000), (1.4, 4300))}
 
 SCRATCH = {"ps": ("psum", [128, 4096], F32)}
-for _d, _l in ((BF, "fa528 fb528 fk528 ab1040 ar1040 mvd1024 mvn1024 mve1024 xp1024 ap1024 fm1024 xf1024 vt512 "
+for _d, _l in ((BF, "fa528 fb528 fk2080 ab1040 ar1040 mvd1024 mvn1024 mve1024 xp1024 ap1024 fm1024 xf1024 vt512 "
                     "cma2048 cmb2048 csa1024 csb1024 oo512 on256 ox512 ids256 so128 fi256 fs256 ub128 uc128 cc256 bx256 "
-                    "bz256 kc1280 jb1024"),
+                    "bz256 kc1056 jb1024"),
                (F32, "wd256 wn256 we256 vd256 vb256 vn256 ve256 ua256 us128 de256 um256 dd512 mk256 wr256 ee256 dw256 ra16 "
-                     "of256 da256 dq128 th96 yo256 pf24 ka160 im64 rs128 ff192 kb16"),
-               (U16, "rku16 rks8 ofy16 ofm32 ofz32 ofs8 pl96 lu48"), (I32, "pi12"),
-               (CD, "wq512 vq128 xq256"), (U8, "wp512 vp128 xs256")):
+                     "of256 da256 dq128 th96 yo256 pf22 ka64 im64 rs128 ff192 kb16"),
+               (U16, "rku16 rks8 ofy16 ofm32 ofz32 ofs8 pl112 lu34"), (I32, "pi10"),
+               (CD, "wq512 vq128 xq384 lq512"), (U8, "wp512 vp128 xs384 ls512")):
     for _w in _l.split():
         _n = _w.rstrip("0123456789")
         SCRATCH[_n] = ("sbuf", [128, int(_w[len(_n):])], _d)
@@ -32,13 +36,8 @@ for _s in STAGES:
 for _t in range(3):
     SCRATCH["mq%d" % _t] = ("sbuf", [128, 256], CD)
     SCRATCH["ms%d" % _t] = ("sbuf", [128, 256], U8)
-    SCRATCH["lq%d" % _t] = ("sbuf", [128, 256], CD)
-    SCRATCH["ls%d" % _t] = ("sbuf", [128, 256], U8)
 
-POOL = {"v": 48, "a": 36, "t": 12, "g": 16}
-NDMA = 24
-SEMAPHORES = ([k + "%d" % i for k in POOL for i in range(POOL[k])] + ["dma%d" % i for i in range(NDMA)]
-              + ["arr%d" % i for i in range(6)] + ["sent"])
+SEMAPHORES = list("vatg") + ["dma%d" % i for i in range(20)] + ["arr%d" % i for i in range(6)] + ["sent"]
 PLAN = {}
 
 
@@ -64,7 +63,7 @@ def lanes(T, topo, rank):
 
 def build(T, topo, rank):
     ops = []
-    sent, lead, room = [0], [0], [0]
+    sent, lead, stage, ahead = [0], [0], [0, 0], [0]
     A, AF = AluOpType, ActivationFunctionType
 
     def ap(v, cast=None):
@@ -81,11 +80,11 @@ def build(T, topo, rank):
     def add(alt, rd, wr, kind="c", pre=None):
         rd = [x for x in rd if isinstance(x, tuple)]
         wr = [x for x in wr if isinstance(x, tuple)]
-        ops.append((alt, rd + [x[5] for x in rd + wr if x[5] is not None], wr, kind, pre, lead[0]))
+        ops.append((alt, rd + [x[5] for x in rd + wr if x[5] is not None], wr, kind, pre, lead[0], stage[1]))
 
     def halves():
         for h in range(2):
-            lead[0] = TUNE["lead"] * (1 - h)
+            lead[0] = TUNE["leads"][stage[0]] * (1 - h) + ahead[0]
             yield h
 
     def time(q, o, ins, rate=1.0):
@@ -95,6 +94,8 @@ def build(T, topo, rank):
             return (60 if q == "v" else 78) + TUNE["gather"] * size(o)
         if q == "v" and rate == 1.0 and all(SCRATCH[x[0]][2] in (BF, U16) for x in [o] + ins):
             rate = 0.5
+        if q == "a":
+            return max(TUNE["amin"], TUNE["afix"] + size(o))
         return max(TUNE["least"], rate * size(o))
 
     def tt(o, x, y, op):
@@ -109,8 +110,8 @@ def build(T, topo, rank):
         add({"v": (f, time("v", o, [x]))}, [x, s1, s2], [o])
 
     def scan(o, d0, d1, op0=A.mult, op1=A.add, first=0.0):
-        add({"v": (lambda e: e.tensor_tensor_scan(ap(o), ap(d0), ap(d1), ap(first), op0, op1), time("v", o, [d0, d1]))},
-            [d0, d1, first], [o])
+        add({"v": (lambda e: e.tensor_tensor_scan(ap(o), ap(d0), ap(d1), first, op0, op1), time("v", o, [d0, d1]))},
+            [d0, d1], [o])
 
     def tr(o, i):
         add({"v": (lambda e: e.transpose(ap(o), ap(i)), time("v", o, [i]))}, [i], [o])
@@ -144,7 +145,8 @@ def build(T, topo, rank):
         if "a" in on:
             alt["a"] = (lambda e: e.activation(ap(o), ap(i), AF.Copy), time("a", o, [i]))
         if "g" in on:
-            alt["g"] = (lambda e: e.affine_select(ap(o), ap(i), [[0, size(o)]], A.is_ge, 0.0, 0, 0), 205 + 2 * size(o))
+            alt["g"] = (lambda e: e.affine_select(ap(o), ap(i), [[0, size(o)]], A.is_ge, 0.0, 0, 0),
+                        TUNE["gx"] * (205 + 2 * size(o)))
         add(alt, [i], [o])
 
     def quant(c, s, i):
@@ -159,10 +161,10 @@ def build(T, topo, rank):
             f = lambda e: e.iota(ap(o), pat, base, cm)
         else:
             f = lambda e: e.iota(ap(o), pat, base, cm, allow_small_or_imprecise_dtypes=True)
-        add({"g": (f, 156 + 2 * size(o))}, [], [o])
+        add({"g": (f, TUNE["gx"] * (156 + 2 * size(o)))}, [], [o])
 
-    def dma(q, o, i, oc=None, ic=None, after=()):
-        add({q: (lambda e: e.dma_start(ap(o, oc), ap(i, ic)), 100)}, [i] + list(after), [o], "d")
+    def dma(q, o, i, oc=None, ic=None, after=(), pre=None):
+        add({q: (lambda e: e.dma_start(ap(o, oc), ap(i, ic)), 100)}, [i] + list(after), [o], "d", pre)
 
     def col(name, j):
         return V(name, j, j + 1)
@@ -176,153 +178,141 @@ def build(T, topo, rank):
     def half(name, h, a=0, n=64):
         return V(name, a + n * h, a + n * h + n)
 
-    QF, RF, CF, ODD, PL, T4, Q7, Q8, B2, EVN, SC, SC4, T44, Q1, Q2, Q21, Q22, P2, P21, P22, X1, X2 = [
-        col("pf", j) for j in range(22)]
-    PAR, PARS = [EVN, ODD], [col("pf", 22), col("pf", 23)]
+    QF, RF, CF, ODD, PL, T4, Q7, Q8, B2, EVN, SC, SC4, T44, Q1, P1, X1, X2, X3, X4, X5 = [col("pf", j) for j in range(20)]
+    PAR, PARS = [EVN, ODD], [col("pf", 20), col("pf", 21)]
     EXL, CXL, N4L = V("lu", 0, 4), V("lu", 4, 8), V("lu", 8, 9)
     NEAR = {8: (V("lu", 10, 18), V("lu", 18, 26), V("ff", 0, 128)), 4: (V("lu", 26, 30), V("lu", 30, 34), V("ff", 128, 192))}
-    RS4 = V("kb")
+    RS4 = V("kb", 0, 16)
     C16, MK16, RS16, WX, WM, WN = [V("kc", 128 * j, 128 * j + 128) for j in range(6)]
-    WP, TMP = V("kc", 768, 1024), 1024
+    WP = V("kc", 768, 1024)
     MK16H, RS16H = V("kc", 128, 192), V("kc", 256, 320)
     JALL, JHALF, ONES, MS, JKS = V("jb", 0, 256), V("jb", 256, 512), V("jb", 512, 768), V("jb", 768, 896), V("jb", 896, 1024)
 
-    def mark(o, spots, n):
-        head = V(o[0], o[1], o[1] + n)
-        for i, (s, v) in enumerate(spots):
-            tmp = V("kc", TMP + 32 * room[0], TMP + 32 * room[0] + n)
-            room[0] += 1 if i else 0
-            ts(tmp if i else head, V("jb", 0, n), s, A.is_equal, v - 1.0, A.mult)
-            if i:
-                tt(head, head, tmp, A.add)
-        lin(head, head, 1.0, 1.0)
+    def hold(head, one, me, nxt):
+        j = V("jb", 0, size(one))
+        ts(one, j, me, A.not_equal)
+        ts(head, j, nxt, A.is_equal, BIG, A.mult)
+        tt(head, head, one, A.max)
+
+    def repeat(o, n):
         while n < size(o):
             mov(V(o[0], o[1] + n, o[1] + 2 * n), V(o[0], o[1], o[1] + n), "a")
             n *= 2
 
+    lead[0] = TUNE["early"]
     dma("s", V("fa", PAD), T.x[:, 0:512])
     dma("a", V("fb", PAD), T.x[:, 512:1024])
     dma("s", V("wq"), T.wc[:, :], dt.uint8, None, [col("fa", PAD), col("fb", PAD)])
     dma("s", V("wp"), T.ws[:, :], None, None, [col("fa", PAD), col("fb", PAD)])
     dma("s", V("vt"), T.v[:, :], None, None, [col("fa", PAD), col("fb", PAD)])
     iota(col("pi", 0), [[0, 1]], 0, 1)
-    for f in ("fa", "fb", "fk", "ab", "ar"):
+    for f in ("fa", "fb", "ab", "ar"):
         ms(V(f, 0, PAD), 0.0)
     ms(V("fm", 0, 512), 0.0)
-    mov(V("fk", PAD), V("fm", 0, 512), "a")
-    for t in range(3):
-        quant(V("lq%d" % t, 0, 128), V("ls%d" % t, 0, 128), V("fm", 0, 512))
+    for h in range(2):
+        mov(V("fk", 1040 * h, 1040 * h + 272), V("fm", 0, 272), "a")
+    quant(V("lq", 0, 128), V("ls", 0, 128), V("fm", 0, 512))
     p = col("pi", 0)
     ts(col("pi", 1), p, 15, A.bitwise_and)
     ts(col("pi", 2), p, 31, A.bitwise_and)
     ts(col("pi", 3), p, 5, A.arith_shift_right)
     ts(col("pi", 4), p, 4, A.arith_shift_right, 1, A.bitwise_and)
+    mov(V("pf", 0, 4), V("pi", 1, 5), "v")
     ts(col("pi", 5), p, 2, A.arith_shift_right, 3, A.bitwise_and)
     ts(col("pi", 6), p, 3, A.bitwise_and)
     ts(col("pi", 7), p, 7, A.bitwise_and)
     ts(col("pi", 8), p, 3, A.arith_shift_right, 1, A.bitwise_and)
     ts(col("pi", 9), p, 2, A.arith_shift_right, 1, A.bitwise_and)
-    mov(V("pf", 0, 9), V("pi", 1, 10), "v")
+    mov(V("pf", 4, 9), V("pi", 5, 10), "v")
     lin(EVN, ODD, -1.0, 1.0)
     lin(PARS[0], EVN, 0.03125)
     lin(PARS[1], ODD, 0.03125)
-    iota(V("ka", 0, 32), [[32, 4], [0, 4], [16, 2]], 0)
+    iota(V("ka", 0, 32), [[32, 4], [0, 4], [16, 2]], 2)
     iota(V("ka", 32, 64), [[0, 4], [1, 4], [0, 2]], 0)
     ts(V("ka", 0, 32), V("ka", 0, 32), QF, A.add)
     ts(V("ka", 32, 64), V("ka", 32, 64), CF, A.is_equal)
-    for i, (s, b) in enumerate(((1.0, 2.0), (2.0, 2.0), (2.0, 3.0))):
-        z = V("ka", 64 + 32 * i, 96 + 32 * i)
-        lin(z, V("ka", 0, 32), s, b)
-        tt(z, z, V("ka", 32, 64), A.mult)
-        mov(V("pl", 32 * i, 32 * i + 32), z, "v")
+    tt(V("ka", 0, 32), V("ka", 0, 32), V("ka", 32, 64), A.mult)
+    for i, (s, b) in enumerate(((1.0, 0.0), (2.0, -2.0), (2.0, -1.0))):
+        lin(V("pl", 32 * i, 32 * i + 32), V("ka", 0, 32), s, b, "v")
+    lin(V("pl", 96, 112), V("ka", 0, 16), 1.0, 64.0, "v")
     iota(V("im"), [[1, 32], [0, 2]], 0)
     ts(V("im"), V("im"), RF, A.is_equal)
     ms(V("rs", 0, 64), 1.0)
     ms(V("rs", 64, 128), 1e29)
     ms(V("rs", 0, 64, 32), 0.0)
     ms(V("rs", 64, 128, 32), TINY)
-    iota(V("th", 0, 4), [[32, 2], [64, 2]], 31)
-    iota(V("th", 4, 8), [[4, 4]], 3)
-    iota(V("th", 8, 10), [[0, 2]], 31)
-    iota(V("th", 10, 18), [[2, 8]], 0)
-    iota(V("th", 18, 26), [[0, 8]], 15)
-    iota(V("th", 26, 30), [[4, 4]], 0)
-    iota(V("th", 30, 34), [[0, 4]], 15)
-    lin(X1, B2, 64.0)
-    lin(X2, Q8, 32.0, X1)
-    ts(V("th", 8, 10), V("th", 8, 10), X2, A.add)
-    lin(X1, Q7, 16.0)
-    ts(V("th", 10, 18), V("th", 10, 18), X1, A.add, Q8, A.add)
-    ts(V("th", 18, 26), V("th", 18, 26), X1, A.add)
-    lin(X2, T4, 16.0)
-    ts(V("th", 26, 30), V("th", 26, 30), X2, A.add, PL, A.add)
-    ts(V("th", 30, 34), V("th", 30, 34), X2, A.add)
-    mov(V("lu", 0, 34), V("th", 0, 34), "v")
-    iota(C16, [[0, 8], [1, 16]], 0)
+    iota(V("jb", 0, 16), [[1, 16]], 0)
+    iota(V("jb", 16, 256), [[1, 240]], 16)
+    for o, i, s, b in ((X1, B2, 64.0, 31.0), (X1, Q8, 32.0, X1), (X2, Q7, 16.0, Q8), (X3, Q7, 16.0, 15.0), (X4, T4, 16.0, PL),
+                       (X5, T4, 16.0, 15.0)):
+        lin(o, i, s, b, "a")
+    for a, b, z, s, x in ((0, 4, 2, 32.0, 31.0), (1, 4, 2, 32.0, 95.0), (4, 8, 1, 4.0, 3.0), (8, 10, 1, 0.0, X1),
+                          (10, 18, 1, 2.0, X2), (18, 26, 1, 0.0, X3), (26, 30, 1, 4.0, X4), (30, 34, 1, 0.0, X5)):
+        lin(V("lu", a, b, z), V("jb", 0, size(V("lu", a, b, z))), s, x, "v")
     iota(V("ff", 0, 128), [[1, 16], [0, 8]], 0)
     iota(V("ff", 128, 192), [[1, 16], [0, 4]], 0)
-    iota(RS4, [[0, 4], [1, 4]], 0)
-    iota(JALL, [[1, 256]], 0)
-    iota(JHALF, [[1, 128], [0, 2]], 0)
-    iota(V("ids", 128, 256), [[1, 128]], 128)
-    iota(ONES, [[0, 256]], 1)
-    iota(V("cc", 0, 256, 2), [[0, 128]], 0)
-    iota(V("fi", 1, 256, 2), [[2, 128]], 0)
-    iota(MS, [[0, 64], [-1, 2]], 0)
-    lin(JKS, V("jb", 128, 256), SMALL)
-    ts(MK16, C16, QF, A.is_equal)
-    ts(RS16, C16, 1.0, A.min)
-    ts(RS4, RS4, 1.0, A.min)
+    J = V("jb", 0, 128)
+    for o, i, s, b in ((V("jb", 256, 512, 2), J, 1.0, 0.0), (V("jb", 257, 512, 2), J, 1.0, 0.0), (ONES, JALL, 0.0, 1.0),
+                       (V("ids", 128, 256), J, 1.0, 128.0), (JKS, J, SMALL, 128 * SMALL), (V("cc", 0, 256, 2), J, 0.0, 0.0),
+                       (V("fi", 1, 256, 2), J, 2.0, 0.0), (V("jb", 768, 896, 2), V("jb", 0, 64), 0.0, 0.0),
+                       (V("jb", 769, 896, 2), V("jb", 0, 64), 0.0, -1.0), (T44, T4, 1.0, 4.0), (Q1, QF, 1.0, 1.0),
+                       (P1, PL, 1.0, 1.0)):
+        lin(o, i, s, b, "a")
+    ts(V("kc", MK16[1], MK16[1] + 16), V("jb", 0, 16), QF, A.is_equal)
+    act(V("kc", RS16[1], RS16[1] + 16), V("jb", 0, 16), AF.Sign)
+    act(V("kb", 0, 4), V("jb", 0, 4), AF.Sign)
     ts(V("ff"), V("ff"), QF, A.is_lt)
     lin(V("ff"), V("ff"), BELOW - 1.0, 1.0)
     ts(SC, QF, 15.0, A.is_lt, 1.0 / BIG - 1.0, A.mult)
     lin(SC, SC, 1.0, 1.0)
     ts(SC4, PL, 3.0, A.is_lt, 4.0 / BIG - 4.0, A.mult)
     lin(SC4, SC4, 1.0, 4.0)
-    for o, i, s, b in ((T44, T4, 1.0, 4.0), (Q1, QF, 1.0, 1.0), (Q2, QF, 2.0, 0.0), (Q21, QF, 2.0, 1.0), (Q22, QF, 2.0, 2.0),
-                       (P2, PL, 2.0, 0.0), (P21, PL, 2.0, 1.0), (P22, PL, 2.0, 2.0)):
-        lin(o, i, s, b)
-    mark(WX, [(QF, 0.0), (Q1, BIG + 1.0)], 16)
-    mark(WP, [(Q2, 0.0), (Q21, 1.0 / SMALL + 1.0), (Q22, BIG + 1.0)], 32)
-    mark(WM, [(P2, 0.0), (P22, BIG + 1.0)], 8)
-    mark(WN, [(P2, 0.0), (P21, -1.0), (P22, BIG + 1.0)], 8)
+    one = V("kc", 1024, 1040)
+    hold(V("kc", WX[1], WX[1] + 16), one, QF, Q1)
+    mov(V("kc", WP[1], WP[1] + 32, 2), V("kc", WX[1], WX[1] + 16), "a")
+    lin(V("kc", WP[1] + 1, WP[1] + 32, 2), one, -1.0 / SMALL, 1.0 / SMALL + 1.0, "a")
+    one = V("kc", 1040, 1044)
+    hold(V("kc", WM[1], WM[1] + 8, 2), one, PL, P1)
+    mov(V("kc", WN[1], WN[1] + 8, 2), V("kc", WM[1], WM[1] + 8, 2), "a")
+    lin(V("kc", WM[1] + 1, WM[1] + 8, 2), one, 0.0, 1.0, "a")
+    lin(V("kc", WN[1] + 1, WN[1] + 8, 2), one, 2.0, -1.0, "a")
+    for o, n in ((MK16, 16), (RS16, 16), (RS4, 4), (WX, 16), (WP, 32), (WM, 8), (WN, 8)):
+        repeat(o, n)
+    lead[0] = 0
     for t in range(4):
-        mov(plane("xp", t, 0, 128), V("fa", PAD + t, None, 4), "g")
-        mov(plane("xp", t, 128, 256), V("fb", PAD + t, None, 4), "g")
+        mov(plane("xp", t, 0, 128), V("fa", PAD + t, None, 4), "ga")
+        mov(plane("xp", t, 128, 256), V("fb", PAD + t, None, 4), "ga")
 
     def gram(st, f, kind, mv, w, v, b0, lst, only=(0, 1)):
         q, s = "q_" + st, "s_" + st
-        wide = kind == "wide"
-        n = TUNE["mh"] if wide else TUNE["mh0"]
         for h in halves():
             if h not in only:
                 continue
-            base, top = 0, 130
-            if wide and h:
-                quant(V(q, 130, 258), V(s, 130, 258), V(f, 528, 1040))
-                top = 258
-            elif kind == "late" and h:
-                base, top = 160, 290
-                quant(V(q, base, top), V(s, base, top), V(f, 8, 528))
-            elif h == 0:
-                quant(V(q, 0, 130), V(s, 0, 130), V(f, 8, 528))
-            if h < n and kind != "late":
+            base, top, m = 0, 130, 320 + 128 * h
+            if kind == "late":
+                base, top = 160 * h, 160 * h + 130
+                quant(V(q, base, top), V(s, base, top), V(f, 1040 * h + 8, 1040 * h + 528))
+                quant(V(q, m, m + 128), V(s, m, m + 128), V(f, 1040 * h + 528, 1040 * h + 1040))
+            else:
+                if h == 0:
+                    quant(V(q, 0, 130), V(s, 0, 130), V(f, 8, 528))
+                elif kind == "wide":
+                    quant(V(q, 130, 258), V(s, 130, 258), V(f, 528, 1040))
+                    top = 258
                 lead[0] += TUNE["mlead"]
                 for t in range(4):
                     for par in range(2):
-                        z = 1024 // n
-                        src = (V(f, PAD + z * h + 4 + t, PAD + z * h + z, 8) if wide
-                               else V(f, PAD + z // 2 * h + t, PAD + z // 2 * (h + 1), 4))
-                        lin(V(mv, z * h + 4 * par + t, z * h + z, 8), src, PAR[par])
+                        if kind == "wide":
+                            lin(V(mv, 512 * h + 4 * par + t, 512 * h + 512, 8),
+                                V(f, PAD + 512 * h + 4 + t, PAD + 512 * h + 512, 8), PAR[par])
+                        elif h == 0:
+                            lin(V(mv, 4 * par + t, 1024, 8), V(f, PAD + t, PAD + 512, 4), PAR[par])
                 lead[0] -= TUNE["mlead"]
-            m = 320 + 128 * h
-            quant(V(q, m, m + 128), V(s, m, m + 128), half(mv, h, 0, 512))
-            for z in range(TUNE["pk"][h]):
-                cw = 16 // TUNE["pk"][h]
-                off = half("pl", z, 32 * lst + 16 * h, cw)
-                o, i = half("tq_" + st, z, 256 * h, 16 * cw), IND(V(q, base, top), off)
-                add({"v": (lambda e, o=o, i=i: e.tensor_copy(ap(o, dt.uint32), ap(i, dt.uint32)), time("v", o, [i]))}, [i], [o])
-                mov(half("ts_" + st, z, 256 * h, 16 * cw), IND(V(s, base, top), off), "a")
+                quant(V(q, m, m + 128), V(s, m, m + 128), half(mv, h, 0, 512))
+            off = half("pl", h * (kind != "late"), 32 * lst, 16)
+            o, i = half("tq_" + st, h, 0, 256), IND(V(q, base, top), off)
+            add({"v": (lambda e, o=o, i=i: e.tensor_copy(ap(o, dt.uint32), ap(i, dt.uint32)), time("v", o, [i]))}, [i], [o])
+            mov(half("ts_" + st, h, 0, 256), IND(V(s, base, top), off), "a")
             for k in (2 * h, 2 * h + 1):
                 mm(bank(b0 + k), half("tq_" + st, k, 0, 128), half("ts_" + st, k, 0, 128), V(q, m, m + 128), V(s, m, m + 128))
                 tt(half(w, k), bank(b0 + k, 64 * (k % 2), 64), V("im"), A.mult)
@@ -350,45 +340,30 @@ def build(T, topo, rank):
             tt(half("mk", h, a), half("dd", h, a), MK16H, A.mult)
         scan(half("wr", h, a), RS16H, half("mk", h, a))
 
-    def places(a, slot, who, cm, cs, wins, out, times):
-        n, na = len(who), who.count("A")
+    def places(a, slot, n, na, cm, cs, wins, out, times):
         nl, dx, ff = NEAR[n]
         (cm, c0), (cs, s0) = cm, cs
-        w = [size(z) for z in wins(0)] + [0]
+        w = sum(size(z) for z in wins(0))
+        u = (w + 16) // 2
         tt(V("ee", slot, slot + 16 * n), IND(V("dd", a, a + 16 * n), nl), ff, A.mult)
-        tt(V(cm, c0 + n * w[0], c0 + n * w[0] + 16 * n), IND(V("wr", slot, slot + 16 * n), dx), V("ee", slot, slot + 16 * n),
-           A.is_gt)
-
-        def part(m, x, y):
-            return V(cm, c0 + n * x + m, c0 + n * y, n)
-
-        def total(m, x, y, end, first=0.0):
-            u = (y - x) // 2
-            scan(V(cs, end - u, end), part(m, x, x + u), part(m, x + u, y), A.add, A.add, first)
-        for m, e in enumerate(who):
-            me, acc, mid = col("wr", slot + 16 * m + 15), col("ra", slot // 16 + m), w[0] + 16
-            for i, win in enumerate(wins(m)):
-                o = part(m, mid * i, mid * i + w[i])
-                if e == "A" or e == "a" and not i:
+        tt(V(cm, c0 + n * w, c0 + 2 * n * u), IND(V("wr", slot, slot + 16 * n), dx), V("ee", slot, slot + 16 * n), A.is_gt)
+        for m in range(n):
+            me, x = col("wr", slot + 16 * m + 15), 0
+            for win in wins(m):
+                o = V(cm, c0 + n * x + m, c0 + n * (x + size(win)), n)
+                x += size(win)
+                if m < na:
                     act(o, win, AF.Sign, me, -1.0)
                 else:
                     ts(o, win, me, A.is_lt)
-            end = s0 + 128 * m + 128
-            if e in "Aa":
-                z = part(m, 0, mid + w[1] * (e == "A"))
-                act(z, z, AF.Relu, acc=acc)
-            if e == "v":
-                total(m, 0, mid, end - w[1] // 2)
-                acc = col(cs, end - w[1] // 2 - 1)
-            if e == "V":
-                total(m, 0, mid + w[1], end)
-            if e in "av":
-                total(m, mid, mid + w[1], end, acc)
+            if m < na:
+                z = V(cm, c0 + m, c0 + 2 * n * u, n)
+                act(z, z, AF.Relu, acc=col("ra", slot // 16 + m))
+            else:
+                scan(half(cs, m, s0, u), V(cm, c0 + m, c0 + n * u, n), V(cm, c0 + n * u + m, c0 + 2 * n * u, n), A.add, A.add)
         b = out[1]
-        if na:
-            ts(V(out[0], b, b + na), V("ra", slot // 16, slot // 16 + na), times, A.mult)
-        if na < n:
-            ts(V(out[0], b + na, b + n), V(cs, s0 + 128 * na + 127, s0 + 128 * n, 128), times, A.mult)
+        ts(V(out[0], b, b + na), V("ra", slot // 16, slot // 16 + na), times, A.mult)
+        ts(V(out[0], b + na, b + n), V(cs, s0 + u * na + u - 1, s0 + u * n, u), times, A.mult)
 
     def ring(name, a, w):
         return lambda m: [V(name, a + 16 * m + 16, a + 16 * m + 16 + w)]
@@ -398,46 +373,53 @@ def build(T, topo, rank):
 
     def layer(t_, h, f, a):
         come = 2 * len(lanes(T, topo, (rank - STEP[t_]) % len(T.cores)))
-        lq, ls = V("lq%d" % t_, 64 + 64 * h, 192 + 64 * h), V("ls%d" % t_, 64 + 64 * h, 192 + 64 * h)
+        lq, ls = [V(z, 64 + 128 * t_ + 64 * h, 192 + 128 * t_ + 64 * h) for z in ("lq", "ls")]
         lead[0] = TUNE["lead"] * (1 - h)
         for b in range(4):
-            mm(bank(4 + b), half("wq", b, 0, 128), half("wp", b, 0, 128), lq, ls, (T.sem["arr%d" % (2 * t_ + h)], come))
-            lin(V(f, a + 256 * h + b, a + 256 * h + 256, 4), bank(4 + b, 64, 64), 0.03125, None, TUNE["kq"][b])
+            z = b + 4 * (1 - h)
+            mm(bank(z), half("wq", b, 0, 128), half("wp", b, 0, 128), lq, ls, ("arr%d" % (2 * t_ + h), come))
+            lin(V(f, a + b, a + 256, 4), bank(z, 64, 64), 0.03125, None, TUNE["kq"][b])
             for par in range(2 if t_ < 2 else 0):
-                lin(V("mvd", 512 * h + 4 * par + b, 512 * h + 512, 8), bank(4 + b, 64, 64), PARS[par], None, TUNE["kq"][b])
+                lin(V(f, a + 256 + 4 * par + b, a + 768, 8), bank(z, 64, 64), PARS[par], None, TUNE["kq"][b])
+        lead[0] = 0
 
     for t_ in range(3):
         if t_ == 0:
+            ahead[0] = TUNE["ahead"]
             gram("d0", "fa", "", "mvd", "wd", "vd", 0, 0)
-            gram("d0b", "fb", "", "mvn", "wn", "vb", 4, 0)
             for h in halves():
                 sizes("vd", h, 0, 256, False, (0, 128))
+            ahead[0] = 0
+            gram("d0b", "fb", "", "mvn", "wn", "vb", 4, 0)
             for h in halves():
-                sizes("vb", h, 128, 384, True)
-            places(0, 0, TUNE["r0"], ("cma", 0), ("csa", 0), lambda m: ring("de", 0, 112)(m) + [V("dd", 128, 256)],
+                sizes("vb", h, 128, 384, h)
+            places(0, 0, 8, TUNE["r0"][0], ("cma", 0), ("csa", 0), lambda m: ring("de", 0, 112)(m) + [V("dd", 128, 256)],
                    V("rku", 0, 8), 1.0)
-            places(128, 128, TUNE["r0b"], ("cmb", 0), ("csb", 0), ring("dd", 128, 240), V("rku", 8, 16), 1.0)
+            places(128, 128, 8, TUNE["r0"][1], ("cmb", 0), ("csb", 0), ring("dd", 128, 240), V("rku", 8, 16), 1.0)
             mov(IND(V("on"), V("rku")), JALL, "v")
             for h in halves():
                 scan(half("ox", h, 0, 128), WX, half("on", h, 0, 128), A.mult, A.max)
                 ts(half("ofy", h, 0, 8), V("ox", 128 * h + 15, 128 * h + 128, 16), SC, A.mult)
         else:
+            stage[1] = 3 * t_
             for h in range(2):
-                layer(t_ - 1, h, "fk", PAD)
-                for t in range(4 * h):
-                    mov(plane("xp", t, 128, 256), V("fk", PAD + t, None, 4), "g")
-                gram("d%d" % t_, "fk", "late", "mvd", "wd", "vd", 0, 0, (h,))
+                a = 272 + 1040 * h
+                layer(t_ - 1, h, "fk", a)
+                for t in range(4):
+                    mov(plane("xp", t, 128 + 64 * h, 192 + 64 * h), V("fk", a + t, a + 256, 4), "g")
+                gram("d%d" % t_, "fk", "late", None, "wd", "vd", 4, 3, (h,))
                 lead[0] = TUNE["lead"] * (1 - h)
                 sizes("vd", h, 128, 384, h, None if h else (0, 192))
-            places(128, 128, TUNE["r"][0], ("cmb", 0), ("csb", 0), lambda m: ring("de", 0, 176)(m) + [V("dd", 192, 256)],
+            places(128, 128, 4, TUNE["r"][0], ("cmb", 0), ("csb", 0), lambda m: ring("de", 0, 176)(m) + [V("dd", 192, 256)],
                    V("rku", 8, 12), 2.0)
-            places(192, 192, TUNE["r"][1], ("cmb", 1024), ("csb", 512), ring("dd", 192, 240), V("rku", 12, 16), 2.0)
+            places(192, 192, 4, TUNE["r"][1], ("cmb", 1024), ("csb", 512), ring("dd", 192, 240), V("rku", 12, 16), 2.0)
             mov(IND(V("oo"), V("rku", 8, 16)), JKS, "v")
             scan(V("oo", 1, 512, 2), ONES, V("oo", 0, 512, 2), A.mult, A.subtract, -1.0)
             for h in halves():
                 scan(half("ox", h, 0, 256), WP, half("oo", h, 0, 256), A.mult, A.max)
                 ts(half("ofy", h, 0, 8), V("ox", 256 * h + 31, 256 * h + 256, 32), SC, A.mult)
 
+        stage[0], stage[1] = t_ + 1, 3 * t_ + 1
         for h in halves():
             for t in range(4):
                 mov(V("ab", PAD + 512 * h + t, PAD + 512 * h + 512, 4), IND(plane("xp", t), half("ofy", h, 0, 8)))
@@ -459,6 +441,7 @@ def build(T, topo, rank):
                 a = PAD + 512 * h + t
                 scan(V("ar", a, PAD + 512 * h + 512, 4), half("cc", h, 0, 128), V("ab", a, PAD + 512 * h + 512, 4))
         to = topo.addr(T.cores[(rank + STEP[t_]) % len(T.cores)])
+        stage[1] += 1
         gram("e%d" % t_, "ar", "wide", "mve", "we", "ve", 0, 2)
         for h in halves():
             tt(half("ub", h), wide("ve", h), half("dq", h), A.is_ge)
@@ -470,10 +453,10 @@ def build(T, topo, rank):
             m = 128 * h
             quant(V("mq%d" % t_, m, m + 128), V("ms%d" % t_, m, m + 128), V("fm", 256 + 2 * m, 768 + 2 * m))
             for src, dst, cast in (("mq", "lq", dt.uint8), ("ms", "ls", None)):
-                o, i = V(dst + "%d" % t_, 128 + 64 * h, 192 + 64 * h), V(src + "%d" % t_, m + 64, m + 128)
+                o, i = half(dst, 2 * t_ + h, 128), V(src + "%d" % t_, m + 64, m + 128)
                 add({"g": (lambda e, o=o, i=i, cast=cast, arr=T.sem["arr%d" % (2 * t_ + h)], to=to:
-                           e.remote_dma(ap(o, cast), ap(i, cast), arr, T.sem.sent, to[1], to[0], mask), TUNE["send"])},
-                    [i], [o], "r")
+                           e.remote_dma(ap(o, cast), ap(i, cast), arr, T.sem.sent, to[1], to[0], mask),
+                           TUNE["send"] + TUNE["first"] * (not sent[0]))}, [i], [o], "r")
                 sent[0] += len(eng)
 
         if t_ < 2:
@@ -486,7 +469,7 @@ def build(T, topo, rank):
                 tt(half("mk", h), half("dd", h, 128), MK16H, A.mult)
                 scan(half("wr", h), RS16H, half("mk", h))
             lin(V("de", 64, 192), V("dd", 128, 256), BELOW)
-            places(128, 0, TUNE["ss"], ("cma", 0), ("csa", 0), ring("dd", 128, 112), V("rks", 0, 8), 1.0)
+            places(128, 0, 8, TUNE["ss"], ("cma", 0), ("csa", 0), ring("dd", 128, 112), V("rks", 0, 8), 1.0)
             mov(V("dw", 0, 256, 2), V("dd", 128, 256), "ga")
             mov(V("dw", 1, 256, 2), V("dd", 128, 256), "ga")
             for t in range(4):
@@ -507,18 +490,18 @@ def build(T, topo, rank):
             quant(V("vq"), V("vp"), V("vt"))
             quant(V("xq", 0, 128), V("xs", 0, 128), V("xf", 0, 512))
             mm(bank(0), V("vq"), V("vp"), V("xq", 0, 128), V("xs", 0, 128))
-            dma("s", T.oc[:, 0:512], V("xq", 0, 128), None, dt.uint8)
             mov(V("yo", 0, 128), bank(0))
+            dma("s", T.oc[:, 0:512], V("xq", 0, 128), None, dt.uint8)
             dma("s", T.y[:, 0:128], V("yo", 0, 128))
 
     for h in range(2):
-        layer(2, h, "xf", 512)
+        layer(2, h, "xf", 512 + 256 * h)
     quant(V("xq", 128, 256), V("xs", 128, 256), V("xf", 512, 1024))
-    mm(bank(1), V("vq"), V("vp"), V("xq", 128, 256), V("xs", 128, 256))
+    mm(bank(4), V("vq"), V("vp"), V("xq", 128, 256), V("xs", 128, 256))
     dma("a", T.oc[:, 512:1024], V("xq", 128, 256), None, dt.uint8)
-    for k, e in enumerate("saaa"):
-        dma(e, T.osc[4 * k:4 * k + 4, :], V("xs", None, None, None, (32 * k, 32 * k + 4)))
-    mov(V("yo", 128, 256), bank(1))
+    for k, e in enumerate("ssaa"):
+        dma(e, T.osc[4 * k:4 * k + 4, :], V("xs", 0, 256, None, (32 * k, 32 * k + 4)))
+    mov(V("yo", 128, 256), bank(4), "v")
     dma("s", T.y[:, 128:256], V("yo", 128, 256))
     return ops, sent[0]
 
@@ -533,7 +516,7 @@ def order(ops):
         return int.from_bytes(np.packbits(m).tobytes(), "big")
 
     seen, deps = {}, []
-    for i, (alt, rd, wr, kind, pre, lead) in enumerate(ops):
+    for i, (alt, rd, wr, kind, pre, lead, part) in enumerate(ops):
         acc = [(v[0], cols(v), False) for v in rd] + [(v[0], cols(v), True) for v in wr]
         deps.append({j for name, m, w in acc for j, mj, wj in seen.get(name, []) if m & mj and (
             w or wj or name == "ps" and len(set(alt) | set(ops[j][0])) > 1)})
@@ -541,12 +524,18 @@ def order(ops):
             seen.setdefault(name, []).append((i, m, w))
     late = {"c": TUNE["wake"], "d": TUNE["dma"], "r": TUNE["far"]}
     n = len(ops)
-    togo, users = [0.0] * n, [set() for i in range(n)]
-    for i in range(n - 1, -1, -1):
-        togo[i] += min(c for f, c in ops[i][0].values()) + late[ops[i][3]]
+    users = [set() for i in range(n)]
+    for i in range(n):
         for j in deps[i]:
-            togo[j] = max(togo[j], togo[i] + max(0, ops[j][5] - ops[i][5]))
             users[j].add(i)
+
+    def urgent(weight):
+        togo = [0.0] * n
+        for i in range(n - 1, -1, -1):
+            togo[i] += min(c for f, c in ops[i][0].values()) + late[ops[i][3]]
+            for j in deps[i]:
+                togo[j] = max(togo[j], togo[i] + weight[ops[j][6]] * max(0, ops[j][5] - ops[i][5]))
+        return sorted(range(n), key=lambda i: (-togo[i], i))
 
     def place(seq, back):
         busy, start, end, queue = {q: [] for q in "vatgs"}, {}, {}, {}
@@ -584,15 +573,91 @@ def order(ops):
         return seq
 
     rng = np.random.default_rng(TUNE["seed"])
-    best = place(sorted(range(n), key=lambda i: (-togo[i], i)), False)
-    for turn in range(TUNE["turns"]):
-        shake = rng.random(n) * TUNE["shake"] * (turn > 0)
-        back = place(sort([-best[2][i] + shake[i] for i in range(n)], users, deps), True)
-        now = place(sorted(range(n), key=lambda i: (-back[2][i], i)), False)
-        if now[0] <= best[0]:
-            best = now
+
+    def settle(weight, turns):
+        good = place(urgent(weight), False)
+        for turn in range(turns):
+            shake = rng.random(n) * TUNE["shake"] * (turn > 0)
+            back = place(sort([-good[2][i] + shake[i] for i in range(n)], users, deps), True)
+            now = place(sorted(range(n), key=lambda i: (-back[2][i], i)), False)
+            if now[0] <= good[0]:
+                good = now
+        return good
+
+    weight = [1.0] * 9
+    best = settle(weight, 1)
+    for part in range(9):
+        for w in TUNE["weights"]:
+            other = weight[:part] + [w] + weight[part + 1:]
+            now = settle(other, 1)
+            if now[0] < best[0]:
+                best, weight = now, other
+    now = settle(weight, TUNE["turns"])
+    if now[0] < best[0]:
+        best = now
     PLAN["time"] = best[0]
-    return deps, best[3], sorted(range(n), key=lambda i: (best[1][i], i))
+    seq, queue = sorted(range(n), key=lambda i: (best[1][i], i)), dict(best[3])
+    cost = [{q: c for q, (f, c) in o[0].items()} for o in ops]
+    for a in [a for first in TUNE["passes"] for a in range(first, n - TUNE["step"], TUNE["step"])]:
+        b = min(n, a + TUNE["span"])
+        part, inside, cases = seq[a:b], set(seq[a:b]), []
+        for f, far in TUNE["cases"]:
+            lat = [far if o[3] == "r" else late[o[3]] for o in ops]
+            free, end, tail, nxt = {}, {}, {}, {}
+            for i in seq[:a]:
+                q = queue[i]
+                end[i] = free[q] = cost[i][q] * f + max([free.get(q, 0.0)] + [end[j] + lat[j] for j in deps[i]])
+            for i in reversed(seq[b:]):
+                q = queue[i]
+                tail[i] = nxt[q] = cost[i][q] * f + max([nxt.get(q, 0.0), lat[i]] + [lat[i] + tail[j] for j in users[i]])
+            head = {i: max([end[j] + lat[j] for j in deps[i] if j not in inside], default=0.0) for i in part}
+            out = {i: max([lat[i] + tail[j] for j in users[i] if j not in inside], default=lat[i]) for i in part}
+            cases.append((f, lat, free, nxt, head, out))
+        near = {i: [j for j in deps[i] if j in inside] for i in part}
+
+        def worth(part):
+            total = 0.0
+            for f, lat, free, nxt, head, out in cases:
+                free, end, top, mean = dict(free), {}, 0.0, 0.0
+                for i in part:
+                    q = queue[i]
+                    t = max(free.get(q, 0.0), head[i])
+                    for j in near[i]:
+                        if end[j] > t:
+                            t = end[j]
+                    t += cost[i][q] * f
+                    free[q], end[i] = t, t + lat[i]
+                    t += out[i]
+                    mean += t
+                    if t > top:
+                        top = t
+                total += (max([top] + [free.get(q, 0.0) + nxt[q] for q in nxt]) + 0.3 * mean / len(part)) / f
+            return total
+        now = worth(part)
+        keep = (now, part, dict(queue))
+        for turn, (u, v, w, x) in enumerate(rng.random((TUNE["moves"], 4)).tolist()):
+            k = z = int(u * len(part))
+            i, far = part[k], int((v - 0.5) * 2 * TUNE["reach"])
+            was = queue[i]
+            if len(cost[i]) > 1 and w < 0.3:
+                queue[i] = [q for q in cost[i] if q != was][0]
+            while z > max(0, k + far) and part[z - 1] not in deps[i]:
+                z -= 1
+            while z < min(len(part) - 1, k + far) and i not in deps[part[z + 1]]:
+                z += 1
+            if z == k and queue[i] == was:
+                continue
+            other = part[:k] + part[k + 1:]
+            other.insert(z, i)
+            new = worth(other)
+            if new <= now - TUNE["heat"] * (1 - turn / TUNE["moves"]) * math.log(x + 1e-12):
+                part, now = other, new
+                if now < keep[0]:
+                    keep = (now, part, dict(queue))
+            else:
+                queue[i] = was
+        seq[a:b], queue = keep[1], keep[2]
+    return deps, queue, seq
 
 
 def emit(g, T, ops, sent):
@@ -602,56 +667,42 @@ def emit(g, T, ops, sent):
     deps, queue, seq = PLAN["order"]
     at = {i: k for k, i in enumerate(seq)}
 
-    known = {q: 0 for q in eng}
-    at_issue, waits, needed = {}, {}, set()
+    known, done = {q: 0 for q in eng}, {q: 0 for q in eng}
+    at_end, waits, needed = {}, {}, set()
     for i in seq:
         q, ws = queue[i], []
         for j in sorted(deps[i], key=lambda j: -at[j]):
             if ops[j][3] != "r" and not known[q] >> j & 1:
                 ws.append(j)
-                known[q] |= at_issue[j] | 1 << j
+                known[q] |= at_end[j]
         waits[i] = ws
         needed.update(ws)
-        at_issue[i] = known[q]
+        if ops[i][3] == "c":
+            done[q] |= 1 << i
+        at_end[i] = known[q] | (done[q] if ops[i][3] == "c" else 1 << i)
 
-    known = {q: 0 for q in eng}
-    at_issue, tag, last, turn, count = {}, {}, {}, {q: 0 for q in eng}, {}
-    ndma, open_dma, come = [0], [], []
-
-    def wait(q, j):
-        if not known[q] >> j & 1:
-            eng[q].wait_ge(T.sem[tag[j][0]], tag[j][1])
-            known[q] |= at_issue[j] | 1 << j
-
+    tag, count, ndma, open_dma, come = {}, {q: 0 for q in eng}, [0], [], []
     for i in seq:
-        alt, rd, wr, kind, pre, lead = ops[i]
+        alt, rd, wr, kind, pre, lead, part = ops[i]
         q = queue[i]
-        if pre is not None and rd[2] not in come:
-            come.append(rd[2])
-            eng[q].wait_ge(pre[0], pre[1])
+        if pre is not None and pre not in come:
+            come.append(pre)
+            eng[q].wait_ge(T.sem[pre[0]], pre[1])
         for j in waits[i]:
-            wait(q, j)
-        name = None
+            eng[q].wait_ge(T.sem[tag[j][0]], tag[j][1])
+        ins = alt[q][0](eng[q])
         if kind == "d":
-            name = "dma%d" % ndma[0]
+            tag[i] = ("dma%d" % ndma[0], 16)
             ndma[0] += 1
-            tag[i] = (name, 16)
+            ins.then_inc(T.sem[tag[i][0]], 16)
             if i not in needed:
                 open_dma.append(i)
         elif kind == "c" and i in needed:
-            name = q + "%d" % (turn[q] % POOL[q])
-            turn[q] += 1
-            if name in last:
-                wait(q, last[name])
-            last[name] = i
-            count[name] = count.get(name, 0) + 1
-            tag[i] = (name, count[name])
-        at_issue[i] = known[q]
-        ins = alt[q][0](eng[q])
-        if name is not None:
-            ins.then_inc(T.sem[name], 16 if kind == "d" else 1)
+            count[q] += 1
+            tag[i] = (q, count[q])
+            ins.then_inc(T.sem[q], 1)
     for j in open_dma:
-        wait(queue[j], j)
+        eng[queue[j]].wait_ge(T.sem[tag[j][0]], 16)
     g.wait_ge(T.sem.sent, sent)
 
 

import math
import numpy as np
from concourse.mybir import dt, AluOpType, ActivationFunctionType

F32, BF, I32, U16, CD, U8 = "float32", "bfloat16", "int32", "uint16", "float8_e4m3fn_x4", "uint8"
STEP = [1, 2, 4]
STAGES = ["d0", "d0b", "n0", "e0", "d1", "n1", "e1", "d2", "n2", "e2"]
TINY = 2.0 ** -100
BELOW = 1.0 - 2.0 ** -24
BIG = 65536.0
SMALL = 2.0 ** -23
PAD = 16
TUNE = {"r0": (3, 4), "r": (2, 2), "ss": 4, "kq": "avav",
        "wake": 268, "dma": 3100, "far": 2400, "send": 360, "first": 120, "least": 64, "gather": 1.56, "scatter": 3.8,
        "amin": 64, "afix": 0, "spare": 80, "leads": (360, 700, 700, 400), "lead": 900, "mlead": -150, "ahead": 500,
        "early": 20000, "gx": 1.4, "turns": 2, "shake": 100, "seed": 3, "weights": (0.6, 1.3),
        "passes": (0, 45, 20), "step": 90, "span": 140, "moves": 9000, "reach": 30, "heat": 8,
        "cases": ((1.0, 2400), (1.25, 3000), (1.4, 4300))}

SCRATCH = {"ps": ("psum", [128, 4096], F32)}
for _d, _l in ((BF, "fa528 fb528 fk2080 ab1040 ar1040 mvd1024 mvn1024 mve1024 xp1024 ap1024 fm1024 xf1024 vt512 "
                    "cma2048 cmb2048 csa1024 csb1024 oo512 on256 ox512 ids256 so128 fi256 fs256 ub128 uc128 cc256 bx256 "
                    "bz256 kc1056 jb1024"),
               (F32, "wd256 wn256 we256 vd256 vb256 vn256 ve256 ua256 us128 de256 um256 dd512 mk256 wr256 ee256 dw256 ra16 "
                     "of256 da256 dq128 th96 yo256 pf22 ka64 im64 rs128 ff192 kb16"),
               (U16, "rku16 rks8 ofy16 ofm32 ofz32 ofs8 pl112 lu34"), (I32, "pi10"),
               (CD, "wq512 vq128 xq384 lq512"), (U8, "wp512 vp128 xs384 ls512")):
    for _w in _l.split():
        _n = _w.rstrip("0123456789")
        SCRATCH[_n] = ("sbuf", [128, int(_w[len(_n):])], _d)
for _s in STAGES:
    SCRATCH["q_" + _s] = ("sbuf", [128, 576], CD)
    SCRATCH["s_" + _s] = ("sbuf", [128, 576], U8)
    SCRATCH["tq_" + _s] = ("sbuf", [128, 512], CD)
    SCRATCH["ts_" + _s] = ("sbuf", [128, 512], U8)
for _t in range(3):
    SCRATCH["mq%d" % _t] = ("sbuf", [128, 256], CD)
    SCRATCH["ms%d" % _t] = ("sbuf", [128, 256], U8)

SEMAPHORES = list("vatg") + ["dma%d" % i for i in range(20)] + ["arr%d" % i for i in range(6)] + ["sent"]
PLAN = {}


def V(name, a=None, b=None, s=None, p=None):
    return (name, a, b, s, p, None)


def IND(win, off):
    return win[:5] + (off,)


def size(v):
    if v[5] is not None:
        return 16 * size(v[5])
    return len(range(*slice(v[1], v[2], v[3]).indices(SCRATCH[v[0]][1][1])))


def lanes(T, topo, rank):
    n = len(T.cores)
    sets = [topo.engines(T.cores[rank], T.cores[(rank + s) % n]) for s in STEP]
    return [k for k in sets[0] if all(k in z for z in sets)]


def build(T, topo, rank):
    ops = []
    sent, lead, stage, ahead = [0], [0], [0, 0], [0]
    A, AF = AluOpType, ActivationFunctionType

    def ap(v, cast=None):
        if not isinstance(v, tuple):
            return v
        name, a, b, s, p, off = v
        x = T[name][slice(None) if p is None else slice(*p), slice(a, b, s)]
        if cast is not None:
            x = x.bitcast(cast)
        if off is not None:
            x = x.indirect(ap(off))
        return x

    def add(alt, rd, wr, kind="c", pre=None):
        rd = [x for x in rd if isinstance(x, tuple)]
        wr = [x for x in wr if isinstance(x, tuple)]
        ops.append((alt, rd + [x[5] for x in rd + wr if x[5] is not None], wr, kind, pre, lead[0], stage[1]))

    def halves():
        for h in range(2):
            lead[0] = TUNE["leads"][stage[0]] * (1 - h) + ahead[0]
            yield h

    def time(q, o, ins, rate=1.0):
        if o[5] is not None:
            return 60 + TUNE["scatter"] * size(o)
        if ins and ins[0][5] is not None:
            return (60 if q == "v" else 78) + TUNE["gather"] * size(o)
        if q == "v" and rate == 1.0 and all(SCRATCH[x[0]][2] in (BF, U16) for x in [o] + ins):
            rate = 0.5
        if q == "a":
            return max(TUNE["amin"], TUNE["afix"] + size(o))
        return max(TUNE["least"], rate * size(o))

    def tt(o, x, y, op):
        add({"v": (lambda e: e.tensor_tensor(ap(o), ap(x), ap(y), op), time("v", o, [x, y], 1.01 if x[0] == "ps" else 2.0))},
            [x, y], [o])

    def ts(o, x, s1, op0, s2=None, op1=None):
        if op1 is None:
            f = lambda e: e.tensor_scalar(ap(o), ap(x), ap(s1), None, op0)
        else:
            f = lambda e: e.tensor_scalar(ap(o), ap(x), ap(s1), ap(s2), op0, op1)
        add({"v": (f, time("v", o, [x]))}, [x, s1, s2], [o])

    def scan(o, d0, d1, op0=A.mult, op1=A.add, first=0.0):
        add({"v": (lambda e: e.tensor_tensor_scan(ap(o), ap(d0), ap(d1), first, op0, op1), time("v", o, [d0, d1]))},
            [d0, d1], [o])

    def tr(o, i):
        add({"v": (lambda e: e.transpose(ap(o), ap(i)), time("v", o, [i]))}, [i], [o])

    def ms(o, c):
        add({"v": (lambda e: e.memset(ap(o), c), time("v", o, []))}, [], [o])

    def act(o, i, f, bias=0.0, scale=1.0, acc=None):
        if acc is not None:
            g = lambda e: e.activation(ap(o), ap(i), f, bias=ap(bias), scale=ap(scale), accum_out=ap(acc))
        else:
            g = lambda e: e.activation(ap(o), ap(i), f, bias=ap(bias), scale=ap(scale))
        add({"a": (g, time("a", o, [i]) + (24 if acc else 0))}, [i, bias, scale], [o, acc])

    def lin(o, i, scale, bias=None, on="va"):
        alt = {}
        if "v" in on:
            if bias is None:
                alt["v"] = (lambda e: e.tensor_scalar(ap(o), ap(i), ap(scale), None, A.mult), time("v", o, [i]))
            else:
                alt["v"] = (lambda e: e.tensor_scalar(ap(o), ap(i), ap(scale), ap(bias), A.mult, A.add), time("v", o, [i]))
        if "a" in on:
            alt["a"] = (lambda e: e.activation(ap(o), ap(i), AF.Identity, bias=ap(0.0 if bias is None else bias),
                                               scale=ap(scale)), time("a", o, [i]))
        add(alt, [i, scale, bias], [o])

    def mov(o, i, on="va"):
        alt = {}
        if "v" in on:
            alt["v"] = (lambda e: e.tensor_copy(ap(o), ap(i)), time("v", o, [i]))
        if "a" in on:
            alt["a"] = (lambda e: e.activation(ap(o), ap(i), AF.Copy), time("a", o, [i]))
        if "g" in on:
            alt["g"] = (lambda e: e.affine_select(ap(o), ap(i), [[0, size(o)]], A.is_ge, 0.0, 0, 0),
                        TUNE["gx"] * (205 + 2 * size(o)))
        add(alt, [i], [o])

    def quant(c, s, i):
        add({"v": (lambda e: e.quantize_mx(ap(c), ap(s), ap(i)), 15 + 0.265 * size(i))}, [i], [c, s])

    def mm(o, lq, ls, rq, rs, pre=None):
        add({"t": (lambda e: e.matmul_mx(ap(o), ap(lq), ap(ls), ap(rq), ap(rs), True, True), 16 + size(o))},
            [lq, ls, rq, rs], [o], "c", pre)

    def iota(o, pat, base, cm=0):
        if SCRATCH[o[0]][2] == I32:
            f = lambda e: e.iota(ap(o), pat, base, cm)
        else:
            f = lambda e: e.iota(ap(o), pat, base, cm, allow_small_or_imprecise_dtypes=True)
        add({"g": (f, TUNE["gx"] * (156 + 2 * size(o)))}, [], [o])

    def dma(q, o, i, oc=None, ic=None, after=(), pre=None):
        add({q: (lambda e: e.dma_start(ap(o, oc), ap(i, ic)), 100)}, [i] + list(after), [o], "d", pre)

    def col(name, j):
        return V(name, j, j + 1)

    def bank(b, a=0, n=128):
        return V("ps", 512 * b + a, 512 * b + a + n)

    def plane(name, t, a=0, b=256):
        return V(name, 256 * t + a, 256 * t + b)

    def half(name, h, a=0, n=64):
        return V(name, a + n * h, a + n * h + n)

    QF, RF, CF, ODD, PL, T4, Q7, Q8, B2, EVN, SC, SC4, T44, Q1, P1, X1, X2, X3, X4, X5 = [col("pf", j) for j in range(20)]
    PAR, PARS = [EVN, ODD], [col("pf", 20), col("pf", 21)]
    EXL, CXL, N4L = V("lu", 0, 4), V("lu", 4, 8), V("lu", 8, 9)
    NEAR = {8: (V("lu", 10, 18), V("lu", 18, 26), V("ff", 0, 128)), 4: (V("lu", 26, 30), V("lu", 30, 34), V("ff", 128, 192))}
    RS4 = V("kb", 0, 16)
    C16, MK16, RS16, WX, WM, WN = [V("kc", 128 * j, 128 * j + 128) for j in range(6)]
    WP = V("kc", 768, 1024)
    MK16H, RS16H = V("kc", 128, 192), V("kc", 256, 320)
    JALL, JHALF, ONES, MS, JKS = V("jb", 0, 256), V("jb", 256, 512), V("jb", 512, 768), V("jb", 768, 896), V("jb", 896, 1024)

    def hold(head, one, me, nxt):
        j = V("jb", 0, size(one))
        ts(one, j, me, A.not_equal)
        ts(head, j, nxt, A.is_equal, BIG, A.mult)
        tt(head, head, one, A.max)

    def repeat(o, n):
        while n < size(o):
            mov(V(o[0], o[1] + n, o[1] + 2 * n), V(o[0], o[1], o[1] + n), "a")
            n *= 2

    lead[0] = TUNE["early"]
    dma("s", V("fa", PAD), T.x[:, 0:512])
    dma("a", V("fb", PAD), T.x[:, 512:1024])
    dma("s", V("wq"), T.wc[:, :], dt.uint8, None, [col("fa", PAD), col("fb", PAD)])
    dma("s", V("wp"), T.ws[:, :], None, None, [col("fa", PAD), col("fb", PAD)])
    dma("s", V("vt"), T.v[:, :], None, None, [col("fa", PAD), col("fb", PAD)])
    iota(col("pi", 0), [[0, 1]], 0, 1)
    for f in ("fa", "fb", "ab", "ar"):
        ms(V(f, 0, PAD), 0.0)
    ms(V("fm", 0, 512), 0.0)
    for h in range(2):
        mov(V("fk", 1040 * h, 1040 * h + 272), V("fm", 0, 272), "a")
    quant(V("lq", 0, 128), V("ls", 0, 128), V("fm", 0, 512))
    p = col("pi", 0)
    ts(col("pi", 1), p, 15, A.bitwise_and)
    ts(col("pi", 2), p, 31, A.bitwise_and)
    ts(col("pi", 3), p, 5, A.arith_shift_right)
    ts(col("pi", 4), p, 4, A.arith_shift_right, 1, A.bitwise_and)
    mov(V("pf", 0, 4), V("pi", 1, 5), "v")
    ts(col("pi", 5), p, 2, A.arith_shift_right, 3, A.bitwise_and)
    ts(col("pi", 6), p, 3, A.bitwise_and)
    ts(col("pi", 7), p, 7, A.bitwise_and)
    ts(col("pi", 8), p, 3, A.arith_shift_right, 1, A.bitwise_and)
    ts(col("pi", 9), p, 2, A.arith_shift_right, 1, A.bitwise_and)
    mov(V("pf", 4, 9), V("pi", 5, 10), "v")
    lin(EVN, ODD, -1.0, 1.0)
    lin(PARS[0], EVN, 0.03125)
    lin(PARS[1], ODD, 0.03125)
    iota(V("ka", 0, 32), [[32, 4], [0, 4], [16, 2]], 2)
    iota(V("ka", 32, 64), [[0, 4], [1, 4], [0, 2]], 0)
    ts(V("ka", 0, 32), V("ka", 0, 32), QF, A.add)
    ts(V("ka", 32, 64), V("ka", 32, 64), CF, A.is_equal)
    tt(V("ka", 0, 32), V("ka", 0, 32), V("ka", 32, 64), A.mult)
    for i, (s, b) in enumerate(((1.0, 0.0), (2.0, -2.0), (2.0, -1.0))):
        lin(V("pl", 32 * i, 32 * i + 32), V("ka", 0, 32), s, b, "v")
    lin(V("pl", 96, 112), V("ka", 0, 16), 1.0, 64.0, "v")
    iota(V("im"), [[1, 32], [0, 2]], 0)
    ts(V("im"), V("im"), RF, A.is_equal)
    ms(V("rs", 0, 64), 1.0)
    ms(V("rs", 64, 128), 1e29)
    ms(V("rs", 0, 64, 32), 0.0)
    ms(V("rs", 64, 128, 32), TINY)
    iota(V("jb", 0, 16), [[1, 16]], 0)
    iota(V("jb", 16, 256), [[1, 240]], 16)
    for o, i, s, b in ((X1, B2, 64.0, 31.0), (X1, Q8, 32.0, X1), (X2, Q7, 16.0, Q8), (X3, Q7, 16.0, 15.0), (X4, T4, 16.0, PL),
                       (X5, T4, 16.0, 15.0)):
        lin(o, i, s, b, "a")
    for a, b, z, s, x in ((0, 4, 2, 32.0, 31.0), (1, 4, 2, 32.0, 95.0), (4, 8, 1, 4.0, 3.0), (8, 10, 1, 0.0, X1),
                          (10, 18, 1, 2.0, X2), (18, 26, 1, 0.0, X3), (26, 30, 1, 4.0, X4), (30, 34, 1, 0.0, X5)):
        lin(V("lu", a, b, z), V("jb", 0, size(V("lu", a, b, z))), s, x, "v")
    iota(V("ff", 0, 128), [[1, 16], [0, 8]], 0)
    iota(V("ff", 128, 192), [[1, 16], [0, 4]], 0)
    J = V("jb", 0, 128)
    for o, i, s, b in ((V("jb", 256, 512, 2), J, 1.0, 0.0), (V("jb", 257, 512, 2), J, 1.0, 0.0), (ONES, JALL, 0.0, 1.0),
                       (V("ids", 128, 256), J, 1.0, 128.0), (JKS, J, SMALL, 128 * SMALL), (V("cc", 0, 256, 2), J, 0.0, 0.0),
                       (V("fi", 1, 256, 2), J, 2.0, 0.0), (V("jb", 768, 896, 2), V("jb", 0, 64), 0.0, 0.0),
                       (V("jb", 769, 896, 2), V("jb", 0, 64), 0.0, -1.0), (T44, T4, 1.0, 4.0), (Q1, QF, 1.0, 1.0),
                       (P1, PL, 1.0, 1.0)):
        lin(o, i, s, b, "a")
    ts(V("kc", MK16[1], MK16[1] + 16), V("jb", 0, 16), QF, A.is_equal)
    act(V("kc", RS16[1], RS16[1] + 16), V("jb", 0, 16), AF.Sign)
    act(V("kb", 0, 4), V("jb", 0, 4), AF.Sign)
    ts(V("ff"), V("ff"), QF, A.is_lt)
    lin(V("ff"), V("ff"), BELOW - 1.0, 1.0)
    ts(SC, QF, 15.0, A.is_lt, 1.0 / BIG - 1.0, A.mult)
    lin(SC, SC, 1.0, 1.0)
    ts(SC4, PL, 3.0, A.is_lt, 4.0 / BIG - 4.0, A.mult)
    lin(SC4, SC4, 1.0, 4.0)
    one = V("kc", 1024, 1040)
    hold(V("kc", WX[1], WX[1] + 16), one, QF, Q1)
    mov(V("kc", WP[1], WP[1] + 32, 2), V("kc", WX[1], WX[1] + 16), "a")
    lin(V("kc", WP[1] + 1, WP[1] + 32, 2), one, -1.0 / SMALL, 1.0 / SMALL + 1.0, "a")
    one = V("kc", 1040, 1044)
    hold(V("kc", WM[1], WM[1] + 8, 2), one, PL, P1)
    mov(V("kc", WN[1], WN[1] + 8, 2), V("kc", WM[1], WM[1] + 8, 2), "a")
    lin(V("kc", WM[1] + 1, WM[1] + 8, 2), one, 0.0, 1.0, "a")
    lin(V("kc", WN[1] + 1, WN[1] + 8, 2), one, 2.0, -1.0, "a")
    for o, n in ((MK16, 16), (RS16, 16), (RS4, 4), (WX, 16), (WP, 32), (WM, 8), (WN, 8)):
        repeat(o, n)
    lead[0] = 0
    for t in range(4):
        mov(plane("xp", t, 0, 128), V("fa", PAD + t, None, 4), "ga")
        mov(plane("xp", t, 128, 256), V("fb", PAD + t, None, 4), "ga")

    def gram(st, f, kind, mv, w, v, b0, lst, only=(0, 1)):
        q, s = "q_" + st, "s_" + st
        for h in halves():
            if h not in only:
                continue
            base, top, m = 0, 130, 320 + 128 * h
            if kind == "late":
                base, top = 160 * h, 160 * h + 130
                quant(V(q, base, top), V(s, base, top), V(f, 1040 * h + 8, 1040 * h + 528))
                quant(V(q, m, m + 128), V(s, m, m + 128), V(f, 1040 * h + 528, 1040 * h + 1040))
            else:
                if h == 0:
                    quant(V(q, 0, 130), V(s, 0, 130), V(f, 8, 528))
                elif kind == "wide":
                    quant(V(q, 130, 258), V(s, 130, 258), V(f, 528, 1040))
                    top = 258
                lead[0] += TUNE["mlead"]
                for t in range(4):
                    for par in range(2):
                        if kind == "wide":
                            lin(V(mv, 512 * h + 4 * par + t, 512 * h + 512, 8),
                                V(f, PAD + 512 * h + 4 + t, PAD + 512 * h + 512, 8), PAR[par])
                        elif h == 0:
                            lin(V(mv, 4 * par + t, 1024, 8), V(f, PAD + t, PAD + 512, 4), PAR[par])
                lead[0] -= TUNE["mlead"]
                quant(V(q, m, m + 128), V(s, m, m + 128), half(mv, h, 0, 512))
            off = half("pl", h * (kind != "late"), 32 * lst, 16)
            o, i = half("tq_" + st, h, 0, 256), IND(V(q, base, top), off)
            add({"v": (lambda e, o=o, i=i: e.tensor_copy(ap(o, dt.uint32), ap(i, dt.uint32)), time("v", o, [i]))}, [i], [o])
            mov(half("ts_" + st, h, 0, 256), IND(V(s, base, top), off), "a")
            for k in (2 * h, 2 * h + 1):
                mm(bank(b0 + k), half("tq_" + st, k, 0, 128), half("ts_" + st, k, 0, 128), V(q, m, m + 128), V(s, m, m + 128))
                tt(half(w, k), bank(b0 + k, 64 * (k % 2), 64), V("im"), A.mult)
            for pi in range(2):
                o, i = V(v, 128 * h + 64 * pi, 128 * h + 64 * pi + 64), V(w, 128 * h + pi, 128 * h + 128, 2)
                if st[0] == "n":
                    scan(o, V("rs", 0, 64), i)
                else:
                    scan(o, V("rs", 64, 128), i, A.min, A.max, TINY)

    def wide(v, h):
        return IND(half(v, h, 0, 128), EXL)

    def sizes(v, h, a, low, fast, also=None):
        mov(half("ua", h, a), wide(v, h))
        tr(half("dd", h, a), half("ua", h, a))
        lin(half("dd", h, low), half("dd", h, a), BELOW)
        if also:
            tr(half("de", h, also[0]), half("ua", h, a))
            lin(half("de", h, also[1]), half("de", h, also[0]), BELOW)
        if fast:
            tt(half("um", h, a), wide(v, h), MK16H, A.mult)
            tr(half("mk", h, a), half("um", h, a))
        else:
            tt(half("mk", h, a), half("dd", h, a), MK16H, A.mult)
        scan(half("wr", h, a), RS16H, half("mk", h, a))

    def places(a, slot, n, na, cm, cs, wins, out, times):
        nl, dx, ff = NEAR[n]
        (cm, c0), (cs, s0) = cm, cs
        w = sum(size(z) for z in wins(0))
        u = (w + 16) // 2
        tt(V("ee", slot, slot + 16 * n), IND(V("dd", a, a + 16 * n), nl), ff, A.mult)
        tt(V(cm, c0 + n * w, c0 + 2 * n * u), IND(V("wr", slot, slot + 16 * n), dx), V("ee", slot, slot + 16 * n), A.is_gt)
        for m in range(n):
            me, x = col("wr", slot + 16 * m + 15), 0
            for win in wins(m):
                o = V(cm, c0 + n * x + m, c0 + n * (x + size(win)), n)
                x += size(win)
                if m < na:
                    act(o, win, AF.Sign, me, -1.0)
                else:
                    ts(o, win, me, A.is_lt)
            if m < na:
                z = V(cm, c0 + m, c0 + 2 * n * u, n)
                act(z, z, AF.Relu, acc=col("ra", slot // 16 + m))
            else:
                scan(half(cs, m, s0, u), V(cm, c0 + m, c0 + n * u, n), V(cm, c0 + n * u + m, c0 + 2 * n * u, n), A.add, A.add)
        b = out[1]
        ts(V(out[0], b, b + na), V("ra", slot // 16, slot // 16 + na), times, A.mult)
        ts(V(out[0], b + na, b + n), V(cs, s0 + u * na + u - 1, s0 + u * n, u), times, A.mult)

    def ring(name, a, w):
        return lambda m: [V(name, a + 16 * m + 16, a + 16 * m + 16 + w)]

    eng = lanes(T, topo, rank)
    mask = sum(1 << k for k in eng)

    def layer(t_, h, f, a):
        come = 2 * len(lanes(T, topo, (rank - STEP[t_]) % len(T.cores)))
        lq, ls = [V(z, 64 + 128 * t_ + 64 * h, 192 + 128 * t_ + 64 * h) for z in ("lq", "ls")]
        lead[0] = TUNE["lead"] * (1 - h)
        for b in range(4):
            z = b + 4 * (1 - h)
            mm(bank(z), half("wq", b, 0, 128), half("wp", b, 0, 128), lq, ls, ("arr%d" % (2 * t_ + h), come))
            lin(V(f, a + b, a + 256, 4), bank(z, 64, 64), 0.03125, None, TUNE["kq"][b])
            for par in range(2 if t_ < 2 else 0):
                lin(V(f, a + 256 + 4 * par + b, a + 768, 8), bank(z, 64, 64), PARS[par], None, TUNE["kq"][b])
        lead[0] = 0

    for t_ in range(3):
        if t_ == 0:
            ahead[0] = TUNE["ahead"]
            gram("d0", "fa", "", "mvd", "wd", "vd", 0, 0)
            for h in halves():
                sizes("vd", h, 0, 256, False, (0, 128))
            ahead[0] = 0
            gram("d0b", "fb", "", "mvn", "wn", "vb", 4, 0)
            for h in halves():
                sizes("vb", h, 128, 384, h)
            places(0, 0, 8, TUNE["r0"][0], ("cma", 0), ("csa", 0), lambda m: ring("de", 0, 112)(m) + [V("dd", 128, 256)],
                   V("rku", 0, 8), 1.0)
            places(128, 128, 8, TUNE["r0"][1], ("cmb", 0), ("csb", 0), ring("dd", 128, 240), V("rku", 8, 16), 1.0)
            mov(IND(V("on"), V("rku")), JALL, "v")
            for h in halves():
                scan(half("ox", h, 0, 128), WX, half("on", h, 0, 128), A.mult, A.max)
                ts(half("ofy", h, 0, 8), V("ox", 128 * h + 15, 128 * h + 128, 16), SC, A.mult)
        else:
            stage[1] = 3 * t_
            for h in range(2):
                a = 272 + 1040 * h
                layer(t_ - 1, h, "fk", a)
                for t in range(4):
                    mov(plane("xp", t, 128 + 64 * h, 192 + 64 * h), V("fk", a + t, a + 256, 4), "g")
                gram("d%d" % t_, "fk", "late", None, "wd", "vd", 4, 3, (h,))
                lead[0] = TUNE["lead"] * (1 - h)
                sizes("vd", h, 128, 384, h, None if h else (0, 192))
            places(128, 128, 4, TUNE["r"][0], ("cmb", 0), ("csb", 0), lambda m: ring("de", 0, 176)(m) + [V("dd", 192, 256)],
                   V("rku", 8, 12), 2.0)
            places(192, 192, 4, TUNE["r"][1], ("cmb", 1024), ("csb", 512), ring("dd", 192, 240), V("rku", 12, 16), 2.0)
            mov(IND(V("oo"), V("rku", 8, 16)), JKS, "v")
            scan(V("oo", 1, 512, 2), ONES, V("oo", 0, 512, 2), A.mult, A.subtract, -1.0)
            for h in halves():
                scan(half("ox", h, 0, 256), WP, half("oo", h, 0, 256), A.mult, A.max)
                ts(half("ofy", h, 0, 8), V("ox", 256 * h + 31, 256 * h + 256, 32), SC, A.mult)

        stage[0], stage[1] = t_ + 1, 3 * t_ + 1
        for h in halves():
            for t in range(4):
                mov(V("ab", PAD + 512 * h + t, PAD + 512 * h + 512, 4), IND(plane("xp", t), half("ofy", h, 0, 8)))
            mov(half("da", h, 0, 128), IND(V("dd", 0, 256), half("ofy", h, 0, 8)))
            tr(half("dq", h), V("da", 128 * h, 128 * h + 128, 2))
        if t_ == 2:
            mov(V("of"), IND(V("ids"), V("ofy")))
            dma("s", T.ol[:, :], V("of", None, None, None, (0, 128, 16)))
        for i, c in ((0, 0.75), (2, 0.25)):
            lin(V("th", i, 32, 4), V("dq", 0, 128, 16), c)
            lin(V("th", i + 1, 32, 4), V("th", i, 32, 4), -BELOW)
        gram("n%d" % t_, "ab", "wide", "mvn", "wn", "vn", 0, 1)
        for h in halves():
            tt(half("th", h, 32, 16), IND(half("vn", h, 0, 128), N4L), half("th", h, 0, 16), A.is_ge)
            scan(half("th", h, 64, 16), RS4, half("th", h, 32, 16))
            lin(half("uc", h), IND(half("th", h, 64, 16), CXL), -0.5, 1.0)
            tr(V("cc", 128 * h + 1, 128 * h + 128, 2), half("uc", h))
            for t in range(4):
                a = PAD + 512 * h + t
                scan(V("ar", a, PAD + 512 * h + 512, 4), half("cc", h, 0, 128), V("ab", a, PAD + 512 * h + 512, 4))
        to = topo.addr(T.cores[(rank + STEP[t_]) % len(T.cores)])
        stage[1] += 1
        gram("e%d" % t_, "ar", "wide", "mve", "we", "ve", 0, 2)
        for h in halves():
            tt(half("ub", h), wide("ve", h), half("dq", h), A.is_ge)
            tr(V("fi", 128 * h, 128 * h + 128, 2), half("ub", h))
            scan(half("bx", h, 0, 128), WM, half("fi", h, 0, 128))
            ts(half("ofm", h, 0, 16), V("bx", 128 * h + 7, 128 * h + 128, 8), SC4, A.mult, T4, A.add)
            for z in (2 * h, 2 * h + 1):
                mov(half("fm", z, 512, 128), IND(V("ar", PAD), half("ofm", z, 0, 8)))
            m = 128 * h
            quant(V("mq%d" % t_, m, m + 128), V("ms%d" % t_, m, m + 128), V("fm", 256 + 2 * m, 768 + 2 * m))
            for src, dst, cast in (("mq", "lq", dt.uint8), ("ms", "ls", None)):
                o, i = half(dst, 2 * t_ + h, 128), V(src + "%d" % t_, m + 64, m + 128)
                add({"g": (lambda e, o=o, i=i, cast=cast, arr=T.sem["arr%d" % (2 * t_ + h)], to=to:
                           e.remote_dma(ap(o, cast), ap(i, cast), arr, T.sem.sent, to[1], to[0], mask),
                           TUNE["send"] + TUNE["first"] * (not sent[0]))}, [i], [o], "r")
                sent[0] += len(eng)

        if t_ < 2:
            iota(V("oo", 0, 512, 2), [[0, 256]], -1)
            for h in halves():
                tt(half("us", h), wide("ve", h), half("dq", h), A.min)
                tr(half("dd", h, 128), half("us", h))
                scan(half("fs", h, 0, 128), MS, half("fi", h, 0, 128))
                lin(half("dd", h, 256), half("dd", h, 128), BELOW)
                tt(half("mk", h), half("dd", h, 128), MK16H, A.mult)
                scan(half("wr", h), RS16H, half("mk", h))
            lin(V("de", 64, 192), V("dd", 128, 256), BELOW)
            places(128, 0, 8, TUNE["ss"], ("cma", 0), ("csa", 0), ring("dd", 128, 112), V("rks", 0, 8), 1.0)
            mov(V("dw", 0, 256, 2), V("dd", 128, 256), "ga")
            mov(V("dw", 1, 256, 2), V("dd", 128, 256), "ga")
            for t in range(4):
                mov(plane("ap", t), V("ar", PAD + t, None, 4), "ga")
            mov(IND(V("so"), V("rks")), V("fs", 1, 256, 2), "v")
            scan(V("bz", 0, 128), WX, V("so"))
            ts(V("ofs"), V("bz", 15, 128, 16), SC, A.mult, 1.0, A.add)
            for t in range(4):
                mov(plane("xp", t, 0, 128), IND(plane("ap", t), V("ofs")))
            mov(V("dd", 0, 128), IND(V("dw"), V("ofs")))
            if t_ == 1:
                mov(V("ids", 0, 128), IND(JHALF, V("ofs")))
        else:
            for h in halves():
                scan(half("bz", h, 0, 128), WN, half("fi", h, 0, 128))
                ts(half("ofz", h, 0, 16), V("bz", 128 * h + 7, 128 * h + 128, 8), SC4, A.mult, T44, A.add)
                mov(half("xf", h, 0, 256), IND(V("ar", PAD), half("ofz", h, 0, 16)))
            quant(V("vq"), V("vp"), V("vt"))
            quant(V("xq", 0, 128), V("xs", 0, 128), V("xf", 0, 512))
            mm(bank(0), V("vq"), V("vp"), V("xq", 0, 128), V("xs", 0, 128))
            mov(V("yo", 0, 128), bank(0))
            dma("s", T.oc[:, 0:512], V("xq", 0, 128), None, dt.uint8)
            dma("s", T.y[:, 0:128], V("yo", 0, 128))

    for h in range(2):
        layer(2, h, "xf", 512 + 256 * h)
    quant(V("xq", 128, 256), V("xs", 128, 256), V("xf", 512, 1024))
    mm(bank(4), V("vq"), V("vp"), V("xq", 128, 256), V("xs", 128, 256))
    dma("a", T.oc[:, 512:1024], V("xq", 128, 256), None, dt.uint8)
    for k, e in enumerate("ssaa"):
        dma(e, T.osc[4 * k:4 * k + 4, :], V("xs", 0, 256, None, (32 * k, 32 * k + 4)))
    mov(V("yo", 128, 256), bank(4), "v")
    dma("s", T.y[:, 128:256], V("yo", 128, 256))
    return ops, sent[0]


def order(ops):
    def cols(v):
        m = np.zeros(SCRATCH[v[0]][1][1], bool)
        if v[0] == "ps":
            m[v[1] // 512 * 512:v[1] // 512 * 512 + 512] = True
        else:
            m[slice(v[1], v[2], v[3])] = True
        return int.from_bytes(np.packbits(m).tobytes(), "big")

    seen, deps = {}, []
    for i, (alt, rd, wr, kind, pre, lead, part) in enumerate(ops):
        acc = [(v[0], cols(v), False) for v in rd] + [(v[0], cols(v), True) for v in wr]
        deps.append({j for name, m, w in acc for j, mj, wj in seen.get(name, []) if m & mj and (
            w or wj or name == "ps" and len(set(alt) | set(ops[j][0])) > 1)})
        for name, m, w in acc:
            seen.setdefault(name, []).append((i, m, w))
    late = {"c": TUNE["wake"], "d": TUNE["dma"], "r": TUNE["far"]}
    n = len(ops)
    users = [set() for i in range(n)]
    for i in range(n):
        for j in deps[i]:
            users[j].add(i)

    def urgent(weight):
        togo = [0.0] * n
        for i in range(n - 1, -1, -1):
            togo[i] += min(c for f, c in ops[i][0].values()) + late[ops[i][3]]
            for j in deps[i]:
                togo[j] = max(togo[j], togo[i] + weight[ops[j][6]] * max(0, ops[j][5] - ops[i][5]))
        return sorted(range(n), key=lambda i: (-togo[i], i))

    def place(seq, back):
        busy, start, end, queue = {q: [] for q in "vatgs"}, {}, {}, {}
        for i in seq:
            if back:
                ready = max([end[j] for j in users[i]], default=0.0) + late[ops[i][3]]
            else:
                ready = max([end[j] + late[ops[j][3]] for j in deps[i]], default=0.0)
            best = None
            for q, (f, c) in ops[i][0].items():
                t, k, row = ready, 0, busy[q]
                while k < len(row) and t + c > row[k][0]:
                    t = max(t, row[k][1])
                    k += 1
                mark = t + c + (TUNE["spare"] if q == "v" else 0)
                if best is None or mark < best[0]:
                    best = (mark, t, q, k, t + c)
            busy[best[2]].insert(best[3], (best[1], best[4]))
            start[i], end[i], queue[i] = best[1], best[4], best[2]
        return max(end[i] + (0 if back else late[ops[i][3]]) for i in seq), start, end, queue

    def sort(key, first, then):
        left = [len(z) for z in first]
        ready, seq = sorted((key[i], i) for i in range(n) if not left[i]), []
        while ready:
            i = ready.pop(0)[1]
            seq.append(i)
            new = []
            for j in then[i]:
                left[j] -= 1
                if not left[j]:
                    new.append((key[j], j))
            if new:
                ready = sorted(ready + new)
        return seq

    rng = np.random.default_rng(TUNE["seed"])

    def settle(weight, turns):
        good = place(urgent(weight), False)
        for turn in range(turns):
            shake = rng.random(n) * TUNE["shake"] * (turn > 0)
            back = place(sort([-good[2][i] + shake[i] for i in range(n)], users, deps), True)
            now = place(sorted(range(n), key=lambda i: (-back[2][i], i)), False)
            if now[0] <= good[0]:
                good = now
        return good

    weight = [1.0] * 9
    best = settle(weight, 1)
    for part in range(9):
        for w in TUNE["weights"]:
            other = weight[:part] + [w] + weight[part + 1:]
            now = settle(other, 1)
            if now[0] < best[0]:
                best, weight = now, other
    now = settle(weight, TUNE["turns"])
    if now[0] < best[0]:
        best = now
    PLAN["time"] = best[0]
    seq, queue = sorted(range(n), key=lambda i: (best[1][i], i)), dict(best[3])
    cost = [{q: c for q, (f, c) in o[0].items()} for o in ops]
    for a in [a for first in TUNE["passes"] for a in range(first, n - TUNE["step"], TUNE["step"])]:
        b = min(n, a + TUNE["span"])
        part, inside, cases = seq[a:b], set(seq[a:b]), []
        for f, far in TUNE["cases"]:
            lat = [far if o[3] == "r" else late[o[3]] for o in ops]
            free, end, tail, nxt = {}, {}, {}, {}
            for i in seq[:a]:
                q = queue[i]
                end[i] = free[q] = cost[i][q] * f + max([free.get(q, 0.0)] + [end[j] + lat[j] for j in deps[i]])
            for i in reversed(seq[b:]):
                q = queue[i]
                tail[i] = nxt[q] = cost[i][q] * f + max([nxt.get(q, 0.0), lat[i]] + [lat[i] + tail[j] for j in users[i]])
            head = {i: max([end[j] + lat[j] for j in deps[i] if j not in inside], default=0.0) for i in part}
            out = {i: max([lat[i] + tail[j] for j in users[i] if j not in inside], default=lat[i]) for i in part}
            cases.append((f, lat, free, nxt, head, out))
        near = {i: [j for j in deps[i] if j in inside] for i in part}

        def worth(part):
            total = 0.0
            for f, lat, free, nxt, head, out in cases:
                free, end, top, mean = dict(free), {}, 0.0, 0.0
                for i in part:
                    q = queue[i]
                    t = max(free.get(q, 0.0), head[i])
                    for j in near[i]:
                        if end[j] > t:
                            t = end[j]
                    t += cost[i][q] * f
                    free[q], end[i] = t, t + lat[i]
                    t += out[i]
                    mean += t
                    if t > top:
                        top = t
                total += (max([top] + [free.get(q, 0.0) + nxt[q] for q in nxt]) + 0.3 * mean / len(part)) / f
            return total
        now = worth(part)
        keep = (now, part, dict(queue))
        for turn, (u, v, w, x) in enumerate(rng.random((TUNE["moves"], 4)).tolist()):
            k = z = int(u * len(part))
            i, far = part[k], int((v - 0.5) * 2 * TUNE["reach"])
            was = queue[i]
            if len(cost[i]) > 1 and w < 0.3:
                queue[i] = [q for q in cost[i] if q != was][0]
            while z > max(0, k + far) and part[z - 1] not in deps[i]:
                z -= 1
            while z < min(len(part) - 1, k + far) and i not in deps[part[z + 1]]:
                z += 1
            if z == k and queue[i] == was:
                continue
            other = part[:k] + part[k + 1:]
            other.insert(z, i)
            new = worth(other)
            if new <= now - TUNE["heat"] * (1 - turn / TUNE["moves"]) * math.log(x + 1e-12):
                part, now = other, new
                if now < keep[0]:
                    keep = (now, part, dict(queue))
            else:
                queue[i] = was
        seq[a:b], queue = keep[1], keep[2]
    return deps, queue, seq


def emit(g, T, ops, sent):
    eng = {"v": g.vector, "a": g.scalar, "t": g.tensor, "g": g, "s": g.sync}
    if "order" not in PLAN:
        PLAN["order"] = order(ops)
    deps, queue, seq = PLAN["order"]
    at = {i: k for k, i in enumerate(seq)}

    known, done = {q: 0 for q in eng}, {q: 0 for q in eng}
    at_end, waits, needed = {}, {}, set()
    for i in seq:
        q, ws = queue[i], []
        for j in sorted(deps[i], key=lambda j: -at[j]):
            if ops[j][3] != "r" and not known[q] >> j & 1:
                ws.append(j)
                known[q] |= at_end[j]
        waits[i] = ws
        needed.update(ws)
        if ops[i][3] == "c":
            done[q] |= 1 << i
        at_end[i] = known[q] | (done[q] if ops[i][3] == "c" else 1 << i)

    tag, count, ndma, open_dma, come = {}, {q: 0 for q in eng}, [0], [], []
    for i in seq:
        alt, rd, wr, kind, pre, lead, part = ops[i]
        q = queue[i]
        if pre is not None and pre not in come:
            come.append(pre)
            eng[q].wait_ge(T.sem[pre[0]], pre[1])
        for j in waits[i]:
            eng[q].wait_ge(T.sem[tag[j][0]], tag[j][1])
        ins = alt[q][0](eng[q])
        if kind == "d":
            tag[i] = ("dma%d" % ndma[0], 16)
            ndma[0] += 1
            ins.then_inc(T.sem[tag[i][0]], 16)
            if i not in needed:
                open_dma.append(i)
        elif kind == "c" and i in needed:
            count[q] += 1
            tag[i] = (q, count[q])
            ins.then_inc(T.sem[q], 1)
    for j in open_dma:
        eng[queue[j]].wait_ge(T.sem[tag[j][0]], 16)
    g.wait_ge(T.sem.sent, sent)


def rank_program(g, core, T, topo):
    rank = T.rank_of(core)
    if rank is None:
        return
    ops, sent = build(T, topo, rank)
    emit(g, T, ops, sent)
